import numpy as np
import ml_dtypes


def mxq(x, axis, fmt="e4m3"):
    dtype, down = {"e4m3": (ml_dtypes.float8_e4m3fn, 7), "e5m2": (ml_dtypes.float8_e5m2, 14)}[fmt]
    v = np.moveaxis(np.asarray(x, np.float32).astype(ml_dtypes.bfloat16).astype(np.float64), axis, -1)
    blocks = v.reshape(v.shape[:-1] + (-1, 32))
    amax = np.abs(blocks).max(-1, keepdims=True)
    byte = np.maximum(np.where(amax > 0, np.frexp(amax)[1] - 1 + 127, 0) - down, 1)
    scale = np.exp2(byte - 127.0)
    codes = (blocks / scale).astype(np.float32).astype(dtype).astype(np.float64)
    return np.moveaxis((codes * scale).reshape(v.shape), -1, axis)


WIDE = False


def mx_kscale(k):
    if not WIDE:
        return np.ones(k)
    levels = np.array([24, -24, 12, -12, 0])
    if k % 512:
        return np.exp2(np.random.permutation(np.resize(levels, k // 32))).repeat(32)
    a = np.empty((k // 512, 16))
    for p in range(k // 512):
        a[p, :8] = np.random.permutation(np.resize(levels, 8))
        for g in range(8):
            far = levels[np.abs(levels - a[p, g]) >= 10]
            a[p, g + 8] = far[np.random.randint(len(far))]
    return np.exp2(a.ravel()).repeat(32)


def f64(x):
    return np.asarray(x).astype(np.float64)


def striped(idx):
    return np.tile(idx.reshape(-1, 16).T, (8, 1)).astype(np.uint16)


def unstriped(offs):
    return offs[:16].T.reshape(-1).astype(np.int64)


E2M1 = np.array([0.0, 0.5, 1.0, 1.5, 2.0, 3.0, 4.0, 6.0, -0.0, -0.5, -1.0, -1.5, -2.0, -3.0, -4.0, -6.0])


def pack_weight(w, fmt):
    k, n = w.shape
    w = f64(np.asarray(w, np.float32).astype(ml_dtypes.bfloat16)).reshape(k // 32, 32, n)
    amax = np.abs(w).max(1)
    if fmt == "e4m3":
        byte = np.frexp(amax)[1] - 1 + 127 - 7
    else:
        mant, ex = np.frexp(amax / 6.0)
        byte = np.where(mant > 0.5, ex, ex - 1) + 127
    byte = np.clip(np.where(amax > 0, byte, 1), 1, 254)
    scaled = (w * np.exp2(127.0 - byte)[:, None, :]).reshape(k, n).astype(np.float32)
    by_word = np.ascontiguousarray(scaled.reshape(k // 512, 128, 4, n).transpose(0, 1, 3, 2))
    if fmt == "e4m3":
        words = by_word.astype(ml_dtypes.float8_e4m3fn).view(np.uint8)
    else:
        c = by_word.astype(ml_dtypes.float4_e2m1fn).view(np.uint8) & 0xF
        words = (c[..., 0::2] | (c[..., 1::2] << 4)).reshape(k // 512, 128, 2 * n)
    return np.ascontiguousarray(words), np.ascontiguousarray(byte.astype(np.uint8).reshape(k // 512, 16, n))


def unpack_weight(words, scales, fmt):
    g, _, n = scales.shape
    words = np.ascontiguousarray(words).reshape(g, 128, n, -1)
    if fmt == "e4m3":
        vals = words.view(ml_dtypes.float8_e4m3fn).astype(np.float64)
    else:
        nib = np.empty((g, 128, n, 4), np.uint8)
        nib[..., 0::2] = words & 0xF
        nib[..., 1::2] = words >> 4
        vals = E2M1[nib]
    vals = vals * np.repeat(np.exp2(scales.astype(np.float64) - 127.0), 8, axis=1)[..., None]
    return vals.transpose(0, 1, 3, 2).reshape(g * 512, n)


def planes(y):
    n, m = y.shape
    v = y.astype(np.float32).astype(ml_dtypes.bfloat16).astype(np.float64).reshape(n // 32, 32, m)
    top = np.abs(v).max(1)
    byte = np.clip(np.where(top > 0, np.frexp(top)[1] - 1 + 127 - 7, 1), 1, 254)
    codes = (v * np.exp2(127.0 - byte)[:, None, :]).reshape(n, m).astype(np.float32).astype(ml_dtypes.float8_e4m3fn).view(np.uint8)
    words = codes.reshape(n // 512, 128, 4, m).transpose(0, 1, 3, 2)
    return np.ascontiguousarray(words), np.ascontiguousarray(byte.astype(np.uint8).reshape(n // 512, 16, m))


K, R, N, T, J = 512, 512, 512, 2048, 1024


def setup_inputs():
    n = np.random.standard_normal
    s = mx_kscale(K)[:, None]
    u = mx_kscale(R)[:, None]
    p_tab = pack_weight(n((K, T)) * s, "e4m3")
    p_wb = pack_weight(0.7 * n((K, N)) / np.sqrt(K) / s, "e2m1")
    p_upw = pack_weight(2.0 * n((R, N)) / np.sqrt(R) / u, "e2m1")
    return {
        "tab_words": p_tab[0],
        "tab_scales": p_tab[1],
        "wb_words": p_wb[0],
        "wb_scales": p_wb[1],
        "dn": (n((K, R)) / np.sqrt(K) / s * u.T).astype(np.float32),
        "upw_words": p_upw[0],
        "upw_scales": p_upw[1],
        "x0T": (n((N, T))).astype(np.float32),
        "b": (0.3 * n(N)).astype(np.float32),
        "offs": striped(np.random.permutation(T)[:J]),
    }


def reference(tab_words, tab_scales, wb_words, wb_scales, dn, upw_words, upw_scales, x0T, b, offs):
    idx = unstriped(offs)
    tab_ = unpack_weight(tab_words, tab_scales, "e4m3")[:, idx]
    wb_ = unpack_weight(wb_words, wb_scales, "e2m1")
    dn_ = mxq(f64(dn), 0, "e4m3")
    hs = dn_.T @ tab_
    h = np.maximum(hs, 0.0)
    h_ = mxq(h, 0, "e4m3")
    upw_ = unpack_weight(upw_words, upw_scales, "e2m1")
    y = wb_.T @ tab_ + upw_.T @ h_
    out_0 = f64(x0T)[:, idx] * (y + f64(b)[:, None]) + f64(x0T)[:, idx]
    return (out_0,) + planes(out_0)

@@ -1,0 +1,145 @@
+from contextlib import ExitStack
+
+import concourse.mybir as mybir
+
+K, R, N, T, J = 512, 512, 512, 2048, 1024
+FLOPS = 2 * J * (K * R + K * N + R * N)
+
+F32 = mybir.dt.float32
+BF16 = mybir.dt.bfloat16
+I32 = mybir.dt.int32
+U32 = mybir.dt.uint32
+U16 = mybir.dt.uint16
+U8 = mybir.dt.uint8
+FP8X4 = mybir.dt.float8_e4m3fn_x4
+FP4X4 = mybir.dt.float4_e2m1fn_x4
+ALU = mybir.AluOpType
+ACT = mybir.ActivationFunctionType
+
+P = 128
+PACK = 4
+HALF = 512
+SUB = 128
+
+
+def tile_list_xcross_reluP_kernel(tc, tab_words, tab_scales, wb_words, wb_scales, dn, upw_words, upw_scales, x0T, b, offs, out_0, out_1, out_2):
+    nc = tc.nc
+    with ExitStack() as ctx:
+        held = ctx.enter_context(tc.tile_pool(name="held", bufs=1))
+        ring = ctx.enter_context(tc.tile_pool(name="ring", bufs=4))
+        psum_h = ctx.enter_context(tc.psum_pool(name="psum_h", bufs=3))
+        psum_y = ctx.enter_context(tc.psum_pool(name="psum_y", bufs=5))
+
+        def keep(name, shape, dtype):
+            return held.tile(shape, dtype, name=name, align_bytes=64)
+
+        def listed(j0, count):
+            return offsets[:, j0 // 16 : (j0 + count) // 16]
+
+        offsets = held.tile([P, J // 16], U16, name="offsets")
+        tab_w = keep("tab_w", [P, T], U32)
+        tab_s = keep("tab_s", [P, T], U8)
+        dn_raw = keep("dn_raw", [P, PACK, R], F32)
+        w_raw = [keep("w_raw%d" % u, [P, 2 * N], U8) for u in range(2)]
+        ws_raw = [keep("ws_raw%d" % u, [P, N], U8) for u in range(2)]
+        x0 = [keep("x0_%d" % t, [P, T], F32) for t in range(PACK)]
+        bias = keep("bias", [P, PACK], F32)
+        bias1 = keep("bias1", [P, PACK], F32)
+
+        def load_plane(plane, scales):
+            for q in range(4):
+                nc.sync.dma_start(plane[32 * q : 32 * q + 4, :].bitcast(I32), scales[0, 4 * q : 4 * q + 4, :].bitcast(I32))
+
+        nc.gpsimd.memset(tab_s[:].bitcast(I32), 0)
+        for u in range(2):
+            nc.gpsimd.memset(ws_raw[u][:].bitcast(I32), 0)
+        x0_rows = x0T.rearrange("(p t) c -> p t c", t=PACK)
+        nc.sync.dma_start(offsets[:], offs)
+        nc.sync.dma_start(w_raw[0][:].bitcast(I32), wb_words[0].bitcast(I32))
+        nc.sync.dma_start(w_raw[1][:].bitcast(I32), upw_words[0].bitcast(I32))
+        nc.sync.dma_start(bias[:], b.rearrange("(p t) -> p t", t=PACK))
+        load_plane(tab_s, tab_scales)
+        nc.sync.dma_start(dn_raw[:], dn.rearrange("(p i) r -> p i r", i=PACK))
+        nc.sync.dma_start(tab_w[:].bitcast(I32), tab_words[0].rearrange("p t i -> p (t i)").bitcast(I32))
+        load_plane(ws_raw[0], wb_scales)
+        nc.sync.dma_start(x0[0][:], x0_rows[:, 0, :])
+        load_plane(ws_raw[1], upw_scales)
+        for t in range(1, PACK):
+            nc.sync.dma_start(x0[t][:], x0_rows[:, t, :])
+        nc.gpsimd.tensor_scalar(bias1[:], bias[:], 1.0, 1.0, ALU.mult, ALU.add)
+
+        v_s = [keep("v_s%d" % h, [P, HALF], U8) for h in range(2)]
+        v_w = [keep("v_w%d" % h, [P, HALF], U32) for h in range(2)]
+        for h in range(2):
+            nc.vector.tensor_copy(v_s[h][:], tab_s[:].indirect(listed(h * HALF, HALF)))
+        dn_bf = keep("dn_bf", [P, R * PACK], BF16)
+        dn_dealt = dn_bf[:].rearrange("p (t m i) -> p m i t", t=PACK, i=PACK)
+        dn_src = dn_raw[:].rearrange("p i (m t) -> p m i t", t=PACK)
+        nc.scalar.copy(dn_dealt[:, :64], dn_src[:, :64])
+        nc.vector.tensor_copy(dn_dealt[:, 64:], dn_src[:, 64:])
+        dn_w = keep("dn_w", [P, R], U32)
+        dn_s = keep("dn_s", [P, R], U8)
+        nc.vector.quantize_mx(out=dn_w[:].bitcast(FP8X4), scales=dn_s[:], in_=dn_bf[:])
+        for h, c0, width in ((0, 0, 256), (0, 256, 256), (1, 0, 512)):
+            nc.vector.tensor_copy(v_w[h][:, c0 : c0 + width], tab_w[:].indirect(listed(h * HALF + c0, width)))
+
+        w_w = [keep("w_w%d" % u, [P, 2 * N], U8) for u in range(2)]
+        w_s = [keep("w_s%d" % u, [P, N], U8) for u in range(2)]
+        for u in range(2):
+            nc.vector.tensor_copy(w_w[u][:].bitcast(U16).rearrange("p (t m) -> p m t", t=PACK), w_raw[u][:].bitcast(U16).rearrange("p (m t) -> p m t", t=PACK))
+            nc.vector.tensor_copy(w_s[u][:].rearrange("p (t m) -> p m t", t=PACK), ws_raw[u][:].rearrange("p (m t) -> p m t", t=PACK))
+
+        h_w = [keep("h_w%d" % h, [P, HALF], U32) for h in range(2)]
+        h_s = [keep("h_s%d" % h, [P, HALF], U8) for h in range(2)]
+        h_bf = [keep("h_bf%d" % h, [P, HALF * PACK], BF16) for h in range(2)]
+        for h in range(2):
+            for c in range(HALF // SUB):
+                cols = slice(c * SUB, (c + 1) * SUB)
+                hs = psum_h.tile([P, PACK, SUB], F32, name="hs")
+                for t in range(PACK):
+                    rows = slice(t * P, (t + 1) * P)
+                    nc.tensor.matmul_mx(out=hs[:, t, :], lhsT=dn_w[:, rows].bitcast(FP8X4), lhsT_scale=dn_s[:, rows],
+                                        rhs=v_w[h][:, cols].bitcast(FP8X4), rhs_scale=v_s[h][:, cols], start=True, stop=True)
+                nc.scalar.activation(h_bf[h][:, c * SUB * PACK : (c + 1) * SUB * PACK].rearrange("p (j t) -> p j t", t=PACK),
+                                     hs[:].rearrange("p t j -> p j t"), ACT.Relu)
+            nc.vector.quantize_mx(out=h_w[h][:].bitcast(FP8X4), scales=h_s[h][:], in_=h_bf[h][:])
+
+        x_first = [keep("x_first%d" % h, [P, HALF], F32) for h in range(2)]
+        for h in range(2):
+            nc.vector.tensor_copy(x_first[h][:], x0[0][:].indirect(listed(h * HALF, HALF)))
+        res = [keep("res%d" % h, [P, PACK, HALF], F32) for h in range(2)]
+        res_bf = [keep("res_bf%d" % g, [P, 256 * PACK], BF16) for g in range(4)]
+        res_w = keep("res_w", [P, J], U32)
+        res_s = keep("res_s", [P, J], U8)
+        out_rows = out_0.rearrange("(p t) j -> p t j", t=PACK)
+        out_words = out_1[0].rearrange("p j i -> p (j i)").bitcast(I32)
+        for h in range(2):
+            for t in range(PACK):
+                y = psum_y.tile([P, HALF], F32, name="y")
+                for u, (mw, ms) in enumerate(((v_w[h], v_s[h]), (h_w[h], h_s[h]))):
+                    nc.tensor.matmul_mx(out=y[:], lhsT=w_w[u][:, 2 * t * P : 2 * (t + 1) * P].bitcast(FP4X4), lhsT_scale=w_s[u][:, t * P : (t + 1) * P],
+                                        rhs=mw[:].bitcast(FP8X4), rhs_scale=ms[:], start=(u == 0), stop=(u == 1))
+                if t == 0:
+                    nc.vector.scalar_tensor_tensor(res[h][:, t, :], y[:], bias1[:, t : t + 1], x_first[h][:], ALU.add, ALU.mult)
+                else:
+                    y1 = ring.tile([P, HALF], F32, name="y1")
+                    nc.scalar.activation(y1[:], y[:], ACT.Identity, bias=bias1[:, t : t + 1])
+                    if t < 3:
+                        nc.vector.tensor_tensor(res[h][:, t, :], x0[t][:].indirect(listed(h * HALF, HALF)), y1[:], ALU.mult)
+                    else:
+                        for g in range(2):
+                            nc.vector.tensor_tensor(res[h][:, t, g * 256 : (g + 1) * 256], x0[t][:].indirect(listed(h * HALF + g * 256, 256)), y1[:, g * 256 : (g + 1) * 256], ALU.mult)
+                nc.sync.dma_start(out_rows[:, t, h * HALF : (h + 1) * HALF], res[h][:, t, :])
+            for g in range(2):
+                gg = 2 * h + g
+                dst = res_bf[gg][:].rearrange("p (c i t) -> p c t i", i=4, t=PACK)
+                src = res[h][:, :, g * 256 : (g + 1) * 256].rearrange("p t (c i) -> p c t i", i=4)
+                if gg == 3:
+                    nc.vector.tensor_copy(dst, src)
+                else:
+                    nc.scalar.copy(dst, src)
+                cols = slice(gg * 256, (gg + 1) * 256)
+                nc.vector.quantize_mx(out=res_w[:, cols].bitcast(FP8X4), scales=res_s[:, cols], in_=res_bf[gg][:])
+            nc.sync.dma_start(out_words[:, h * HALF : (h + 1) * HALF], res_w[:, h * HALF : (h + 1) * HALF].bitcast(I32))
+        for q in range(4):
+            nc.scalar.dma_start(out_2[0, 4 * q : 4 * q + 4, :].bitcast(I32), res_s[32 * q : 32 * q + 4, :].bitcast(I32))

@@ -19,6 +19,7 @@ ACT = mybir.ActivationFunctionType
 P = 128
 PACK = 4
 HALF = 512
+QUARTER = 256
 SUB = 128
 
 
@@ -26,72 +27,83 @@ def tile_list_xcross_reluP_kernel(tc, tab_words, tab_scales, wb_words, wb_scales
     nc = tc.nc
     with ExitStack() as ctx:
         held = ctx.enter_context(tc.tile_pool(name="held", bufs=1))
-        ring = ctx.enter_context(tc.tile_pool(name="ring", bufs=4))
         psum_h = ctx.enter_context(tc.psum_pool(name="psum_h", bufs=3))
         psum_y = ctx.enter_context(tc.psum_pool(name="psum_y", bufs=5))
 
-        def keep(name, shape, dtype):
-            return held.tile(shape, dtype, name=name, align_bytes=64)
+        def keep(name, shape, dtype, tag=None):
+            return held.tile(shape, dtype, name=name, tag=tag or name, align_bytes=64)
 
         def listed(j0, count):
             return offsets[:, j0 // 16 : (j0 + count) // 16]
 
         offsets = held.tile([P, J // 16], U16, name="offsets")
-        tab_w = keep("tab_w", [P, T], U32)
         tab_s = keep("tab_s", [P, T], U8)
-        dn_raw = keep("dn_raw", [P, PACK, R], F32)
+        ws_raw = keep("ws_raw", [P, 2 * N], U8)
+        w_s = keep("w_s", [P, 2 * N], U8)
+        nc.vector.memset(tab_s[:, : T // 2].bitcast(I32), 0)
+        nc.gpsimd.memset(tab_s[:, T // 2 :].bitcast(I32), 0)
+        nc.vector.memset(ws_raw[:].bitcast(I32), 0)
+        nc.gpsimd.memset(w_s[:].bitcast(I32), 0)
         w_raw = [keep("w_raw%d" % u, [P, 2 * N], U8) for u in range(2)]
-        ws_raw = [keep("ws_raw%d" % u, [P, N], U8) for u in range(2)]
-        x0 = [keep("x0_%d" % t, [P, T], F32) for t in range(PACK)]
-        bias = keep("bias", [P, PACK], F32)
-        bias1 = keep("bias1", [P, PACK], F32)
-
-        def load_plane(plane, scales):
-            for q in range(4):
-                nc.sync.dma_start(plane[32 * q : 32 * q + 4, :].bitcast(I32), scales[0, 4 * q : 4 * q + 4, :].bitcast(I32))
-
-        nc.gpsimd.memset(tab_s[:].bitcast(I32), 0)
-        for u in range(2):
-            nc.gpsimd.memset(ws_raw[u][:].bitcast(I32), 0)
-        x0_rows = x0T.rearrange("(p t) c -> p t c", t=PACK)
+        dn_raw = [keep("dn_raw%d" % u, [P, PACK, R // 2], F32) for u in range(2)]
+        dn_rows = dn.rearrange("(p i) r -> p i r", i=PACK)
         nc.sync.dma_start(offsets[:], offs)
-        nc.sync.dma_start(w_raw[0][:].bitcast(I32), wb_words[0].bitcast(I32))
-        nc.sync.dma_start(w_raw[1][:].bitcast(I32), upw_words[0].bitcast(I32))
-        nc.sync.dma_start(bias[:], b.rearrange("(p t) -> p t", t=PACK))
-        load_plane(tab_s, tab_scales)
-        nc.sync.dma_start(dn_raw[:], dn.rearrange("(p i) r -> p i r", i=PACK))
+        for u, words in enumerate((wb_words, upw_words)):
+            nc.sync.dma_start(w_raw[u][:].bitcast(I32), words[0].bitcast(I32))
+        for q in range(4):
+            nc.sync.dma_start(tab_s[32 * q : 32 * q + 4, :].bitcast(I32), tab_scales[0, 4 * q : 4 * q + 4, :].bitcast(I32))
+        nc.sync.dma_start(dn_raw[0][:], dn_rows[:, :, : R // 2])
+        nc.sync.dma_start(dn_raw[1][:], dn_rows[:, :, R // 2 :])
+        for u, scales in enumerate((wb_scales, upw_scales)):
+            nc.sync.dma_start(ws_raw[:16, u * N : (u + 1) * N].bitcast(I32), scales[0].bitcast(I32))
+        tab_w = keep("tab_w", [P, T], U32)
         nc.sync.dma_start(tab_w[:].bitcast(I32), tab_words[0].rearrange("p t i -> p (t i)").bitcast(I32))
-        load_plane(ws_raw[0], wb_scales)
-        nc.sync.dma_start(x0[0][:], x0_rows[:, 0, :])
-        load_plane(ws_raw[1], upw_scales)
-        for t in range(1, PACK):
-            nc.sync.dma_start(x0[t][:], x0_rows[:, t, :])
-        nc.gpsimd.tensor_scalar(bias1[:], bias[:], 1.0, 1.0, ALU.mult, ALU.add)
 
-        v_s = [keep("v_s%d" % h, [P, HALF], U8) for h in range(2)]
-        v_w = [keep("v_w%d" % h, [P, HALF], U32) for h in range(2)]
-        for h in range(2):
-            nc.vector.tensor_copy(v_s[h][:], tab_s[:].indirect(listed(h * HALF, HALF)))
+        w_w = [keep("w_w%d" % u, [P, 2 * N], U8) for u in range(2)]
+        for u in range(2):
+            nc.vector.tensor_copy(w_w[u][:].bitcast(U16).rearrange("p (t m) -> p m t", t=PACK), w_raw[u][:].bitcast(U16).rearrange("p (m t) -> p m t", t=PACK))
+        ws_dealt = keep("ws_dealt", [P, 2 * N], U8)
+        nc.vector.tensor_copy(ws_dealt[:].rearrange("p (u t m) -> p u m t", u=2, t=PACK), ws_raw[:].rearrange("p (u m t) -> p u m t", u=2, t=PACK))
+        for q in range(4):
+            nc.scalar.dma_start(w_s[32 * q : 32 * q + 4, :].bitcast(I32), ws_dealt[4 * q : 4 * q + 4, :].bitcast(I32))
+        x0_rows = x0T.rearrange("(p t) c -> p t c", t=PACK)
+        x0 = []
+
+        def load_x0(t, tag):
+            x0.append(keep("x0_%d" % t, [P, T], F32, tag=tag))
+            nc.sync.dma_start(x0[t][:], x0_rows[:, t, :])
+
+
         dn_bf = keep("dn_bf", [P, R * PACK], BF16)
         dn_dealt = dn_bf[:].rearrange("p (t m i) -> p m i t", t=PACK, i=PACK)
-        dn_src = dn_raw[:].rearrange("p i (m t) -> p m i t", t=PACK)
-        nc.scalar.copy(dn_dealt[:, :64], dn_src[:, :64])
-        nc.vector.tensor_copy(dn_dealt[:, 64:], dn_src[:, 64:])
+        for u in range(2):
+            nc.scalar.copy(dn_dealt[:, 64 * u : 64 * (u + 1)], dn_raw[u][:].rearrange("p i (m t) -> p m i t", t=PACK))
+            if u == 0:
+                load_x0(0, "dn_raw0")
+        bias = keep("bias", [P, PACK], F32, tag="dn_raw1")
+        nc.sync.dma_start(bias[:], b.rearrange("(p t) -> p t", t=PACK))
+        bias1 = keep("bias1", [P, PACK], F32)
+        nc.gpsimd.tensor_scalar(bias1[:], bias[:], 1.0, 1.0, ALU.mult, ALU.add)
+        v_s_all = keep("v_s", [P, J], U8)
+        v_s = [v_s_all[:, :HALF], v_s_all[:, HALF:]]
+        v_w = [keep("v_w%d" % h, [P, HALF], U32) for h in range(2)]
+        nc.vector.tensor_copy(v_s_all[:], tab_s[:].indirect(offsets[:]))
         dn_w = keep("dn_w", [P, R], U32)
         dn_s = keep("dn_s", [P, R], U8)
         nc.vector.quantize_mx(out=dn_w[:].bitcast(FP8X4), scales=dn_s[:], in_=dn_bf[:])
+        load_x0(1, "dn_bf")
+        load_x0(2, "ws_dealt")
         for h, c0, width in ((0, 0, 256), (0, 256, 256), (1, 0, 512)):
             nc.vector.tensor_copy(v_w[h][:, c0 : c0 + width], tab_w[:].indirect(listed(h * HALF + c0, width)))
+        load_x0(3, "tab_w")
 
-        w_w = [keep("w_w%d" % u, [P, 2 * N], U8) for u in range(2)]
-        w_s = [keep("w_s%d" % u, [P, N], U8) for u in range(2)]
-        for u in range(2):
-            nc.vector.tensor_copy(w_w[u][:].bitcast(U16).rearrange("p (t m) -> p m t", t=PACK), w_raw[u][:].bitcast(U16).rearrange("p (m t) -> p m t", t=PACK))
-            nc.vector.tensor_copy(w_s[u][:].rearrange("p (t m) -> p m t", t=PACK), ws_raw[u][:].rearrange("p (m t) -> p m t", t=PACK))
-
-        h_w = [keep("h_w%d" % h, [P, HALF], U32) for h in range(2)]
+        x_first = [keep("x_first0", [P, HALF], F32)]
+        nc.vector.tensor_copy(x_first[0][:], x0[0][:].indirect(listed(0, HALF)))
         h_s = [keep("h_s%d" % h, [P, HALF], U8) for h in range(2)]
         h_bf = [keep("h_bf%d" % h, [P, HALF * PACK], BF16) for h in range(2)]
+        h_w = []
+        y_up = {}
+        res0 = keep("res0", [P, PACK, HALF], F32)
         for h in range(2):
             for c in range(HALF // SUB):
                 cols = slice(c * SUB, (c + 1) * SUB)
@@ -99,47 +111,60 @@ def tile_list_xcross_reluP_kernel(tc, tab_words, tab_scales, wb_words, wb_scales
                 for t in range(PACK):
                     rows = slice(t * P, (t + 1) * P)
                     nc.tensor.matmul_mx(out=hs[:, t, :], lhsT=dn_w[:, rows].bitcast(FP8X4), lhsT_scale=dn_s[:, rows],
-                                        rhs=v_w[h][:, cols].bitcast(FP8X4), rhs_scale=v_s[h][:, cols], start=True, stop=True)
+                                        rhs=v_w[h][:, cols].bitcast(FP8X4), rhs_scale=v_s_all[:, h * HALF + c * SUB : h * HALF + (c + 1) * SUB], start=True, stop=True)
                 nc.scalar.activation(h_bf[h][:, c * SUB * PACK : (c + 1) * SUB * PACK].rearrange("p (j t) -> p j t", t=PACK),
                                      hs[:].rearrange("p t j -> p j t"), ACT.Relu)
-            nc.vector.quantize_mx(out=h_w[h][:].bitcast(FP8X4), scales=h_s[h][:], in_=h_bf[h][:])
-
-        x_first = [keep("x_first%d" % h, [P, HALF], F32) for h in range(2)]
         for h in range(2):
-            nc.vector.tensor_copy(x_first[h][:], x0[0][:].indirect(listed(h * HALF, HALF)))
-        res = [keep("res%d" % h, [P, PACK, HALF], F32) for h in range(2)]
-        res_bf = [keep("res_bf%d" % g, [P, 256 * PACK], BF16) for g in range(4)]
+            h_w.append(keep("h_w%d" % h, [P, HALF], U32, tag=("dn_raw1", "x_first0")[h]))
+            nc.vector.quantize_mx(out=h_w[h][:].bitcast(FP8X4), scales=h_s[h][:], in_=h_bf[h][:])
+            if h == 0:
+                x_first.append(keep("x_first1", [P, HALF], F32, tag="h_bf0"))
+                nc.vector.tensor_copy(x_first[1][:], x0[0][:].indirect(listed(HALF, HALF)))
+            for t in range(PACK):
+                y = psum_y.tile([P, HALF], F32, name="y")
+                for u, (mw, ms) in enumerate(((v_w[h], v_s[h]), (h_w[h], h_s[h][:]))):
+                    nc.tensor.matmul_mx(out=y[:], lhsT=w_w[u][:, 2 * t * P : 2 * (t + 1) * P].bitcast(FP4X4), lhsT_scale=w_s[:, u * N + t * P : u * N + (t + 1) * P],
+                                        rhs=mw[:].bitcast(FP8X4), rhs_scale=ms, start=(u == 0), stop=(u == 1))
+                if (h, t) == (0, 0):
+                    nc.vector.scalar_tensor_tensor(res0[:, t, :], y[:], bias1[:, t : t + 1], x_first[0][:], ALU.add, ALU.mult)
+                elif t == 0:
+                    y_first = y
+                else:
+                    y_up[h, t] = keep("y_up%d%d" % (h, t), [P, HALF], F32)
+                    nc.scalar.activation(y_up[h, t][:], y[:], ACT.Identity, bias=bias1[:, t : t + 1])
+
         res_w = keep("res_w", [P, J], U32)
         res_s = keep("res_s", [P, J], U8)
         out_rows = out_0.rearrange("(p t) j -> p t j", t=PACK)
         out_words = out_1[0].rearrange("p j i -> p (j i)").bitcast(I32)
-        for h in range(2):
-            for t in range(PACK):
-                y = psum_y.tile([P, HALF], F32, name="y")
-                for u, (mw, ms) in enumerate(((v_w[h], v_s[h]), (h_w[h], h_s[h]))):
-                    nc.tensor.matmul_mx(out=y[:], lhsT=w_w[u][:, 2 * t * P : 2 * (t + 1) * P].bitcast(FP4X4), lhsT_scale=w_s[u][:, t * P : (t + 1) * P],
-                                        rhs=mw[:].bitcast(FP8X4), rhs_scale=ms[:], start=(u == 0), stop=(u == 1))
-                if t == 0:
-                    nc.vector.scalar_tensor_tensor(res[h][:, t, :], y[:], bias1[:, t : t + 1], x_first[h][:], ALU.add, ALU.mult)
-                else:
-                    y1 = ring.tile([P, HALF], F32, name="y1")
-                    nc.scalar.activation(y1[:], y[:], ACT.Identity, bias=bias1[:, t : t + 1])
-                    if t < 3:
-                        nc.vector.tensor_tensor(res[h][:, t, :], x0[t][:].indirect(listed(h * HALF, HALF)), y1[:], ALU.mult)
-                    else:
-                        for g in range(2):
-                            nc.vector.tensor_tensor(res[h][:, t, g * 256 : (g + 1) * 256], x0[t][:].indirect(listed(h * HALF + g * 256, 256)), y1[:, g * 256 : (g + 1) * 256], ALU.mult)
-                nc.sync.dma_start(out_rows[:, t, h * HALF : (h + 1) * HALF], res[h][:, t, :])
-            for g in range(2):
-                gg = 2 * h + g
-                dst = res_bf[gg][:].rearrange("p (c i t) -> p c t i", i=4, t=PACK)
-                src = res[h][:, :, g * 256 : (g + 1) * 256].rearrange("p t (c i) -> p c t i", i=4)
-                if gg == 3:
-                    nc.vector.tensor_copy(dst, src)
-                else:
-                    nc.scalar.copy(dst, src)
-                cols = slice(gg * 256, (gg + 1) * 256)
-                nc.vector.quantize_mx(out=res_w[:, cols].bitcast(FP8X4), scales=res_s[:, cols], in_=res_bf[gg][:])
-            nc.sync.dma_start(out_words[:, h * HALF : (h + 1) * HALF], res_w[:, h * HALF : (h + 1) * HALF].bitcast(I32))
+
+        def round_out(engine_copy, dst, src):
+            engine_copy(dst.rearrange("p (c i t) -> p c t i", i=4, t=PACK), src.rearrange("p t (c i) -> p c t i", i=4))
+
+        def quantise_out(g, src):
+            rounded = keep("rounded%d" % g, [P, QUARTER * PACK], BF16)
+            if g < 3:
+                round_out(nc.scalar.copy, rounded[:], src)
+            else:
+                round_out(nc.scalar.copy, rounded[:, : 96 * PACK], src[:, :, :96])
+                round_out(nc.vector.tensor_copy, rounded[:, 96 * PACK :], src[:, :, 96:])
+            cols = slice(g * QUARTER, (g + 1) * QUARTER)
+            nc.vector.quantize_mx(out=res_w[:, cols].bitcast(FP8X4), scales=res_s[:, cols], in_=rounded[:])
+
+        for t in range(1, PACK):
+            nc.vector.tensor_tensor(res0[:, t, :], x0[t][:].indirect(listed(0, HALF)), y_up[0, t][:], ALU.mult)
+        nc.sync.dma_start(out_rows[:, :, :HALF], res0[:])
+        for g in range(2):
+            quantise_out(g, res0[:, :, g * QUARTER : (g + 1) * QUARTER])
+        nc.sync.dma_start(out_words[:, :HALF], res_w[:, :HALF].bitcast(I32))
+        res1 = keep("res1", [P, 2, PACK, QUARTER], F32, tag="y_up03")
+        for g in range(2):
+            j0 = HALF + g * QUARTER
+            nc.vector.scalar_tensor_tensor(res1[:, g, 0, :], y_first[:, g * QUARTER : (g + 1) * QUARTER], bias1[:, 0:1], x_first[1][:, g * QUARTER : (g + 1) * QUARTER], ALU.add, ALU.mult)
+            for t in range(1, PACK):
+                nc.vector.tensor_tensor(res1[:, g, t, :], x0[t][:].indirect(listed(j0, QUARTER)), y_up[1, t][:, g * QUARTER : (g + 1) * QUARTER], ALU.mult)
+            nc.sync.dma_start(out_rows[:, :, j0 : j0 + QUARTER], res1[:, g])
+            quantise_out(2 + g, res1[:, g])
+            nc.sync.dma_start(out_words[:, j0 : j0 + QUARTER], res_w[:, j0 : j0 + QUARTER].bitcast(I32))
         for q in range(4):
             nc.scalar.dma_start(out_2[0, 4 * q : 4 * q + 4, :].bitcast(I32), res_s[32 * q : 32 * q + 4, :].bitcast(I32))

@@ -37,35 +37,31 @@ def tile_list_xcross_reluP_kernel(tc, tab_words, tab_scales, wb_words, wb_scales
             return offsets[:, j0 // 16 : (j0 + count) // 16]
 
         offsets = held.tile([P, J // 16], U16, name="offsets")
-        tab_s = keep("tab_s", [P, T], U8)
         ws_raw = keep("ws_raw", [P, 2 * N], U8)
-        w_s = keep("w_s", [P, 2 * N], U8)
+        tab_s = keep("tab_s", [P, T], U8)
+        nc.vector.memset(ws_raw[:].bitcast(I32), 0)
         nc.vector.memset(tab_s[:, : T // 2].bitcast(I32), 0)
         nc.gpsimd.memset(tab_s[:, T // 2 :].bitcast(I32), 0)
-        nc.vector.memset(ws_raw[:].bitcast(I32), 0)
-        nc.gpsimd.memset(w_s[:].bitcast(I32), 0)
         w_raw = [keep("w_raw%d" % u, [P, 2 * N], U8) for u in range(2)]
         dn_raw = [keep("dn_raw%d" % u, [P, PACK, R // 2], F32) for u in range(2)]
         dn_rows = dn.rearrange("(p i) r -> p i r", i=PACK)
         nc.sync.dma_start(offsets[:], offs)
         for u, words in enumerate((wb_words, upw_words)):
             nc.sync.dma_start(w_raw[u][:].bitcast(I32), words[0].bitcast(I32))
-        for q in range(4):
-            nc.sync.dma_start(tab_s[32 * q : 32 * q + 4, :].bitcast(I32), tab_scales[0, 4 * q : 4 * q + 4, :].bitcast(I32))
-        nc.sync.dma_start(dn_raw[0][:], dn_rows[:, :, : R // 2])
-        nc.sync.dma_start(dn_raw[1][:], dn_rows[:, :, R // 2 :])
         for u, scales in enumerate((wb_scales, upw_scales)):
             nc.sync.dma_start(ws_raw[:16, u * N : (u + 1) * N].bitcast(I32), scales[0].bitcast(I32))
+        nc.sync.dma_start(dn_raw[0][:], dn_rows[:, :, : R // 2])
+        for q in range(4):
+            nc.sync.dma_start(tab_s[32 * q : 32 * q + 4, :].bitcast(I32), tab_scales[0, 4 * q : 4 * q + 4, :].bitcast(I32))
+        nc.sync.dma_start(dn_raw[1][:], dn_rows[:, :, R // 2 :])
         tab_w = keep("tab_w", [P, T], U32)
         nc.sync.dma_start(tab_w[:].bitcast(I32), tab_words[0].rearrange("p t i -> p (t i)").bitcast(I32))
 
         w_w = [keep("w_w%d" % u, [P, 2 * N], U8) for u in range(2)]
         for u in range(2):
-            nc.vector.tensor_copy(w_w[u][:].bitcast(U16).rearrange("p (t m) -> p m t", t=PACK), w_raw[u][:].bitcast(U16).rearrange("p (m t) -> p m t", t=PACK))
-        ws_dealt = keep("ws_dealt", [P, 2 * N], U8)
-        nc.vector.tensor_copy(ws_dealt[:].rearrange("p (u t m) -> p u m t", u=2, t=PACK), ws_raw[:].rearrange("p (u m t) -> p u m t", u=2, t=PACK))
-        for q in range(4):
-            nc.scalar.dma_start(w_s[32 * q : 32 * q + 4, :].bitcast(I32), ws_dealt[4 * q : 4 * q + 4, :].bitcast(I32))
+            nc.vector.tensor_copy(w_w[u][:].bitcast(U16).rearrange("p (t m) -> p t m", t=PACK), w_raw[u][:].bitcast(U16).rearrange("p (m t) -> p t m", t=PACK))
+        w_s = keep("w_s", [P, 2 * N], U8)
+        nc.vector.tensor_copy(w_s[:].rearrange("p (u t m) -> p u t m", u=2, t=PACK), ws_raw[:].rearrange("p (u m t) -> p u t m", u=2, t=PACK))
         x0_rows = x0T.rearrange("(p t) c -> p t c", t=PACK)
         x0 = []
 
@@ -73,15 +69,17 @@ def tile_list_xcross_reluP_kernel(tc, tab_words, tab_scales, wb_words, wb_scales
             x0.append(keep("x0_%d" % t, [P, T], F32, tag=tag))
             nc.sync.dma_start(x0[t][:], x0_rows[:, t, :])
 
+        load_x0(0, None)
+        bias = keep("bias", [P, PACK], F32)
+        nc.sync.dma_start(bias[:], b.rearrange("(p t) -> p t", t=PACK))
+        for q in range(1, 4):
+            nc.sync.dma_start(w_s[32 * q : 32 * q + 4, :].bitcast(I32), w_s[4 * q : 4 * q + 4, :].bitcast(I32))
 
         dn_bf = keep("dn_bf", [P, R * PACK], BF16)
         dn_dealt = dn_bf[:].rearrange("p (t m i) -> p m i t", t=PACK, i=PACK)
         for u in range(2):
             nc.scalar.copy(dn_dealt[:, 64 * u : 64 * (u + 1)], dn_raw[u][:].rearrange("p i (m t) -> p m i t", t=PACK))
-            if u == 0:
-                load_x0(0, "dn_raw0")
-        bias = keep("bias", [P, PACK], F32, tag="dn_raw1")
-        nc.sync.dma_start(bias[:], b.rearrange("(p t) -> p t", t=PACK))
+            load_x0(1 + u, "dn_raw%d" % u)
         bias1 = keep("bias1", [P, PACK], F32)
         nc.gpsimd.tensor_scalar(bias1[:], bias[:], 1.0, 1.0, ALU.mult, ALU.add)
         v_s_all = keep("v_s", [P, J], U8)
@@ -91,11 +89,9 @@ def tile_list_xcross_reluP_kernel(tc, tab_words, tab_scales, wb_words, wb_scales
         dn_w = keep("dn_w", [P, R], U32)
         dn_s = keep("dn_s", [P, R], U8)
         nc.vector.quantize_mx(out=dn_w[:].bitcast(FP8X4), scales=dn_s[:], in_=dn_bf[:])
-        load_x0(1, "dn_bf")
-        load_x0(2, "ws_dealt")
+        load_x0(3, "dn_bf")
         for h, c0, width in ((0, 0, 256), (0, 256, 256), (1, 0, 512)):
             nc.vector.tensor_copy(v_w[h][:, c0 : c0 + width], tab_w[:].indirect(listed(h * HALF + c0, width)))
-        load_x0(3, "tab_w")
 
         x_first = [keep("x_first0", [P, HALF], F32)]
         nc.vector.tensor_copy(x_first[0][:], x0[0][:].indirect(listed(0, HALF)))
@@ -115,7 +111,7 @@ def tile_list_xcross_reluP_kernel(tc, tab_words, tab_scales, wb_words, wb_scales
                 nc.scalar.activation(h_bf[h][:, c * SUB * PACK : (c + 1) * SUB * PACK].rearrange("p (j t) -> p j t", t=PACK),
                                      hs[:].rearrange("p t j -> p j t"), ACT.Relu)
         for h in range(2):
-            h_w.append(keep("h_w%d" % h, [P, HALF], U32, tag=("dn_raw1", "x_first0")[h]))
+            h_w.append(keep("h_w%d" % h, [P, HALF], U32, tag=("bias", "x_first0")[h]))
             nc.vector.quantize_mx(out=h_w[h][:].bitcast(FP8X4), scales=h_s[h][:], in_=h_bf[h][:])
             if h == 0:
                 x_first.append(keep("x_first1", [P, HALF], F32, tag="h_bf0"))
@@ -146,25 +142,27 @@ def tile_list_xcross_reluP_kernel(tc, tab_words, tab_scales, wb_words, wb_scales
             if g < 3:
                 round_out(nc.scalar.copy, rounded[:], src)
             else:
-                round_out(nc.scalar.copy, rounded[:, : 96 * PACK], src[:, :, :96])
-                round_out(nc.vector.tensor_copy, rounded[:, 96 * PACK :], src[:, :, 96:])
+                round_out(nc.vector.tensor_copy, rounded[:], src)
             cols = slice(g * QUARTER, (g + 1) * QUARTER)
             nc.vector.quantize_mx(out=res_w[:, cols].bitcast(FP8X4), scales=res_s[:, cols], in_=rounded[:])
 
+        nc.sync.dma_start(out_rows[:, 0, :HALF], res0[:, 0, :])
         for t in range(1, PACK):
             nc.vector.tensor_tensor(res0[:, t, :], x0[t][:].indirect(listed(0, HALF)), y_up[0, t][:], ALU.mult)
-        nc.sync.dma_start(out_rows[:, :, :HALF], res0[:])
+            nc.sync.dma_start(out_rows[:, t, :HALF], res0[:, t, :])
         for g in range(2):
             quantise_out(g, res0[:, :, g * QUARTER : (g + 1) * QUARTER])
         nc.sync.dma_start(out_words[:, :HALF], res_w[:, :HALF].bitcast(I32))
-        res1 = keep("res1", [P, 2, PACK, QUARTER], F32, tag="y_up03")
         for g in range(2):
             j0 = HALF + g * QUARTER
-            nc.vector.scalar_tensor_tensor(res1[:, g, 0, :], y_first[:, g * QUARTER : (g + 1) * QUARTER], bias1[:, 0:1], x_first[1][:, g * QUARTER : (g + 1) * QUARTER], ALU.add, ALU.mult)
+            res1 = keep("res1%d" % g, [P, PACK, QUARTER], F32, tag=("res10", "y_up03")[g])
+            nc.vector.scalar_tensor_tensor(res1[:, 0, :], y_first[:, g * QUARTER : (g + 1) * QUARTER], bias1[:, 0:1], x_first[1][:, g * QUARTER : (g + 1) * QUARTER], ALU.add, ALU.mult)
             for t in range(1, PACK):
-                nc.vector.tensor_tensor(res1[:, g, t, :], x0[t][:].indirect(listed(j0, QUARTER)), y_up[1, t][:, g * QUARTER : (g + 1) * QUARTER], ALU.mult)
-            nc.sync.dma_start(out_rows[:, :, j0 : j0 + QUARTER], res1[:, g])
-            quantise_out(2 + g, res1[:, g])
+                nc.vector.tensor_tensor(res1[:, t, :], x0[t][:].indirect(listed(j0, QUARTER)), y_up[1, t][:, g * QUARTER : (g + 1) * QUARTER], ALU.mult)
+                if t == 2:
+                    nc.sync.dma_start(out_rows[:, :3, j0 : j0 + QUARTER], res1[:, :3, :])
+            nc.sync.dma_start(out_rows[:, 3, j0 : j0 + QUARTER], res1[:, 3, :])
+            quantise_out(2 + g, res1[:])
             nc.sync.dma_start(out_words[:, j0 : j0 + QUARTER], res_w[:, j0 : j0 + QUARTER].bitcast(I32))
         for q in range(4):
             nc.scalar.dma_start(out_2[0, 4 * q : 4 * q + 4, :].bitcast(I32), res_s[32 * q : 32 * q + 4, :].bitcast(I32))

@@ -27,8 +27,7 @@ def tile_list_xcross_reluP_kernel(tc, tab_words, tab_scales, wb_words, wb_scales
     nc = tc.nc
     with ExitStack() as ctx:
         held = ctx.enter_context(tc.tile_pool(name="held", bufs=1))
-        psum_h = ctx.enter_context(tc.psum_pool(name="psum_h", bufs=3))
-        psum_y = ctx.enter_context(tc.psum_pool(name="psum_y", bufs=5))
+        psum = ctx.enter_context(tc.psum_pool(name="psum", bufs=1))
 
         def keep(name, shape, dtype, tag=None):
             return held.tile(shape, dtype, name=name, tag=tag or name, align_bytes=64)
@@ -39,29 +38,23 @@ def tile_list_xcross_reluP_kernel(tc, tab_words, tab_scales, wb_words, wb_scales
         offsets = held.tile([P, J // 16], U16, name="offsets")
         ws_raw = keep("ws_raw", [P, 2 * N], U8)
         tab_s = keep("tab_s", [P, T], U8)
-        nc.vector.memset(ws_raw[:].bitcast(I32), 0)
         nc.vector.memset(tab_s[:, : T // 2].bitcast(I32), 0)
         nc.gpsimd.memset(tab_s[:, T // 2 :].bitcast(I32), 0)
+        nc.gpsimd.memset(ws_raw[:].bitcast(I32), 0)
         w_raw = [keep("w_raw%d" % u, [P, 2 * N], U8) for u in range(2)]
         dn_raw = [keep("dn_raw%d" % u, [P, PACK, R // 2], F32) for u in range(2)]
         dn_rows = dn.rearrange("(p i) r -> p i r", i=PACK)
         nc.sync.dma_start(offsets[:], offs)
         for u, words in enumerate((wb_words, upw_words)):
             nc.sync.dma_start(w_raw[u][:].bitcast(I32), words[0].bitcast(I32))
-        for u, scales in enumerate((wb_scales, upw_scales)):
-            nc.sync.dma_start(ws_raw[:16, u * N : (u + 1) * N].bitcast(I32), scales[0].bitcast(I32))
         nc.sync.dma_start(dn_raw[0][:], dn_rows[:, :, : R // 2])
         for q in range(4):
             nc.sync.dma_start(tab_s[32 * q : 32 * q + 4, :].bitcast(I32), tab_scales[0, 4 * q : 4 * q + 4, :].bitcast(I32))
         nc.sync.dma_start(dn_raw[1][:], dn_rows[:, :, R // 2 :])
+        for u, scales in enumerate((wb_scales, upw_scales)):
+            nc.sync.dma_start(ws_raw[:16, u * N : (u + 1) * N].bitcast(I32), scales[0].bitcast(I32))
         tab_w = keep("tab_w", [P, T], U32)
         nc.sync.dma_start(tab_w[:].bitcast(I32), tab_words[0].rearrange("p t i -> p (t i)").bitcast(I32))
-
-        w_w = [keep("w_w%d" % u, [P, 2 * N], U8) for u in range(2)]
-        for u in range(2):
-            nc.vector.tensor_copy(w_w[u][:].bitcast(U16).rearrange("p (t m) -> p t m", t=PACK), w_raw[u][:].bitcast(U16).rearrange("p (m t) -> p t m", t=PACK))
-        w_s = keep("w_s", [P, 2 * N], U8)
-        nc.vector.tensor_copy(w_s[:].rearrange("p (u t m) -> p u t m", u=2, t=PACK), ws_raw[:].rearrange("p (u m t) -> p u t m", u=2, t=PACK))
         x0_rows = x0T.rearrange("(p t) c -> p t c", t=PACK)
         x0 = []
 
@@ -72,97 +65,128 @@ def tile_list_xcross_reluP_kernel(tc, tab_words, tab_scales, wb_words, wb_scales
         load_x0(0, None)
         bias = keep("bias", [P, PACK], F32)
         nc.sync.dma_start(bias[:], b.rearrange("(p t) -> p t", t=PACK))
+
+        w_w = [keep("w_w%d" % u, [P, 2 * N], U8) for u in range(2)]
+        for u in range(2):
+            nc.vector.tensor_copy(w_w[u][:].bitcast(U16).rearrange("p (t m) -> p t m", t=PACK), w_raw[u][:].bitcast(U16).rearrange("p (m t) -> p t m", t=PACK))
+        v_s_all = keep("v_s", [P, J], U8)
+        v_s = [v_s_all[:, :HALF], v_s_all[:, HALF:]]
+        nc.vector.tensor_copy(v_s_all[:], tab_s[:].indirect(offsets[:]))
+        w_s = keep("w_s", [P, 2 * N], U8)
+        nc.vector.tensor_copy(w_s[:].rearrange("p (u t m) -> p u t m", u=2, t=PACK), ws_raw[:].rearrange("p (u m t) -> p u t m", u=2, t=PACK))
         for q in range(1, 4):
             nc.sync.dma_start(w_s[32 * q : 32 * q + 4, :].bitcast(I32), w_s[4 * q : 4 * q + 4, :].bitcast(I32))
-
+        load_x0(1, "ws_raw")
         dn_bf = keep("dn_bf", [P, R * PACK], BF16)
         dn_dealt = dn_bf[:].rearrange("p (t m i) -> p m i t", t=PACK, i=PACK)
         for u in range(2):
             nc.scalar.copy(dn_dealt[:, 64 * u : 64 * (u + 1)], dn_raw[u][:].rearrange("p i (m t) -> p m i t", t=PACK))
-            load_x0(1 + u, "dn_raw%d" % u)
         bias1 = keep("bias1", [P, PACK], F32)
         nc.gpsimd.tensor_scalar(bias1[:], bias[:], 1.0, 1.0, ALU.mult, ALU.add)
-        v_s_all = keep("v_s", [P, J], U8)
-        v_s = [v_s_all[:, :HALF], v_s_all[:, HALF:]]
-        v_w = [keep("v_w%d" % h, [P, HALF], U32) for h in range(2)]
-        nc.vector.tensor_copy(v_s_all[:], tab_s[:].indirect(offsets[:]))
         dn_w = keep("dn_w", [P, R], U32)
         dn_s = keep("dn_s", [P, R], U8)
         nc.vector.quantize_mx(out=dn_w[:].bitcast(FP8X4), scales=dn_s[:], in_=dn_bf[:])
-        load_x0(3, "dn_bf")
+        load_x0(2, "dn_raw1")
+        for bank in (3, 4):
+            warm = psum.tile([P, HALF], F32, name="warm%d" % bank, tag="bank%d" % bank)
+            nc.tensor.matmul_mx(out=warm[:], lhsT=dn_w[:, :P].bitcast(FP8X4), lhsT_scale=dn_s[:, :P], rhs=dn_w[:].bitcast(FP8X4), rhs_scale=dn_s[:], start=True, stop=True)
+        v_w = [keep("v_w%d" % h, [P, HALF], U32, tag=("dn_bf", "v_w1")[h]) for h in range(2)]
         for h, c0, width in ((0, 0, 256), (0, 256, 256), (1, 0, 512)):
             nc.vector.tensor_copy(v_w[h][:, c0 : c0 + width], tab_w[:].indirect(listed(h * HALF + c0, width)))
+        load_x0(3, "tab_w")
 
-        x_first = [keep("x_first0", [P, HALF], F32)]
-        nc.vector.tensor_copy(x_first[0][:], x0[0][:].indirect(listed(0, HALF)))
-        h_s = [keep("h_s%d" % h, [P, HALF], U8) for h in range(2)]
-        h_bf = [keep("h_bf%d" % h, [P, HALF * PACK], BF16) for h in range(2)]
-        h_w = []
-        y_up = {}
-        res0 = keep("res0", [P, PACK, HALF], F32)
-        for h in range(2):
-            for c in range(HALF // SUB):
-                cols = slice(c * SUB, (c + 1) * SUB)
-                hs = psum_h.tile([P, PACK, SUB], F32, name="hs")
-                for t in range(PACK):
-                    rows = slice(t * P, (t + 1) * P)
-                    nc.tensor.matmul_mx(out=hs[:, t, :], lhsT=dn_w[:, rows].bitcast(FP8X4), lhsT_scale=dn_s[:, rows],
-                                        rhs=v_w[h][:, cols].bitcast(FP8X4), rhs_scale=v_s_all[:, h * HALF + c * SUB : h * HALF + (c + 1) * SUB], start=True, stop=True)
-                nc.scalar.activation(h_bf[h][:, c * SUB * PACK : (c + 1) * SUB * PACK].rearrange("p (j t) -> p j t", t=PACK),
-                                     hs[:].rearrange("p t j -> p j t"), ACT.Relu)
-        for h in range(2):
-            h_w.append(keep("h_w%d" % h, [P, HALF], U32, tag=("bias", "x_first0")[h]))
-            nc.vector.quantize_mx(out=h_w[h][:].bitcast(FP8X4), scales=h_s[h][:], in_=h_bf[h][:])
-            if h == 0:
-                x_first.append(keep("x_first1", [P, HALF], F32, tag="h_bf0"))
-                nc.vector.tensor_copy(x_first[1][:], x0[0][:].indirect(listed(HALF, HALF)))
+        h_bf = [keep("h_bf%d" % g, [P, width * PACK], BF16) for g, width in enumerate((QUARTER, QUARTER, HALF))]
+        for c in range(J // SUB):
+            h, c0 = divmod(c * SUB, HALF)
+            g, g0 = (c // 2, (c % 2) * SUB) if h == 0 else (2, c0)
+            hs = psum.tile([P, PACK, SUB], F32, name="hs%d" % c, tag="bank%d" % (c % 3))
             for t in range(PACK):
-                y = psum_y.tile([P, HALF], F32, name="y")
+                rows = slice(t * P, (t + 1) * P)
+                nc.tensor.matmul_mx(out=hs[:, t, :], lhsT=dn_w[:, rows].bitcast(FP8X4), lhsT_scale=dn_s[:, rows],
+                                    rhs=v_w[h][:, c0 : c0 + SUB].bitcast(FP8X4), rhs_scale=v_s_all[:, c * SUB : (c + 1) * SUB], start=True, stop=True)
+            nc.scalar.activation(h_bf[g][:, g0 * PACK : (g0 + SUB) * PACK].rearrange("p (j t) -> p j t", t=PACK),
+                                 hs[:].rearrange("p t j -> p j t"), ACT.Relu)
+
+        h_s = [keep("h_s%d" % h, [P, HALF], U8) for h in range(2)]
+        h_w = [keep("h_w0", [P, HALF], U32)]
+        for u in range(2):
+            cols = slice(u * QUARTER, (u + 1) * QUARTER)
+            nc.vector.quantize_mx(out=h_w[0][:, cols].bitcast(FP8X4), scales=h_s[0][:, cols], in_=h_bf[u][:])
+        x_first = [keep("x_first%d" % h, [P, HALF], F32, tag=("x_first0", "h_bf1")[h]) for h in range(2)]
+        for h in range(2):
+            nc.vector.tensor_copy(x_first[h][:], x0[0][:].indirect(listed(h * HALF, HALF)))
+
+        res0 = keep("res0", [P, PACK, HALF], F32)
+        res1 = [keep("res1%d" % g, [P, PACK, QUARTER], F32) for g in range(2)]
+        y_up = {}
+        for h in range(2):
+            if h == 1:
+                h_w.append(keep("h_w1", [P, HALF], U32, tag="x_first0"))
+                nc.vector.quantize_mx(out=h_w[1][:].bitcast(FP8X4), scales=h_s[1][:], in_=h_bf[2][:])
+            for t in range(PACK):
+                y = psum.tile([P, HALF], F32, name="y%d%d" % (h, t), tag="bank%d" % ((3, 4, 5, 6), (7, 2, 0, 1))[h][t])
                 for u, (mw, ms) in enumerate(((v_w[h], v_s[h]), (h_w[h], h_s[h][:]))):
                     nc.tensor.matmul_mx(out=y[:], lhsT=w_w[u][:, 2 * t * P : 2 * (t + 1) * P].bitcast(FP4X4), lhsT_scale=w_s[:, u * N + t * P : u * N + (t + 1) * P],
                                         rhs=mw[:].bitcast(FP8X4), rhs_scale=ms, start=(u == 0), stop=(u == 1))
                 if (h, t) == (0, 0):
                     nc.vector.scalar_tensor_tensor(res0[:, t, :], y[:], bias1[:, t : t + 1], x_first[0][:], ALU.add, ALU.mult)
                 elif t == 0:
-                    y_first = y
+                    for g in range(2):
+                        cols = slice(g * QUARTER, (g + 1) * QUARTER)
+                        nc.vector.scalar_tensor_tensor(res1[g][:, 0, :], y[:, cols], bias1[:, :1], x_first[1][:, cols], ALU.add, ALU.mult)
                 else:
-                    y_up[h, t] = keep("y_up%d%d" % (h, t), [P, HALF], F32)
-                    nc.scalar.activation(y_up[h, t][:], y[:], ACT.Identity, bias=bias1[:, t : t + 1])
+                    if t == 3:
+                        y_up[h, t] = res1[h][:, 1:3, :].rearrange("p a j -> p (a j)")
+                    else:
+                        y_up[h, t] = keep("y_up%d%d" % (h, t), [P, HALF], F32)[:]
+                    nc.scalar.activation(y_up[h, t], y[:], ACT.Identity, bias=bias1[:, t : t + 1])
 
         res_w = keep("res_w", [P, J], U32)
         res_s = keep("res_s", [P, J], U8)
         out_rows = out_0.rearrange("(p t) j -> p t j", t=PACK)
         out_words = out_1[0].rearrange("p j i -> p (j i)").bitcast(I32)
 
+        def cross(dst, t, j0, count):
+            h, c0 = divmod(j0, HALF)
+            nc.vector.tensor_tensor(dst, x0[t][:].indirect(listed(j0, count)), y_up[h, t][:, c0 : c0 + count], ALU.mult)
+
         def round_out(engine_copy, dst, src):
             engine_copy(dst.rearrange("p (c i t) -> p c t i", i=4, t=PACK), src.rearrange("p t (c i) -> p c t i", i=4))
 
-        def quantise_out(g, src):
-            rounded = keep("rounded%d" % g, [P, QUARTER * PACK], BF16)
-            if g < 3:
-                round_out(nc.scalar.copy, rounded[:], src)
-            else:
-                round_out(nc.vector.tensor_copy, rounded[:], src)
-            cols = slice(g * QUARTER, (g + 1) * QUARTER)
-            nc.vector.quantize_mx(out=res_w[:, cols].bitcast(FP8X4), scales=res_s[:, cols], in_=rounded[:])
+        def quantise_out(g, j0, count):
+            cols = slice(j0, j0 + count)
+            nc.vector.quantize_mx(out=res_w[:, cols].bitcast(FP8X4), scales=res_s[:, cols], in_=rounded[g][:])
 
+        rounded = [keep("rounded%d" % g, [P, width * PACK], BF16) for g, width in enumerate((HALF, QUARTER, QUARTER))]
         nc.sync.dma_start(out_rows[:, 0, :HALF], res0[:, 0, :])
-        for t in range(1, PACK):
-            nc.vector.tensor_tensor(res0[:, t, :], x0[t][:].indirect(listed(0, HALF)), y_up[0, t][:], ALU.mult)
-            nc.sync.dma_start(out_rows[:, t, :HALF], res0[:, t, :])
-        for g in range(2):
-            quantise_out(g, res0[:, :, g * QUARTER : (g + 1) * QUARTER])
-        nc.sync.dma_start(out_words[:, :HALF], res_w[:, :HALF].bitcast(I32))
         for g in range(2):
             j0 = HALF + g * QUARTER
-            res1 = keep("res1%d" % g, [P, PACK, QUARTER], F32, tag=("res10", "y_up03")[g])
-            nc.vector.scalar_tensor_tensor(res1[:, 0, :], y_first[:, g * QUARTER : (g + 1) * QUARTER], bias1[:, 0:1], x_first[1][:, g * QUARTER : (g + 1) * QUARTER], ALU.add, ALU.mult)
-            for t in range(1, PACK):
-                nc.vector.tensor_tensor(res1[:, t, :], x0[t][:].indirect(listed(j0, QUARTER)), y_up[1, t][:, g * QUARTER : (g + 1) * QUARTER], ALU.mult)
-                if t == 2:
-                    nc.sync.dma_start(out_rows[:, :3, j0 : j0 + QUARTER], res1[:, :3, :])
-            nc.sync.dma_start(out_rows[:, 3, j0 : j0 + QUARTER], res1[:, 3, :])
-            quantise_out(2 + g, res1[:])
-            nc.sync.dma_start(out_words[:, j0 : j0 + QUARTER], res_w[:, j0 : j0 + QUARTER].bitcast(I32))
+            nc.sync.dma_start(out_rows[:, 0, j0 : j0 + QUARTER], res1[g][:, 0, :])
+        for t in (1, 2):
+            cross(res0[:, t, :], t, 0, HALF)
+            nc.sync.dma_start(out_rows[:, t, :HALF], res0[:, t, :])
+        for g in range(2):
+            cross(res0[:, 3, g * QUARTER : (g + 1) * QUARTER], 3, g * QUARTER, QUARTER)
+        nc.sync.dma_start(out_rows[:, 3, :HALF], res0[:, 3, :])
+        for g in range(2):
+            round_out(nc.scalar.copy, rounded[0][:, g * QUARTER * PACK : (g + 1) * QUARTER * PACK], res0[:, :, g * QUARTER : (g + 1) * QUARTER])
+        j0 = HALF
+        for t in (1, 2, 3):
+            cross(res1[0][:, t, :], t, j0, QUARTER)
+        nc.sync.dma_start(out_rows[:, 1:, j0 : j0 + QUARTER], res1[0][:, 1:, :])
+        round_out(nc.scalar.copy, rounded[1][:], res1[0][:])
+        j0 = HALF + QUARTER
+        cross(res1[1][:, 1, :], 1, j0, QUARTER)
+        quantise_out(0, 0, HALF)
+        nc.sync.dma_start(out_words[:, :HALF], res_w[:, :HALF].bitcast(I32))
+        for t in (3, 2):
+            cross(res1[1][:, t, :], t, j0, QUARTER)
+        nc.sync.dma_start(out_rows[:, 1:, j0 : j0 + QUARTER], res1[1][:, 1:, :])
+        round_out(nc.scalar.copy, rounded[2][:, : SUB * PACK], res1[1][:, :, :SUB])
+        quantise_out(1, HALF, QUARTER)
+        nc.sync.dma_start(out_words[:, HALF:j0], res_w[:, HALF:j0].bitcast(I32))
+        round_out(nc.vector.tensor_copy, rounded[2][:, SUB * PACK :], res1[1][:, :, SUB:])
+        quantise_out(2, j0, QUARTER)
+        nc.sync.dma_start(out_words[:, j0:], res_w[:, j0:].bitcast(I32))
         for q in range(4):
             nc.scalar.dma_start(out_2[0, 4 * q : 4 * q + 4, :].bitcast(I32), res_s[32 * q : 32 * q + 4, :].bitcast(I32))

@@ -35,24 +35,24 @@ def tile_list_xcross_reluP_kernel(tc, tab_words, tab_scales, wb_words, wb_scales
         def listed(j0, count):
             return offsets[:, j0 // 16 : (j0 + count) // 16]
 
+        rows16 = slice(16, 32)
         offsets = held.tile([P, J // 16], U16, name="offsets")
         ws_raw = keep("ws_raw", [P, 2 * N], U8)
         tab_s = keep("tab_s", [P, T], U8)
-        nc.vector.memset(tab_s[:, : T // 2].bitcast(I32), 0)
-        nc.gpsimd.memset(tab_s[:, T // 2 :].bitcast(I32), 0)
-        nc.gpsimd.memset(ws_raw[:].bitcast(I32), 0)
-        w_raw = [keep("w_raw%d" % u, [P, 2 * N], U8) for u in range(2)]
-        dn_raw = [keep("dn_raw%d" % u, [P, PACK, R // 2], F32) for u in range(2)]
-        dn_rows = dn.rearrange("(p i) r -> p i r", i=PACK)
+        v_s_all = keep("v_s", [P, J], U8)
+        for dead in (slice(0, 16), slice(32, 64), slice(64, P)):
+            nc.vector.memset(tab_s[dead, :].bitcast(I32), 0)
+            nc.gpsimd.memset(ws_raw[dead, :].bitcast(I32), 0)
+        nc.gpsimd.memset(v_s_all[:].bitcast(I32), 0)
         nc.sync.dma_start(offsets[:], offs)
+        nc.sync.dma_start(tab_s[rows16, :].bitcast(I32), tab_scales[0].bitcast(I32))
+        for u, scales in enumerate((wb_scales, upw_scales)):
+            nc.sync.dma_start(ws_raw[rows16, u * N : (u + 1) * N].bitcast(I32), scales[0].bitcast(I32))
+        dn_raw = keep("dn_raw", [P, PACK, R], F32)
+        nc.sync.dma_start(dn_raw[:], dn.rearrange("(p i) r -> p i r", i=PACK))
+        w_raw = [keep("w_raw%d" % u, [P, 2 * N], U8) for u in range(2)]
         for u, words in enumerate((wb_words, upw_words)):
             nc.sync.dma_start(w_raw[u][:].bitcast(I32), words[0].bitcast(I32))
-        nc.sync.dma_start(dn_raw[0][:], dn_rows[:, :, : R // 2])
-        for q in range(4):
-            nc.sync.dma_start(tab_s[32 * q : 32 * q + 4, :].bitcast(I32), tab_scales[0, 4 * q : 4 * q + 4, :].bitcast(I32))
-        nc.sync.dma_start(dn_raw[1][:], dn_rows[:, :, R // 2 :])
-        for u, scales in enumerate((wb_scales, upw_scales)):
-            nc.sync.dma_start(ws_raw[:16, u * N : (u + 1) * N].bitcast(I32), scales[0].bitcast(I32))
         tab_w = keep("tab_w", [P, T], U32)
         nc.sync.dma_start(tab_w[:].bitcast(I32), tab_words[0].rearrange("p t i -> p (t i)").bitcast(I32))
         x0_rows = x0T.rearrange("(p t) c -> p t c", t=PACK)
@@ -62,44 +62,46 @@ def tile_list_xcross_reluP_kernel(tc, tab_words, tab_scales, wb_words, wb_scales
             x0.append(keep("x0_%d" % t, [P, T], F32, tag=tag))
             nc.sync.dma_start(x0[t][:], x0_rows[:, t, :])
 
-        load_x0(0, None)
+        def to_quadrants(plane, rows):
+            for q in range(4):
+                nc.sync.dma_start(plane[32 * q : 32 * q + 4, :].bitcast(I32), rows[16 + 4 * q : 20 + 4 * q, :].bitcast(I32))
+
+        v_rows = keep("v_rows", [P, J], U8)
+        nc.vector.tensor_copy(v_rows[:], tab_s[:].indirect(offsets[:]))
+        to_quadrants(v_s_all, v_rows)
+        v_s = [v_s_all[:, :HALF], v_s_all[:, HALF:]]
+        w_s = keep("w_s", [P, 2 * N], U8)
+        nc.vector.tensor_copy(w_s[:].rearrange("p (u t m) -> p u t m", u=2, t=PACK), ws_raw[:].rearrange("p (u m t) -> p u t m", u=2, t=PACK))
+        load_x0(0, "ws_raw")
         bias = keep("bias", [P, PACK], F32)
         nc.sync.dma_start(bias[:], b.rearrange("(p t) -> p t", t=PACK))
-
+        to_quadrants(w_s, w_s)
         w_w = [keep("w_w%d" % u, [P, 2 * N], U8) for u in range(2)]
         for u in range(2):
             nc.vector.tensor_copy(w_w[u][:].bitcast(U16).rearrange("p (t m) -> p t m", t=PACK), w_raw[u][:].bitcast(U16).rearrange("p (m t) -> p t m", t=PACK))
-        v_s_all = keep("v_s", [P, J], U8)
-        v_s = [v_s_all[:, :HALF], v_s_all[:, HALF:]]
-        nc.vector.tensor_copy(v_s_all[:], tab_s[:].indirect(offsets[:]))
-        w_s = keep("w_s", [P, 2 * N], U8)
-        nc.vector.tensor_copy(w_s[:].rearrange("p (u t m) -> p u t m", u=2, t=PACK), ws_raw[:].rearrange("p (u m t) -> p u t m", u=2, t=PACK))
-        for q in range(1, 4):
-            nc.sync.dma_start(w_s[32 * q : 32 * q + 4, :].bitcast(I32), w_s[4 * q : 4 * q + 4, :].bitcast(I32))
-        load_x0(1, "ws_raw")
+        load_x0(1, "w_raw1")
         dn_bf = keep("dn_bf", [P, R * PACK], BF16)
         dn_dealt = dn_bf[:].rearrange("p (t m i) -> p m i t", t=PACK, i=PACK)
-        for u in range(2):
-            nc.scalar.copy(dn_dealt[:, 64 * u : 64 * (u + 1)], dn_raw[u][:].rearrange("p i (m t) -> p m i t", t=PACK))
+        dn_rows = dn_raw[:].rearrange("p i (m t) -> p m i t", t=PACK)
+        nc.scalar.copy(dn_dealt[:, :88], dn_rows[:, :88])
+        nc.vector.tensor_copy(dn_dealt[:, 88:], dn_rows[:, 88:])
+        load_x0(2, "dn_raw")
+        load_x0(3, "v_rows")
         bias1 = keep("bias1", [P, PACK], F32)
         nc.gpsimd.tensor_scalar(bias1[:], bias[:], 1.0, 1.0, ALU.mult, ALU.add)
         dn_w = keep("dn_w", [P, R], U32)
         dn_s = keep("dn_s", [P, R], U8)
         nc.vector.quantize_mx(out=dn_w[:].bitcast(FP8X4), scales=dn_s[:], in_=dn_bf[:])
-        load_x0(2, "dn_raw1")
-        for bank in (3, 4):
-            warm = psum.tile([P, HALF], F32, name="warm%d" % bank, tag="bank%d" % bank)
-            nc.tensor.matmul_mx(out=warm[:], lhsT=dn_w[:, :P].bitcast(FP8X4), lhsT_scale=dn_s[:, :P], rhs=dn_w[:].bitcast(FP8X4), rhs_scale=dn_s[:], start=True, stop=True)
-        v_w = [keep("v_w%d" % h, [P, HALF], U32, tag=("dn_bf", "v_w1")[h]) for h in range(2)]
+        v_w_all = keep("v_w", [P, J], U32, tag="dn_bf")
+        v_w = [v_w_all[:, :HALF], v_w_all[:, HALF:]]
         for h, c0, width in ((0, 0, 256), (0, 256, 256), (1, 0, 512)):
             nc.vector.tensor_copy(v_w[h][:, c0 : c0 + width], tab_w[:].indirect(listed(h * HALF + c0, width)))
-        load_x0(3, "tab_w")
 
         h_bf = [keep("h_bf%d" % g, [P, width * PACK], BF16) for g, width in enumerate((QUARTER, QUARTER, HALF))]
         for c in range(J // SUB):
             h, c0 = divmod(c * SUB, HALF)
             g, g0 = (c // 2, (c % 2) * SUB) if h == 0 else (2, c0)
-            hs = psum.tile([P, PACK, SUB], F32, name="hs%d" % c, tag="bank%d" % (c % 3))
+            hs = psum.tile([P, PACK, SUB], F32, name="hs%d" % c, tag="bank%d" % c)
             for t in range(PACK):
                 rows = slice(t * P, (t + 1) * P)
                 nc.tensor.matmul_mx(out=hs[:, t, :], lhsT=dn_w[:, rows].bitcast(FP8X4), lhsT_scale=dn_s[:, rows],
@@ -124,10 +126,10 @@ def tile_list_xcross_reluP_kernel(tc, tab_words, tab_scales, wb_words, wb_scales
                 h_w.append(keep("h_w1", [P, HALF], U32, tag="x_first0"))
                 nc.vector.quantize_mx(out=h_w[1][:].bitcast(FP8X4), scales=h_s[1][:], in_=h_bf[2][:])
             for t in range(PACK):
-                y = psum.tile([P, HALF], F32, name="y%d%d" % (h, t), tag="bank%d" % ((3, 4, 5, 6), (7, 2, 0, 1))[h][t])
-                for u, (mw, ms) in enumerate(((v_w[h], v_s[h]), (h_w[h], h_s[h][:]))):
+                y = psum.tile([P, HALF], F32, name="y%d%d" % (h, t), tag="bank%d" % (PACK * h + t))
+                for u, (mw, ms) in enumerate(((v_w[h], v_s[h]), (h_w[h][:], h_s[h][:]))):
                     nc.tensor.matmul_mx(out=y[:], lhsT=w_w[u][:, 2 * t * P : 2 * (t + 1) * P].bitcast(FP4X4), lhsT_scale=w_s[:, u * N + t * P : u * N + (t + 1) * P],
-                                        rhs=mw[:].bitcast(FP8X4), rhs_scale=ms, start=(u == 0), stop=(u == 1))
+                                        rhs=mw.bitcast(FP8X4), rhs_scale=ms, start=(u == 0), stop=(u == 1))
                 if (h, t) == (0, 0):
                     nc.vector.scalar_tensor_tensor(res0[:, t, :], y[:], bias1[:, t : t + 1], x_first[0][:], ALU.add, ALU.mult)
                 elif t == 0:

@@ -97,34 +97,27 @@ def tile_list_xcross_reluP_kernel(tc, tab_words, tab_scales, wb_words, wb_scales
         for h, c0, width in ((0, 0, 256), (0, 256, 256), (1, 0, 512)):
             nc.vector.tensor_copy(v_w[h][:, c0 : c0 + width], tab_w[:].indirect(listed(h * HALF + c0, width)))
 
-        h_bf = [keep("h_bf%d" % g, [P, width * PACK], BF16) for g, width in enumerate((QUARTER, QUARTER, HALF))]
-        for c in range(J // SUB):
-            h, c0 = divmod(c * SUB, HALF)
-            g, g0 = (c // 2, (c % 2) * SUB) if h == 0 else (2, c0)
-            hs = psum.tile([P, PACK, SUB], F32, name="hs%d" % c, tag="bank%d" % c)
-            for t in range(PACK):
-                rows = slice(t * P, (t + 1) * P)
-                nc.tensor.matmul_mx(out=hs[:, t, :], lhsT=dn_w[:, rows].bitcast(FP8X4), lhsT_scale=dn_s[:, rows],
-                                    rhs=v_w[h][:, c0 : c0 + SUB].bitcast(FP8X4), rhs_scale=v_s_all[:, c * SUB : (c + 1) * SUB], start=True, stop=True)
-            nc.scalar.activation(h_bf[g][:, g0 * PACK : (g0 + SUB) * PACK].rearrange("p (j t) -> p j t", t=PACK),
-                                 hs[:].rearrange("p t j -> p j t"), ACT.Relu)
-
-        h_s = [keep("h_s%d" % h, [P, HALF], U8) for h in range(2)]
-        h_w = [keep("h_w0", [P, HALF], U32)]
-        for u in range(2):
-            cols = slice(u * QUARTER, (u + 1) * QUARTER)
-            nc.vector.quantize_mx(out=h_w[0][:, cols].bitcast(FP8X4), scales=h_s[0][:, cols], in_=h_bf[u][:])
-        x_first = [keep("x_first%d" % h, [P, HALF], F32, tag=("x_first0", "h_bf1")[h]) for h in range(2)]
+        x_first = [keep("x_first%d" % h, [P, HALF], F32) for h in range(2)]
         for h in range(2):
             nc.vector.tensor_copy(x_first[h][:], x0[0][:].indirect(listed(h * HALF, HALF)))
-
-        res0 = keep("res0", [P, PACK, HALF], F32)
-        res1 = [keep("res1%d" % g, [P, PACK, QUARTER], F32) for g in range(2)]
+        h_s = [keep("h_s%d" % h, [P, HALF], U8) for h in range(2)]
+        h_bf = [keep("h_bf%d" % h, [P, HALF * PACK], BF16) for h in range(2)]
+        h_w = []
         y_up = {}
+        res0 = keep("res0", [P, PACK, HALF], F32)
         for h in range(2):
-            if h == 1:
-                h_w.append(keep("h_w1", [P, HALF], U32, tag="x_first0"))
-                nc.vector.quantize_mx(out=h_w[1][:].bitcast(FP8X4), scales=h_s[1][:], in_=h_bf[2][:])
+            for c in range(HALF // SUB):
+                cols = slice(c * SUB, (c + 1) * SUB)
+                hs = psum.tile([P, PACK, SUB], F32, name="hs%d%d" % (h, c), tag="bank%d" % (PACK * h + c))
+                for t in range(PACK):
+                    rows = slice(t * P, (t + 1) * P)
+                    nc.tensor.matmul_mx(out=hs[:, t, :], lhsT=dn_w[:, rows].bitcast(FP8X4), lhsT_scale=dn_s[:, rows],
+                                        rhs=v_w[h][:, cols].bitcast(FP8X4), rhs_scale=v_s_all[:, h * HALF + c * SUB : h * HALF + (c + 1) * SUB], start=True, stop=True)
+                nc.scalar.activation(h_bf[h][:, c * SUB * PACK : (c + 1) * SUB * PACK].rearrange("p (j t) -> p j t", t=PACK),
+                                     hs[:].rearrange("p t j -> p j t"), ACT.Relu)
+        for h in range(2):
+            h_w.append(keep("h_w%d" % h, [P, HALF], U32, tag=("bias", "x_first0")[h]))
+            nc.vector.quantize_mx(out=h_w[h][:].bitcast(FP8X4), scales=h_s[h][:], in_=h_bf[h][:])
             for t in range(PACK):
                 y = psum.tile([P, HALF], F32, name="y%d%d" % (h, t), tag="bank%d" % (PACK * h + t))
                 for u, (mw, ms) in enumerate(((v_w[h], v_s[h]), (h_w[h][:], h_s[h][:]))):
@@ -133,62 +126,45 @@ def tile_list_xcross_reluP_kernel(tc, tab_words, tab_scales, wb_words, wb_scales
                 if (h, t) == (0, 0):
                     nc.vector.scalar_tensor_tensor(res0[:, t, :], y[:], bias1[:, t : t + 1], x_first[0][:], ALU.add, ALU.mult)
                 elif t == 0:
-                    for g in range(2):
-                        cols = slice(g * QUARTER, (g + 1) * QUARTER)
-                        nc.vector.scalar_tensor_tensor(res1[g][:, 0, :], y[:, cols], bias1[:, :1], x_first[1][:, cols], ALU.add, ALU.mult)
+                    y_first = y
                 else:
-                    if t == 3:
-                        y_up[h, t] = res1[h][:, 1:3, :].rearrange("p a j -> p (a j)")
-                    else:
-                        y_up[h, t] = keep("y_up%d%d" % (h, t), [P, HALF], F32)[:]
-                    nc.scalar.activation(y_up[h, t], y[:], ACT.Identity, bias=bias1[:, t : t + 1])
+                    y_up[h, t] = keep("y_up%d%d" % (h, t), [P, HALF], F32)
+                    nc.scalar.activation(y_up[h, t][:], y[:], ACT.Identity, bias=bias1[:, t : t + 1])
 
         res_w = keep("res_w", [P, J], U32)
         res_s = keep("res_s", [P, J], U8)
         out_rows = out_0.rearrange("(p t) j -> p t j", t=PACK)
         out_words = out_1[0].rearrange("p j i -> p (j i)").bitcast(I32)
 
-        def cross(dst, t, j0, count):
-            h, c0 = divmod(j0, HALF)
-            nc.vector.tensor_tensor(dst, x0[t][:].indirect(listed(j0, count)), y_up[h, t][:, c0 : c0 + count], ALU.mult)
-
         def round_out(engine_copy, dst, src):
             engine_copy(dst.rearrange("p (c i t) -> p c t i", i=4, t=PACK), src.rearrange("p t (c i) -> p c t i", i=4))
 
-        def quantise_out(g, j0, count):
-            cols = slice(j0, j0 + count)
-            nc.vector.quantize_mx(out=res_w[:, cols].bitcast(FP8X4), scales=res_s[:, cols], in_=rounded[g][:])
+        def quantise_out(g, src):
+            rounded = keep("rounded%d" % g, [P, QUARTER * PACK], BF16)
+            if g < 3:
+                round_out(nc.scalar.copy, rounded[:], src)
+            else:
+                round_out(nc.vector.tensor_copy, rounded[:], src)
+            cols = slice(g * QUARTER, (g + 1) * QUARTER)
+            nc.vector.quantize_mx(out=res_w[:, cols].bitcast(FP8X4), scales=res_s[:, cols], in_=rounded[:])
 
-        rounded = [keep("rounded%d" % g, [P, width * PACK], BF16) for g, width in enumerate((HALF, QUARTER, QUARTER))]
         nc.sync.dma_start(out_rows[:, 0, :HALF], res0[:, 0, :])
-        for g in range(2):
-            j0 = HALF + g * QUARTER
-            nc.sync.dma_start(out_rows[:, 0, j0 : j0 + QUARTER], res1[g][:, 0, :])
-        for t in (1, 2):
-            cross(res0[:, t, :], t, 0, HALF)
+        for t in range(1, PACK):
+            nc.vector.tensor_tensor(res0[:, t, :], x0[t][:].indirect(listed(0, HALF)), y_up[0, t][:], ALU.mult)
             nc.sync.dma_start(out_rows[:, t, :HALF], res0[:, t, :])
         for g in range(2):
-            cross(res0[:, 3, g * QUARTER : (g + 1) * QUARTER], 3, g * QUARTER, QUARTER)
-        nc.sync.dma_start(out_rows[:, 3, :HALF], res0[:, 3, :])
-        for g in range(2):
-            round_out(nc.scalar.copy, rounded[0][:, g * QUARTER * PACK : (g + 1) * QUARTER * PACK], res0[:, :, g * QUARTER : (g + 1) * QUARTER])
-        j0 = HALF
-        for t in (1, 2, 3):
-            cross(res1[0][:, t, :], t, j0, QUARTER)
-        nc.sync.dma_start(out_rows[:, 1:, j0 : j0 + QUARTER], res1[0][:, 1:, :])
-        round_out(nc.scalar.copy, rounded[1][:], res1[0][:])
-        j0 = HALF + QUARTER
-        cross(res1[1][:, 1, :], 1, j0, QUARTER)
-        quantise_out(0, 0, HALF)
+            quantise_out(g, res0[:, :, g * QUARTER : (g + 1) * QUARTER])
         nc.sync.dma_start(out_words[:, :HALF], res_w[:, :HALF].bitcast(I32))
-        for t in (3, 2):
-            cross(res1[1][:, t, :], t, j0, QUARTER)
-        nc.sync.dma_start(out_rows[:, 1:, j0 : j0 + QUARTER], res1[1][:, 1:, :])
-        round_out(nc.scalar.copy, rounded[2][:, : SUB * PACK], res1[1][:, :, :SUB])
-        quantise_out(1, HALF, QUARTER)
-        nc.sync.dma_start(out_words[:, HALF:j0], res_w[:, HALF:j0].bitcast(I32))
-        round_out(nc.vector.tensor_copy, rounded[2][:, SUB * PACK :], res1[1][:, :, SUB:])
-        quantise_out(2, j0, QUARTER)
-        nc.sync.dma_start(out_words[:, j0:], res_w[:, j0:].bitcast(I32))
+        for g in range(2):
+            j0 = HALF + g * QUARTER
+            res1 = keep("res1%d" % g, [P, PACK, QUARTER], F32, tag=("res10", "y_up03")[g])
+            nc.vector.scalar_tensor_tensor(res1[:, 0, :], y_first[:, g * QUARTER : (g + 1) * QUARTER], bias1[:, 0:1], x_first[1][:, g * QUARTER : (g + 1) * QUARTER], ALU.add, ALU.mult)
+            for t in range(1, PACK):
+                nc.vector.tensor_tensor(res1[:, t, :], x0[t][:].indirect(listed(j0, QUARTER)), y_up[1, t][:, g * QUARTER : (g + 1) * QUARTER], ALU.mult)
+                if t == 2:
+                    nc.sync.dma_start(out_rows[:, :3, j0 : j0 + QUARTER], res1[:, :3, :])
+            nc.sync.dma_start(out_rows[:, 3, j0 : j0 + QUARTER], res1[:, 3, :])
+            quantise_out(2 + g, res1[:])
+            nc.sync.dma_start(out_words[:, j0 : j0 + QUARTER], res_w[:, j0 : j0 + QUARTER].bitcast(I32))
         for q in range(4):
             nc.scalar.dma_start(out_2[0, 4 * q : 4 * q + 4, :].bitcast(I32), res_s[32 * q : 32 * q + 4, :].bitcast(I32))

@@ -35,15 +35,14 @@ def tile_list_xcross_reluP_kernel(tc, tab_words, tab_scales, wb_words, wb_scales
         def listed(j0, count):
             return offsets[:, j0 // 16 : (j0 + count) // 16]
 
-        rows16 = slice(16, 32)
+        rows16 = slice(P - 16, P)
         offsets = held.tile([P, J // 16], U16, name="offsets")
         ws_raw = keep("ws_raw", [P, 2 * N], U8)
         tab_s = keep("tab_s", [P, T], U8)
         v_s_all = keep("v_s", [P, J], U8)
-        for dead in (slice(0, 16), slice(32, 64), slice(64, P)):
-            nc.vector.memset(tab_s[dead, :].bitcast(I32), 0)
-            nc.gpsimd.memset(ws_raw[dead, :].bitcast(I32), 0)
-        nc.gpsimd.memset(v_s_all[:].bitcast(I32), 0)
+        nc.vector.memset(tab_s[: P - 16, :].bitcast(I32), 0)
+        nc.vector.memset(ws_raw[: P - 16, :].bitcast(I32), 0)
+        nc.vector.memset(v_s_all[:].bitcast(I32), 0)
         nc.sync.dma_start(offsets[:], offs)
         nc.sync.dma_start(tab_s[rows16, :].bitcast(I32), tab_scales[0].bitcast(I32))
         for u, scales in enumerate((wb_scales, upw_scales)):
@@ -64,29 +63,29 @@ def tile_list_xcross_reluP_kernel(tc, tab_words, tab_scales, wb_words, wb_scales
 
         def to_quadrants(plane, rows):
             for q in range(4):
-                nc.sync.dma_start(plane[32 * q : 32 * q + 4, :].bitcast(I32), rows[16 + 4 * q : 20 + 4 * q, :].bitcast(I32))
+                nc.sync.dma_start(plane[32 * q : 32 * q + 4, :].bitcast(I32), rows[P - 16 + 4 * q : P - 12 + 4 * q, :].bitcast(I32))
 
         v_rows = keep("v_rows", [P, J], U8)
         nc.vector.tensor_copy(v_rows[:], tab_s[:].indirect(offsets[:]))
         to_quadrants(v_s_all, v_rows)
         v_s = [v_s_all[:, :HALF], v_s_all[:, HALF:]]
-        w_s = keep("w_s", [P, 2 * N], U8)
-        nc.vector.tensor_copy(w_s[:].rearrange("p (u t m) -> p u t m", u=2, t=PACK), ws_raw[:].rearrange("p (u m t) -> p u t m", u=2, t=PACK))
-        load_x0(0, "ws_raw")
+        load_x0(0, "tab_s")
         bias = keep("bias", [P, PACK], F32)
         nc.sync.dma_start(bias[:], b.rearrange("(p t) -> p t", t=PACK))
+        w_s = keep("w_s", [P, 2 * N], U8)
+        nc.vector.tensor_copy(w_s[:].rearrange("p (u t m) -> p u t m", u=2, t=PACK), ws_raw[:].rearrange("p (u m t) -> p u t m", u=2, t=PACK))
         to_quadrants(w_s, w_s)
+        load_x0(1, "ws_raw")
         w_w = [keep("w_w%d" % u, [P, 2 * N], U8) for u in range(2)]
         for u in range(2):
             nc.vector.tensor_copy(w_w[u][:].bitcast(U16).rearrange("p (t m) -> p t m", t=PACK), w_raw[u][:].bitcast(U16).rearrange("p (m t) -> p t m", t=PACK))
-        load_x0(1, "w_raw1")
+        load_x0(2, "w_raw1")
         dn_bf = keep("dn_bf", [P, R * PACK], BF16)
-        dn_dealt = dn_bf[:].rearrange("p (t m i) -> p m i t", t=PACK, i=PACK)
-        dn_rows = dn_raw[:].rearrange("p i (m t) -> p m i t", t=PACK)
-        nc.scalar.copy(dn_dealt[:, :88], dn_rows[:, :88])
-        nc.vector.tensor_copy(dn_dealt[:, 88:], dn_rows[:, 88:])
-        load_x0(2, "dn_raw")
-        load_x0(3, "v_rows")
+        dn_dealt = dn_bf[:].rearrange("p (t c e i) -> p c i e t", t=PACK, e=2, i=PACK)
+        dn_rows = dn_raw[:].rearrange("p i (c e t) -> p c i e t", e=2, t=PACK)
+        nc.scalar.copy(dn_dealt[:, :32], dn_rows[:, :32])
+        nc.vector.tensor_copy(dn_dealt[:, 32:], dn_rows[:, 32:])
+        load_x0(3, "dn_raw")
         bias1 = keep("bias1", [P, PACK], F32)
         nc.gpsimd.tensor_scalar(bias1[:], bias[:], 1.0, 1.0, ALU.mult, ALU.add)
         dn_w = keep("dn_w", [P, R], U32)

@@ -93,12 +93,17 @@ def tile_list_xcross_reluP_kernel(tc, tab_words, tab_scales, wb_words, wb_scales
         nc.vector.quantize_mx(out=dn_w[:].bitcast(FP8X4), scales=dn_s[:], in_=dn_bf[:])
         v_w_all = keep("v_w", [P, J], U32, tag="dn_bf")
         v_w = [v_w_all[:, :HALF], v_w_all[:, HALF:]]
-        for h, c0, width in ((0, 0, 256), (0, 256, 256), (1, 0, 512)):
-            nc.vector.tensor_copy(v_w[h][:, c0 : c0 + width], tab_w[:].indirect(listed(h * HALF + c0, width)))
+        for j0, count in ((0, QUARTER), (QUARTER, QUARTER), (HALF, HALF)):
+            nc.vector.tensor_copy(v_w_all[:, j0 : j0 + count], tab_w[:].indirect(listed(j0, count)))
 
-        x_first = [keep("x_first%d" % h, [P, HALF], F32) for h in range(2)]
-        for h in range(2):
-            nc.vector.tensor_copy(x_first[h][:], x0[0][:].indirect(listed(h * HALF, HALF)))
+        x_first = []
+
+        def gather_first(j0, count, tag):
+            x_first.append(keep("x_first%d" % len(x_first), [P, count], F32, tag=tag))
+            nc.vector.tensor_copy(x_first[-1][:], x0[0][:].indirect(listed(j0, count)))
+
+        gather_first(0, HALF, None)
+        gather_first(HALF, QUARTER, None)
         h_s = [keep("h_s%d" % h, [P, HALF], U8) for h in range(2)]
         h_bf = [keep("h_bf%d" % h, [P, HALF * PACK], BF16) for h in range(2)]
         h_w = []
@@ -117,6 +122,8 @@ def tile_list_xcross_reluP_kernel(tc, tab_words, tab_scales, wb_words, wb_scales
         for h in range(2):
             h_w.append(keep("h_w%d" % h, [P, HALF], U32, tag=("bias", "x_first0")[h]))
             nc.vector.quantize_mx(out=h_w[h][:].bitcast(FP8X4), scales=h_s[h][:], in_=h_bf[h][:])
+            if h == 0:
+                gather_first(HALF + QUARTER, QUARTER, "h_bf0")
             for t in range(PACK):
                 y = psum.tile([P, HALF], F32, name="y%d%d" % (h, t), tag="bank%d" % (PACK * h + t))
                 for u, (mw, ms) in enumerate(((v_w[h], v_s[h]), (h_w[h][:], h_s[h][:]))):
@@ -135,35 +142,43 @@ def tile_list_xcross_reluP_kernel(tc, tab_words, tab_scales, wb_words, wb_scales
         out_rows = out_0.rearrange("(p t) j -> p t j", t=PACK)
         out_words = out_1[0].rearrange("p j i -> p (j i)").bitcast(I32)
 
-        def round_out(engine_copy, dst, src):
-            engine_copy(dst.rearrange("p (c i t) -> p c t i", i=4, t=PACK), src.rearrange("p t (c i) -> p c t i", i=4))
+        rounded = [keep("rounded%d" % h, [P, HALF * PACK], BF16) for h in range(2)]
 
-        def quantise_out(g, src):
-            rounded = keep("rounded%d" % g, [P, QUARTER * PACK], BF16)
-            if g < 3:
-                round_out(nc.scalar.copy, rounded[:], src)
-            else:
-                round_out(nc.vector.tensor_copy, rounded[:], src)
-            cols = slice(g * QUARTER, (g + 1) * QUARTER)
-            nc.vector.quantize_mx(out=res_w[:, cols].bitcast(FP8X4), scales=res_s[:, cols], in_=rounded[:])
+        def cross(res, h, t, c0, count):
+            nc.vector.tensor_tensor(res[:, t, c0 : c0 + count], x0[t][:].indirect(listed(h * HALF + c0, count)), y_up[h, t][:, c0 : c0 + count], ALU.mult)
 
-        nc.sync.dma_start(out_rows[:, 0, :HALF], res0[:, 0, :])
+        def store(res, h, t):
+            nc.sync.dma_start(out_rows[:, t, h * HALF : (h + 1) * HALF], res[:, t, :])
+
+        def round_out(engine_copy, res, h, c0, count):
+            engine_copy(rounded[h][:, c0 * PACK : (c0 + count) * PACK].rearrange("p (c i t) -> p c t i", i=4, t=PACK),
+                        res[:, :, c0 : c0 + count].rearrange("p t (c i) -> p c t i", i=4))
+
+        def quantise_out(h, c0, count):
+            cols = slice(h * HALF + c0, h * HALF + c0 + count)
+            nc.vector.quantize_mx(out=res_w[:, cols].bitcast(FP8X4), scales=res_s[:, cols], in_=rounded[h][:, c0 * PACK : (c0 + count) * PACK])
+            nc.sync.dma_start(out_words[:, cols], res_w[:, cols].bitcast(I32))
+
+        store(res0, 0, 0)
         for t in range(1, PACK):
-            nc.vector.tensor_tensor(res0[:, t, :], x0[t][:].indirect(listed(0, HALF)), y_up[0, t][:], ALU.mult)
-            nc.sync.dma_start(out_rows[:, t, :HALF], res0[:, t, :])
+            cross(res0, 0, t, 0, HALF)
+            store(res0, 0, t)
+        round_out(nc.scalar.copy, res0, 0, 0, HALF)
+        res1 = keep("res1", [P, PACK, HALF], F32, tag="y_up03")
         for g in range(2):
-            quantise_out(g, res0[:, :, g * QUARTER : (g + 1) * QUARTER])
-        nc.sync.dma_start(out_words[:, :HALF], res_w[:, :HALF].bitcast(I32))
-        for g in range(2):
-            j0 = HALF + g * QUARTER
-            res1 = keep("res1%d" % g, [P, PACK, QUARTER], F32, tag=("res10", "y_up03")[g])
-            nc.vector.scalar_tensor_tensor(res1[:, 0, :], y_first[:, g * QUARTER : (g + 1) * QUARTER], bias1[:, 0:1], x_first[1][:, g * QUARTER : (g + 1) * QUARTER], ALU.add, ALU.mult)
-            for t in range(1, PACK):
-                nc.vector.tensor_tensor(res1[:, t, :], x0[t][:].indirect(listed(j0, QUARTER)), y_up[1, t][:, g * QUARTER : (g + 1) * QUARTER], ALU.mult)
-                if t == 2:
-                    nc.sync.dma_start(out_rows[:, :3, j0 : j0 + QUARTER], res1[:, :3, :])
-            nc.sync.dma_start(out_rows[:, 3, j0 : j0 + QUARTER], res1[:, 3, :])
-            quantise_out(2 + g, res1[:])
-            nc.sync.dma_start(out_words[:, j0 : j0 + QUARTER], res_w[:, j0 : j0 + QUARTER].bitcast(I32))
+            cols = slice(g * QUARTER, (g + 1) * QUARTER)
+            nc.vector.scalar_tensor_tensor(res1[:, 0, cols], y_first[:, cols], bias1[:, 0:1], x_first[1 + g][:], ALU.add, ALU.mult)
+        store(res1, 1, 0)
+        for t in (1, 2):
+            cross(res1, 1, t, 0, HALF)
+            store(res1, 1, t)
+        quantise_out(0, 0, HALF)
+        cross(res1, 1, 3, 0, QUARTER)
+        round_out(nc.scalar.copy, res1, 1, 0, QUARTER)
+        cross(res1, 1, 3, QUARTER, QUARTER)
+        store(res1, 1, 3)
+        round_out(nc.vector.tensor_copy, res1, 1, QUARTER, QUARTER)
+        quantise_out(1, 0, QUARTER)
+        quantise_out(1, QUARTER, QUARTER)
         for q in range(4):
             nc.scalar.dma_start(out_2[0, 4 * q : 4 * q + 4, :].bitcast(I32), res_s[32 * q : 32 * q + 4, :].bitcast(I32))

@@ -49,9 +49,6 @@ def tile_list_xcross_reluP_kernel(tc, tab_words, tab_scales, wb_words, wb_scales
             nc.sync.dma_start(ws_raw[rows16, u * N : (u + 1) * N].bitcast(I32), scales[0].bitcast(I32))
         dn_raw = keep("dn_raw", [P, PACK, R], F32)
         nc.sync.dma_start(dn_raw[:], dn.rearrange("(p i) r -> p i r", i=PACK))
-        w_raw = [keep("w_raw%d" % u, [P, 2 * N], U8) for u in range(2)]
-        for u, words in enumerate((wb_words, upw_words)):
-            nc.sync.dma_start(w_raw[u][:].bitcast(I32), words[0].bitcast(I32))
         tab_w = keep("tab_w", [P, T], U32)
         nc.sync.dma_start(tab_w[:].bitcast(I32), tab_words[0].rearrange("p t i -> p (t i)").bitcast(I32))
         x0_rows = x0T.rearrange("(p t) c -> p t c", t=PACK)
@@ -69,23 +66,21 @@ def tile_list_xcross_reluP_kernel(tc, tab_words, tab_scales, wb_words, wb_scales
         nc.vector.tensor_copy(v_rows[:], tab_s[:].indirect(offsets[:]))
         to_quadrants(v_s_all, v_rows)
         v_s = [v_s_all[:, :HALF], v_s_all[:, HALF:]]
-        load_x0(0, "tab_s")
-        bias = keep("bias", [P, PACK], F32)
-        nc.sync.dma_start(bias[:], b.rearrange("(p t) -> p t", t=PACK))
+        w_raw = keep("w_raw", [P, 2, 2 * N], U8, tag="tab_s")
+        for u, words in enumerate((wb_words, upw_words)):
+            nc.sync.dma_start(w_raw[:, u, :].bitcast(I32), words[0].bitcast(I32))
         w_s = keep("w_s", [P, 2 * N], U8)
         nc.vector.tensor_copy(w_s[:].rearrange("p (u t m) -> p u t m", u=2, t=PACK), ws_raw[:].rearrange("p (u m t) -> p u t m", u=2, t=PACK))
+        load_x0(0, "ws_raw")
         to_quadrants(w_s, w_s)
-        load_x0(1, "ws_raw")
-        w_w = [keep("w_w%d" % u, [P, 2 * N], U8) for u in range(2)]
-        for u in range(2):
-            nc.vector.tensor_copy(w_w[u][:].bitcast(U16).rearrange("p (t m) -> p t m", t=PACK), w_raw[u][:].bitcast(U16).rearrange("p (m t) -> p t m", t=PACK))
-        load_x0(2, "w_raw1")
+        bias = keep("bias", [P, PACK], F32, tag="v_rows")
+        nc.sync.dma_start(bias[:], b.rearrange("(p t) -> p t", t=PACK))
         dn_bf = keep("dn_bf", [P, R * PACK], BF16)
         dn_dealt = dn_bf[:].rearrange("p (t c e i) -> p c i e t", t=PACK, e=2, i=PACK)
         dn_rows = dn_raw[:].rearrange("p i (c e t) -> p c i e t", e=2, t=PACK)
         nc.scalar.copy(dn_dealt[:, :32], dn_rows[:, :32])
         nc.vector.tensor_copy(dn_dealt[:, 32:], dn_rows[:, 32:])
-        load_x0(3, "dn_raw")
+        load_x0(1, "dn_raw")
         bias1 = keep("bias1", [P, PACK], F32)
         nc.gpsimd.tensor_scalar(bias1[:], bias[:], 1.0, 1.0, ALU.mult, ALU.add)
         dn_w = keep("dn_w", [P, R], U32)
@@ -95,89 +90,111 @@ def tile_list_xcross_reluP_kernel(tc, tab_words, tab_scales, wb_words, wb_scales
         v_w = [v_w_all[:, :HALF], v_w_all[:, HALF:]]
         for j0, count in ((0, QUARTER), (QUARTER, QUARTER), (HALF, HALF)):
             nc.vector.tensor_copy(v_w_all[:, j0 : j0 + count], tab_w[:].indirect(listed(j0, count)))
+        load_x0(2, "tab_w")
+        w_all = keep("w_all", [P, 2, 2 * N], U8)
+        nc.vector.tensor_copy(w_all[:].bitcast(U16).rearrange("p u (t m) -> p u t m", t=PACK), w_raw[:].bitcast(U16).rearrange("p u (m t) -> p u t m", t=PACK))
+        w_w = [w_all[:, u, :] for u in range(2)]
+        load_x0(3, "tab_s")
 
-        x_first = []
-
-        def gather_first(j0, count, tag):
-            x_first.append(keep("x_first%d" % len(x_first), [P, count], F32, tag=tag))
-            nc.vector.tensor_copy(x_first[-1][:], x0[0][:].indirect(listed(j0, count)))
-
-        gather_first(0, HALF, None)
-        gather_first(HALF, QUARTER, None)
         h_s = [keep("h_s%d" % h, [P, HALF], U8) for h in range(2)]
         h_bf = [keep("h_bf%d" % h, [P, HALF * PACK], BF16) for h in range(2)]
-        h_w = []
-        y_up = {}
         res0 = keep("res0", [P, PACK, HALF], F32)
-        for h in range(2):
-            for c in range(HALF // SUB):
-                cols = slice(c * SUB, (c + 1) * SUB)
-                hs = psum.tile([P, PACK, SUB], F32, name="hs%d%d" % (h, c), tag="bank%d" % (PACK * h + c))
-                for t in range(PACK):
-                    rows = slice(t * P, (t + 1) * P)
-                    nc.tensor.matmul_mx(out=hs[:, t, :], lhsT=dn_w[:, rows].bitcast(FP8X4), lhsT_scale=dn_s[:, rows],
-                                        rhs=v_w[h][:, cols].bitcast(FP8X4), rhs_scale=v_s_all[:, h * HALF + c * SUB : h * HALF + (c + 1) * SUB], start=True, stop=True)
-                nc.scalar.activation(h_bf[h][:, c * SUB * PACK : (c + 1) * SUB * PACK].rearrange("p (j t) -> p j t", t=PACK),
-                                     hs[:].rearrange("p t j -> p j t"), ACT.Relu)
-        for h in range(2):
-            h_w.append(keep("h_w%d" % h, [P, HALF], U32, tag=("bias", "x_first0")[h]))
-            nc.vector.quantize_mx(out=h_w[h][:].bitcast(FP8X4), scales=h_s[h][:], in_=h_bf[h][:])
-            if h == 0:
-                gather_first(HALF + QUARTER, QUARTER, "h_bf0")
+
+        def first(c, bank):
+            cols = slice(c * SUB, (c + 1) * SUB)
+            hs = psum.tile([P, PACK, SUB], F32, name="hs%d" % c, tag="bank%d" % bank)
             for t in range(PACK):
-                y = psum.tile([P, HALF], F32, name="y%d%d" % (h, t), tag="bank%d" % (PACK * h + t))
-                for u, (mw, ms) in enumerate(((v_w[h], v_s[h]), (h_w[h][:], h_s[h][:]))):
-                    nc.tensor.matmul_mx(out=y[:], lhsT=w_w[u][:, 2 * t * P : 2 * (t + 1) * P].bitcast(FP4X4), lhsT_scale=w_s[:, u * N + t * P : u * N + (t + 1) * P],
-                                        rhs=mw.bitcast(FP8X4), rhs_scale=ms, start=(u == 0), stop=(u == 1))
-                if (h, t) == (0, 0):
-                    nc.vector.scalar_tensor_tensor(res0[:, t, :], y[:], bias1[:, t : t + 1], x_first[0][:], ALU.add, ALU.mult)
-                elif t == 0:
-                    y_first = y
-                else:
-                    y_up[h, t] = keep("y_up%d%d" % (h, t), [P, HALF], F32)
-                    nc.scalar.activation(y_up[h, t][:], y[:], ACT.Identity, bias=bias1[:, t : t + 1])
+                rows = slice(t * P, (t + 1) * P)
+                nc.tensor.matmul_mx(out=hs[:, t, :], lhsT=dn_w[:, rows].bitcast(FP8X4), lhsT_scale=dn_s[:, rows],
+                                    rhs=v_w_all[:, cols].bitcast(FP8X4), rhs_scale=v_s_all[:, cols], start=True, stop=True)
+            width = SUB * PACK
+            dst = h_bf[c // 4][:, (c % 4) * width : (c % 4 + 1) * width]
+            nc.scalar.activation(dst.rearrange("p (j t) -> p j t", t=PACK), hs[:].rearrange("p t j -> p j t"), ACT.Relu)
+
+        def second(h, t, bank, h_w):
+            y = psum.tile([P, HALF], F32, name="y%d%d" % (h, t), tag="bank%d" % bank)
+            moving = ((v_w[h], v_s[h]), (h_w[:], h_s[h][:]))
+            for i, u in enumerate(((0, 1), (1, 0))[h]):
+                mw, ms = moving[u]
+                nc.tensor.matmul_mx(out=y[:], lhsT=w_w[u][:, 2 * t * P : 2 * (t + 1) * P].bitcast(FP4X4), lhsT_scale=w_s[:, u * N + t * P : u * N + (t + 1) * P],
+                                    rhs=mw.bitcast(FP8X4), rhs_scale=ms, start=(i == 0), stop=(i == 1))
+            return y
+
+        def lift(dst, y, t, c0, count):
+            nc.scalar.activation(dst, y[:, c0 : c0 + count], ACT.Identity, bias=bias1[:, t : t + 1])
 
         res_w = keep("res_w", [P, J], U32)
         res_s = keep("res_s", [P, J], U8)
         out_rows = out_0.rearrange("(p t) j -> p t j", t=PACK)
         out_words = out_1[0].rearrange("p j i -> p (j i)").bitcast(I32)
+        rounded = {}
 
-        rounded = [keep("rounded%d" % h, [P, HALF * PACK], BF16) for h in range(2)]
-
-        def cross(res, h, t, c0, count):
-            nc.vector.tensor_tensor(res[:, t, c0 : c0 + count], x0[t][:].indirect(listed(h * HALF + c0, count)), y_up[h, t][:, c0 : c0 + count], ALU.mult)
+        def cross(res, h, t, c0, count, lifted):
+            nc.vector.tensor_tensor(res[:, t, c0 : c0 + count], x0[t][:].indirect(listed(h * HALF + c0, count)), lifted, ALU.mult)
 
         def store(res, h, t):
             nc.sync.dma_start(out_rows[:, t, h * HALF : (h + 1) * HALF], res[:, t, :])
 
-        def round_out(engine_copy, res, h, c0, count):
-            engine_copy(rounded[h][:, c0 * PACK : (c0 + count) * PACK].rearrange("p (c i t) -> p c t i", i=4, t=PACK),
+        def round_out(engine_copy, res, h, c0, count, tag=None):
+            rounded[h, c0] = keep("rounded%d_%d" % (h, c0), [P, count * PACK], BF16, tag=tag)
+            engine_copy(rounded[h, c0][:].rearrange("p (c i t) -> p c t i", i=4, t=PACK),
                         res[:, :, c0 : c0 + count].rearrange("p t (c i) -> p c t i", i=4))
 
         def quantise_out(h, c0, count):
             cols = slice(h * HALF + c0, h * HALF + c0 + count)
-            nc.vector.quantize_mx(out=res_w[:, cols].bitcast(FP8X4), scales=res_s[:, cols], in_=rounded[h][:, c0 * PACK : (c0 + count) * PACK])
+            nc.vector.quantize_mx(out=res_w[:, cols].bitcast(FP8X4), scales=res_s[:, cols], in_=rounded[h, c0][:])
             nc.sync.dma_start(out_words[:, cols], res_w[:, cols].bitcast(I32))
 
-        store(res0, 0, 0)
-        for t in range(1, PACK):
-            cross(res0, 0, t, 0, HALF)
-            store(res0, 0, t)
-        round_out(nc.scalar.copy, res0, 0, 0, HALF)
-        res1 = keep("res1", [P, PACK, HALF], F32, tag="y_up03")
+        x_first = [keep("x_first%d" % g, [P, QUARTER], F32) for g in range(2)]
+        for g in range(2):
+            nc.vector.tensor_copy(x_first[g][:], x0[0][:].indirect(listed(g * QUARTER, QUARTER)))
+        for c in range(8):
+            first(c, c)
+        h_w0 = keep("h_w0", [P, HALF], U32, tag="v_rows")
+        nc.vector.quantize_mx(out=h_w0[:].bitcast(FP8X4), scales=h_s[0][:], in_=h_bf[0][:])
+        x_third = keep("x_third", [P, QUARTER], F32, tag="h_bf0")
+        nc.vector.tensor_copy(x_third[:], x0[0][:].indirect(listed(HALF, QUARTER)))
+        y0 = [second(0, t, t, h_w0) for t in range(PACK)]
         for g in range(2):
             cols = slice(g * QUARTER, (g + 1) * QUARTER)
-            nc.vector.scalar_tensor_tensor(res1[:, 0, cols], y_first[:, cols], bias1[:, 0:1], x_first[1 + g][:], ALU.add, ALU.mult)
+            nc.vector.scalar_tensor_tensor(res0[:, 0, cols], y0[0][:, cols], bias1[:, 0:1], x_first[g][:], ALU.add, ALU.mult)
+        store(res0, 0, 0)
+        up0 = {}
+        for t in (1, 2):
+            up0[t] = keep("up0%d" % t, [P, HALF], F32)
+            lift(up0[t][:], y0[t], t, 0, HALF)
+        up03 = [keep("up03%d" % g, [P, QUARTER], F32) for g in range(2)]
+        for g in range(2):
+            lift(up03[g][:], y0[3], 3, g * QUARTER, QUARTER)
+        h_w1 = keep("h_w1", [P, HALF], U32, tag="x_first0")
+        nc.vector.quantize_mx(out=h_w1[:].bitcast(FP8X4), scales=h_s[1][:], in_=h_bf[1][:])
+        y1 = [second(1, t, PACK + t, h_w1) for t in range(PACK)]
+        up10 = keep("up10", [P, QUARTER], F32)
+        lift(up10[:], y1[0], 0, QUARTER, QUARTER)
+        up1 = {}
+        for t in range(1, PACK):
+            up1[t] = keep("up1%d" % t, [P, HALF], F32)
+            lift(up1[t][:], y1[t], t, 0, HALF)
+        for t in (1, 2):
+            cross(res0, 0, t, 0, HALF, up0[t][:])
+            store(res0, 0, t)
+        for g in range(2):
+            cross(res0, 0, 3, g * QUARTER, QUARTER, up03[g][:])
+        store(res0, 0, 3)
+        round_out(nc.scalar.copy, res0, 0, 0, HALF)
+        res1 = keep("res1", [P, PACK, HALF], F32, tag="up030")
+        nc.vector.scalar_tensor_tensor(res1[:, 0, :QUARTER], y1[0][:, :QUARTER], bias1[:, 0:1], x_third[:], ALU.add, ALU.mult)
+        cross(res1, 1, 0, QUARTER, QUARTER, up10[:])
         store(res1, 1, 0)
         for t in (1, 2):
-            cross(res1, 1, t, 0, HALF)
+            cross(res1, 1, t, 0, HALF, up1[t][:])
             store(res1, 1, t)
-        quantise_out(0, 0, HALF)
-        cross(res1, 1, 3, 0, QUARTER)
+        cross(res1, 1, 3, 0, QUARTER, up1[3][:, :QUARTER])
         round_out(nc.scalar.copy, res1, 1, 0, QUARTER)
-        cross(res1, 1, 3, QUARTER, QUARTER)
+        cross(res1, 1, 3, QUARTER, QUARTER, up1[3][:, QUARTER:])
         store(res1, 1, 3)
-        round_out(nc.vector.tensor_copy, res1, 1, QUARTER, QUARTER)
+        quantise_out(0, 0, HALF)
+        round_out(nc.vector.tensor_copy, res1, 1, QUARTER, QUARTER, tag="res0")
         quantise_out(1, 0, QUARTER)
         quantise_out(1, QUARTER, QUARTER)
         for q in range(4):

@@ -97,7 +97,8 @@ def tile_list_xcross_reluP_kernel(tc, tab_words, tab_scales, wb_words, wb_scales
         load_x0(3, "tab_s")
 
         h_s = [keep("h_s%d" % h, [P, HALF], U8) for h in range(2)]
-        h_bf = [keep("h_bf%d" % h, [P, HALF * PACK], BF16) for h in range(2)]
+        h_bf0 = [keep("h_bf0%d" % g, [P, QUARTER * PACK], BF16) for g in range(2)]
+        h_bf1 = keep("h_bf1", [P, HALF * PACK], BF16)
         res0 = keep("res0", [P, PACK, HALF], F32)
 
         def first(c, bank):
@@ -108,7 +109,7 @@ def tile_list_xcross_reluP_kernel(tc, tab_words, tab_scales, wb_words, wb_scales
                 nc.tensor.matmul_mx(out=hs[:, t, :], lhsT=dn_w[:, rows].bitcast(FP8X4), lhsT_scale=dn_s[:, rows],
                                     rhs=v_w_all[:, cols].bitcast(FP8X4), rhs_scale=v_s_all[:, cols], start=True, stop=True)
             width = SUB * PACK
-            dst = h_bf[c // 4][:, (c % 4) * width : (c % 4 + 1) * width]
+            dst = h_bf0[c // 2][:, (c % 2) * width : (c % 2 + 1) * width] if c < 4 else h_bf1[:, (c - 4) * width : (c - 3) * width]
             nc.scalar.activation(dst.rearrange("p (j t) -> p j t", t=PACK), hs[:].rearrange("p t j -> p j t"), ACT.Relu)
 
         def second(h, t, bank, h_w):
@@ -151,41 +152,44 @@ def tile_list_xcross_reluP_kernel(tc, tab_words, tab_scales, wb_words, wb_scales
         for c in range(8):
             first(c, c)
         h_w0 = keep("h_w0", [P, HALF], U32, tag="v_rows")
-        nc.vector.quantize_mx(out=h_w0[:].bitcast(FP8X4), scales=h_s[0][:], in_=h_bf[0][:])
-        x_third = keep("x_third", [P, QUARTER], F32, tag="h_bf0")
-        nc.vector.tensor_copy(x_third[:], x0[0][:].indirect(listed(HALF, QUARTER)))
+        for g in range(2):
+            cols = slice(g * QUARTER, (g + 1) * QUARTER)
+            nc.vector.quantize_mx(out=h_w0[:, cols].bitcast(FP8X4), scales=h_s[0][:, cols], in_=h_bf0[g][:])
+        x_third = keep("x_third", [P, HALF], F32, tag="h_bf00")
+        nc.vector.tensor_copy(x_third[:], x0[0][:].indirect(listed(HALF, HALF)))
         y0 = [second(0, t, t, h_w0) for t in range(PACK)]
         for g in range(2):
             cols = slice(g * QUARTER, (g + 1) * QUARTER)
             nc.vector.scalar_tensor_tensor(res0[:, 0, cols], y0[0][:, cols], bias1[:, 0:1], x_first[g][:], ALU.add, ALU.mult)
         store(res0, 0, 0)
-        up0 = {}
-        for t in (1, 2):
-            up0[t] = keep("up0%d" % t, [P, HALF], F32)
-            lift(up0[t][:], y0[t], t, 0, HALF)
-        up03 = [keep("up03%d" % g, [P, QUARTER], F32) for g in range(2)]
+        res1 = keep("res1", [P, PACK, HALF], F32)
+        up01b = keep("up01b", [P, QUARTER], F32)
+        up01 = [res1[:, 0, SUB : SUB + QUARTER], up01b[:]]
         for g in range(2):
-            lift(up03[g][:], y0[3], 3, g * QUARTER, QUARTER)
+            lift(up01[g], y0[1], 1, g * QUARTER, QUARTER)
+        up02 = keep("up02", [P, HALF], F32)
+        lift(up02[:], y0[2], 2, 0, HALF)
         h_w1 = keep("h_w1", [P, HALF], U32, tag="x_first0")
-        nc.vector.quantize_mx(out=h_w1[:].bitcast(FP8X4), scales=h_s[1][:], in_=h_bf[1][:])
+        nc.vector.quantize_mx(out=h_w1[:].bitcast(FP8X4), scales=h_s[1][:], in_=h_bf1[:])
         y1 = [second(1, t, PACK + t, h_w1) for t in range(PACK)]
-        up10 = keep("up10", [P, QUARTER], F32)
-        lift(up10[:], y1[0], 0, QUARTER, QUARTER)
+        for g in range(2):
+            cross(res0, 0, 1, g * QUARTER, QUARTER, up01[g])
+        store(res0, 0, 1)
+        up03 = [res1[:, 1 + g, :QUARTER] for g in range(2)]
+        for g in range(2):
+            lift(up03[g], y0[3], 3, g * QUARTER, QUARTER)
         up1 = {}
         for t in range(1, PACK):
             up1[t] = keep("up1%d" % t, [P, HALF], F32)
             lift(up1[t][:], y1[t], t, 0, HALF)
-        for t in (1, 2):
-            cross(res0, 0, t, 0, HALF, up0[t][:])
-            store(res0, 0, t)
+        cross(res0, 0, 2, 0, HALF, up02[:])
+        store(res0, 0, 2)
+        nc.vector.scalar_tensor_tensor(res1[:, 0, :], y1[0][:], bias1[:, 0:1], x_third[:], ALU.add, ALU.mult)
+        store(res1, 1, 0)
         for g in range(2):
-            cross(res0, 0, 3, g * QUARTER, QUARTER, up03[g][:])
+            cross(res0, 0, 3, g * QUARTER, QUARTER, up03[g])
         store(res0, 0, 3)
         round_out(nc.scalar.copy, res0, 0, 0, HALF)
-        res1 = keep("res1", [P, PACK, HALF], F32, tag="up030")
-        nc.vector.scalar_tensor_tensor(res1[:, 0, :QUARTER], y1[0][:, :QUARTER], bias1[:, 0:1], x_third[:], ALU.add, ALU.mult)
-        cross(res1, 1, 0, QUARTER, QUARTER, up10[:])
-        store(res1, 1, 0)
         for t in (1, 2):
             cross(res1, 1, t, 0, HALF, up1[t][:])
             store(res1, 1, t)

@@ -21,41 +21,48 @@ PACK = 4
 HALF = 512
 QUARTER = 256
 SUB = 128
+SHARE = 128
 
 
 def tile_list_xcross_reluP_kernel(tc, tab_words, tab_scales, wb_words, wb_scales, dn, upw_words, upw_scales, x0T, b, offs, out_0, out_1, out_2):
     nc = tc.nc
     with ExitStack() as ctx:
         held = ctx.enter_context(tc.tile_pool(name="held", bufs=1))
+        lent = ctx.enter_context(tc.tile_pool(name="lent", bufs=1))
         psum = ctx.enter_context(tc.psum_pool(name="psum", bufs=1))
 
         def keep(name, shape, dtype, tag=None):
             return held.tile(shape, dtype, name=name, tag=tag or name, align_bytes=64)
+
+        def lay(name, shape, dtype, offset):
+            return lent.tile(shape, dtype, name=name, tag=name, align_bytes=64, offset=offset)
 
         def listed(j0, count):
             return offsets[:, j0 // 16 : (j0 + count) // 16]
 
         rows16 = slice(P - 16, P)
         offsets = held.tile([P, J // 16], U16, name="offsets")
-        ws_raw = keep("ws_raw", [P, 2 * N], U8)
-        tab_s = keep("tab_s", [P, T], U8)
+        ws_raw = keep("ws_raw", [P, N], U8)
+        w_s = keep("w_s", [P, 2 * N], U8)
+        tab_s = lay("tab_s", [P, T], U8, 8192)
         v_s_all = keep("v_s", [P, J], U8)
         nc.vector.memset(tab_s[: P - 16, :].bitcast(I32), 0)
-        nc.vector.memset(ws_raw[: P - 16, :].bitcast(I32), 0)
+        nc.vector.memset(ws_raw[: P - 32, :].bitcast(I32), 0)
         nc.vector.memset(v_s_all[:].bitcast(I32), 0)
+        nc.vector.memset(w_s[:].bitcast(I32), 0)
         nc.sync.dma_start(offsets[:], offs)
         nc.sync.dma_start(tab_s[rows16, :].bitcast(I32), tab_scales[0].bitcast(I32))
-        for u, scales in enumerate((wb_scales, upw_scales)):
-            nc.sync.dma_start(ws_raw[rows16, u * N : (u + 1) * N].bitcast(I32), scales[0].bitcast(I32))
         dn_raw = keep("dn_raw", [P, PACK, R], F32)
         nc.sync.dma_start(dn_raw[:], dn.rearrange("(p i) r -> p i r", i=PACK))
+        for u, scales in enumerate((wb_scales, upw_scales)):
+            nc.sync.dma_start(ws_raw[P - 32 + u : P : 2, :].bitcast(I32), scales[0].bitcast(I32))
         tab_w = keep("tab_w", [P, T], U32)
         nc.sync.dma_start(tab_w[:].bitcast(I32), tab_words[0].rearrange("p t i -> p (t i)").bitcast(I32))
         x0_rows = x0T.rearrange("(p t) c -> p t c", t=PACK)
         x0 = []
 
-        def load_x0(t, tag):
-            x0.append(keep("x0_%d" % t, [P, T], F32, tag=tag))
+        def load_x0(t, tag, offset=None):
+            x0.append(keep("x0_%d" % t, [P, T], F32, tag=tag) if offset is None else lay("x0_%d" % t, [P, T], F32, offset))
             nc.sync.dma_start(x0[t][:], x0_rows[:, t, :])
 
         def to_quadrants(plane, rows):
@@ -66,21 +73,22 @@ def tile_list_xcross_reluP_kernel(tc, tab_words, tab_scales, wb_words, wb_scales
         nc.vector.tensor_copy(v_rows[:], tab_s[:].indirect(offsets[:]))
         to_quadrants(v_s_all, v_rows)
         v_s = [v_s_all[:, :HALF], v_s_all[:, HALF:]]
-        w_raw = keep("w_raw", [P, 2, 2 * N], U8, tag="tab_s")
+        w_raw = lay("w_raw", [P, 2, 2 * N], U8, 7168)
         for u, words in enumerate((wb_words, upw_words)):
             nc.sync.dma_start(w_raw[:, u, :].bitcast(I32), words[0].bitcast(I32))
-        w_s = keep("w_s", [P, 2 * N], U8)
-        nc.vector.tensor_copy(w_s[:].rearrange("p (u t m) -> p u t m", u=2, t=PACK), ws_raw[:].rearrange("p (u m t) -> p u t m", u=2, t=PACK))
-        load_x0(0, "ws_raw")
-        to_quadrants(w_s, w_s)
-        bias = keep("bias", [P, PACK], F32, tag="v_rows")
-        nc.sync.dma_start(bias[:], b.rearrange("(p t) -> p t", t=PACK))
+        load_x0(0, None, 9216)
         dn_bf = keep("dn_bf", [P, R * PACK], BF16)
         dn_dealt = dn_bf[:].rearrange("p (t c e i) -> p c i e t", t=PACK, e=2, i=PACK)
         dn_rows = dn_raw[:].rearrange("p i (c e t) -> p c i e t", e=2, t=PACK)
         nc.scalar.copy(dn_dealt[:, :32], dn_rows[:, :32])
         nc.vector.tensor_copy(dn_dealt[:, 32:], dn_rows[:, 32:])
-        load_x0(1, "dn_raw")
+        ws_rows = keep("ws_rows", [P, N], U8)
+        nc.vector.tensor_copy(ws_rows[:].rearrange("p (t m) -> p t m", t=PACK), ws_raw[:].rearrange("p (m t) -> p t m", t=PACK))
+        for q in range(4):
+            nc.sync.dma_start(w_s[32 * q : 32 * q + 4, :].bitcast(I32), ws_rows[P - 32 + 8 * q : P - 24 + 8 * q, :].bitcast(I32))
+        bias = keep("bias", [P, PACK], F32, tag="v_rows")
+        nc.sync.dma_start(bias[:], b.rearrange("(p t) -> p t", t=PACK))
+        load_x0(1, "ws_raw")
         bias1 = keep("bias1", [P, PACK], F32)
         nc.gpsimd.tensor_scalar(bias1[:], bias[:], 1.0, 1.0, ALU.mult, ALU.add)
         dn_w = keep("dn_w", [P, R], U32)
@@ -94,7 +102,7 @@ def tile_list_xcross_reluP_kernel(tc, tab_words, tab_scales, wb_words, wb_scales
         w_all = keep("w_all", [P, 2, 2 * N], U8)
         nc.vector.tensor_copy(w_all[:].bitcast(U16).rearrange("p u (t m) -> p u t m", t=PACK), w_raw[:].bitcast(U16).rearrange("p u (m t) -> p u t m", t=PACK))
         w_w = [w_all[:, u, :] for u in range(2)]
-        load_x0(3, "tab_s")
+        load_x0(3, None, 0)
 
         h_s = [keep("h_s%d" % h, [P, HALF], U8) for h in range(2)]
         h_bf0 = [keep("h_bf0%d" % g, [P, QUARTER * PACK], BF16) for g in range(2)]
@@ -175,7 +183,7 @@ def tile_list_xcross_reluP_kernel(tc, tab_words, tab_scales, wb_words, wb_scales
         for g in range(2):
             cross(res0, 0, 1, g * QUARTER, QUARTER, up01[g])
         store(res0, 0, 1)
-        up03 = [res1[:, 1 + g, :QUARTER] for g in range(2)]
+        up03 = [res1[:, 1 + g, SUB : SUB + QUARTER] for g in range(2)]
         for g in range(2):
             lift(up03[g], y0[3], 3, g * QUARTER, QUARTER)
         up1 = {}
@@ -190,16 +198,21 @@ def tile_list_xcross_reluP_kernel(tc, tab_words, tab_scales, wb_words, wb_scales
             cross(res0, 0, 3, g * QUARTER, QUARTER, up03[g])
         store(res0, 0, 3)
         round_out(nc.scalar.copy, res0, 0, 0, HALF)
-        for t in (1, 2):
-            cross(res1, 1, t, 0, HALF, up1[t][:])
-            store(res1, 1, t)
-        cross(res1, 1, 3, 0, QUARTER, up1[3][:, :QUARTER])
+        cross(res1, 1, 1, 0, HALF, up1[1][:])
+        store(res1, 1, 1)
+        for t in (2, 3):
+            cross(res1, 1, t, 0, QUARTER, up1[t][:, :QUARTER])
         round_out(nc.scalar.copy, res1, 1, 0, QUARTER)
-        cross(res1, 1, 3, QUARTER, QUARTER, up1[3][:, QUARTER:])
-        store(res1, 1, 3)
+        for t in (2, 3):
+            cross(res1, 1, t, QUARTER, QUARTER, up1[t][:, QUARTER:])
+            store(res1, 1, t)
         quantise_out(0, 0, HALF)
-        round_out(nc.vector.tensor_copy, res1, 1, QUARTER, QUARTER, tag="res0")
+        last = keep("rounded_last", [P, QUARTER * PACK], BF16, tag="res0")
+        rounded[1, QUARTER] = last
+        for engine_copy, c0, c1 in ((nc.vector.tensor_copy, SHARE, QUARTER), (nc.scalar.copy, 0, SHARE)):
+            engine_copy(last[:, c0 * PACK : c1 * PACK].rearrange("p (c i t) -> p c t i", i=4, t=PACK),
+                        res1[:, :, QUARTER + c0 : QUARTER + c1].rearrange("p t (c i) -> p c t i", i=4))
         quantise_out(1, 0, QUARTER)
         quantise_out(1, QUARTER, QUARTER)
         for q in range(4):
-            nc.scalar.dma_start(out_2[0, 4 * q : 4 * q + 4, :].bitcast(I32), res_s[32 * q : 32 * q + 4, :].bitcast(I32))
+            (nc.scalar, nc.sync)[q % 2].dma_start(out_2[0, 4 * q : 4 * q + 4, :].bitcast(I32), res_s[32 * q : 32 * q + 4, :].bitcast(I32))

@@ -21,21 +21,16 @@ PACK = 4
 HALF = 512
 QUARTER = 256
 SUB = 128
-SHARE = 128
 
 
 def tile_list_xcross_reluP_kernel(tc, tab_words, tab_scales, wb_words, wb_scales, dn, upw_words, upw_scales, x0T, b, offs, out_0, out_1, out_2):
     nc = tc.nc
     with ExitStack() as ctx:
         held = ctx.enter_context(tc.tile_pool(name="held", bufs=1))
-        lent = ctx.enter_context(tc.tile_pool(name="lent", bufs=1))
         psum = ctx.enter_context(tc.psum_pool(name="psum", bufs=1))
 
         def keep(name, shape, dtype, tag=None):
             return held.tile(shape, dtype, name=name, tag=tag or name, align_bytes=64)
-
-        def lay(name, shape, dtype, offset):
-            return lent.tile(shape, dtype, name=name, tag=name, align_bytes=64, offset=offset)
 
         def listed(j0, count):
             return offsets[:, j0 // 16 : (j0 + count) // 16]
@@ -44,7 +39,7 @@ def tile_list_xcross_reluP_kernel(tc, tab_words, tab_scales, wb_words, wb_scales
         offsets = held.tile([P, J // 16], U16, name="offsets")
         ws_raw = keep("ws_raw", [P, N], U8)
         w_s = keep("w_s", [P, 2 * N], U8)
-        tab_s = lay("tab_s", [P, T], U8, 8192)
+        tab_s = keep("tab_s", [P, T], U8)
         v_s_all = keep("v_s", [P, J], U8)
         nc.vector.memset(tab_s[: P - 16, :].bitcast(I32), 0)
         nc.vector.memset(ws_raw[: P - 32, :].bitcast(I32), 0)
@@ -58,11 +53,14 @@ def tile_list_xcross_reluP_kernel(tc, tab_words, tab_scales, wb_words, wb_scales
             nc.sync.dma_start(ws_raw[P - 32 + u : P : 2, :].bitcast(I32), scales[0].bitcast(I32))
         tab_w = keep("tab_w", [P, T], U32)
         nc.sync.dma_start(tab_w[:].bitcast(I32), tab_words[0].rearrange("p t i -> p (t i)").bitcast(I32))
+        w_raw = keep("w_raw", [P, 2, 2 * N], U8)
+        for u, words in enumerate((wb_words, upw_words)):
+            nc.sync.dma_start(w_raw[:, u, :].bitcast(I32), words[0].bitcast(I32))
         x0_rows = x0T.rearrange("(p t) c -> p t c", t=PACK)
         x0 = []
 
-        def load_x0(t, tag, offset=None):
-            x0.append(keep("x0_%d" % t, [P, T], F32, tag=tag) if offset is None else lay("x0_%d" % t, [P, T], F32, offset))
+        def load_x0(t, tag):
+            x0.append(keep("x0_%d" % t, [P, T], F32, tag=tag))
             nc.sync.dma_start(x0[t][:], x0_rows[:, t, :])
 
         def to_quadrants(plane, rows):
@@ -73,10 +71,7 @@ def tile_list_xcross_reluP_kernel(tc, tab_words, tab_scales, wb_words, wb_scales
         nc.vector.tensor_copy(v_rows[:], tab_s[:].indirect(offsets[:]))
         to_quadrants(v_s_all, v_rows)
         v_s = [v_s_all[:, :HALF], v_s_all[:, HALF:]]
-        w_raw = lay("w_raw", [P, 2, 2 * N], U8, 7168)
-        for u, words in enumerate((wb_words, upw_words)):
-            nc.sync.dma_start(w_raw[:, u, :].bitcast(I32), words[0].bitcast(I32))
-        load_x0(0, None, 9216)
+        load_x0(0, "tab_s")
         dn_bf = keep("dn_bf", [P, R * PACK], BF16)
         dn_dealt = dn_bf[:].rearrange("p (t c e i) -> p c i e t", t=PACK, e=2, i=PACK)
         dn_rows = dn_raw[:].rearrange("p i (c e t) -> p c i e t", e=2, t=PACK)
@@ -102,7 +97,7 @@ def tile_list_xcross_reluP_kernel(tc, tab_words, tab_scales, wb_words, wb_scales
         w_all = keep("w_all", [P, 2, 2 * N], U8)
         nc.vector.tensor_copy(w_all[:].bitcast(U16).rearrange("p u (t m) -> p u t m", t=PACK), w_raw[:].bitcast(U16).rearrange("p u (m t) -> p u t m", t=PACK))
         w_w = [w_all[:, u, :] for u in range(2)]
-        load_x0(3, None, 0)
+        load_x0(3, "w_raw")
 
         h_s = [keep("h_s%d" % h, [P, HALF], U8) for h in range(2)]
         h_bf0 = [keep("h_bf0%d" % g, [P, QUARTER * PACK], BF16) for g in range(2)]
@@ -141,8 +136,8 @@ def tile_list_xcross_reluP_kernel(tc, tab_words, tab_scales, wb_words, wb_scales
         def cross(res, h, t, c0, count, lifted):
             nc.vector.tensor_tensor(res[:, t, c0 : c0 + count], x0[t][:].indirect(listed(h * HALF + c0, count)), lifted, ALU.mult)
 
-        def store(res, h, t):
-            nc.sync.dma_start(out_rows[:, t, h * HALF : (h + 1) * HALF], res[:, t, :])
+        def store(res, h, t, c0=0, count=HALF):
+            nc.sync.dma_start(out_rows[:, t, h * HALF + c0 : h * HALF + c0 + count], res[:, t, c0 : c0 + count])
 
         def round_out(engine_copy, res, h, c0, count, tag=None):
             rounded[h, c0] = keep("rounded%d_%d" % (h, c0), [P, count * PACK], BF16, tag=tag)
@@ -197,22 +192,20 @@ def tile_list_xcross_reluP_kernel(tc, tab_words, tab_scales, wb_words, wb_scales
         for g in range(2):
             cross(res0, 0, 3, g * QUARTER, QUARTER, up03[g])
         store(res0, 0, 3)
-        round_out(nc.scalar.copy, res0, 0, 0, HALF)
-        cross(res1, 1, 1, 0, HALF, up1[1][:])
-        store(res1, 1, 1)
-        for t in (2, 3):
-            cross(res1, 1, t, 0, QUARTER, up1[t][:, :QUARTER])
-        round_out(nc.scalar.copy, res1, 1, 0, QUARTER)
-        for t in (2, 3):
-            cross(res1, 1, t, QUARTER, QUARTER, up1[t][:, QUARTER:])
+        for g in range(2):
+            round_out(nc.scalar.copy, res0, 0, g * QUARTER, QUARTER)
+        for t in (1, 2):
+            cross(res1, 1, t, 0, HALF, up1[t][:])
             store(res1, 1, t)
-        quantise_out(0, 0, HALF)
-        last = keep("rounded_last", [P, QUARTER * PACK], BF16, tag="res0")
-        rounded[1, QUARTER] = last
-        for engine_copy, c0, c1 in ((nc.vector.tensor_copy, SHARE, QUARTER), (nc.scalar.copy, 0, SHARE)):
-            engine_copy(last[:, c0 * PACK : c1 * PACK].rearrange("p (c i t) -> p c t i", i=4, t=PACK),
-                        res1[:, :, QUARTER + c0 : QUARTER + c1].rearrange("p t (c i) -> p c t i", i=4))
+        quantise_out(0, 0, QUARTER)
+        cross(res1, 1, 3, 0, QUARTER, up1[3][:, :QUARTER])
+        store(res1, 1, 3, 0, QUARTER)
+        round_out(nc.scalar.copy, res1, 1, 0, QUARTER)
+        cross(res1, 1, 3, QUARTER, QUARTER, up1[3][:, QUARTER:])
+        store(res1, 1, 3, QUARTER, QUARTER)
+        quantise_out(0, QUARTER, QUARTER)
+        round_out(nc.vector.tensor_copy, res1, 1, QUARTER, QUARTER, tag="res0")
         quantise_out(1, 0, QUARTER)
         quantise_out(1, QUARTER, QUARTER)
         for q in range(4):
-            (nc.scalar, nc.sync)[q % 2].dma_start(out_2[0, 4 * q : 4 * q + 4, :].bitcast(I32), res_s[32 * q : 32 * q + 4, :].bitcast(I32))
+            nc.scalar.dma_start(out_2[0, 4 * q : 4 * q + 4, :].bitcast(I32), res_s[32 * q : 32 * q + 4, :].bitcast(I32))

@@ -21,6 +21,7 @@ PACK = 4
 HALF = 512
 QUARTER = 256
 SUB = 128
+DN_S = 22
 
 
 def tile_list_xcross_reluP_kernel(tc, tab_words, tab_scales, wb_words, wb_scales, dn, upw_words, upw_scales, x0T, b, offs, out_0, out_1, out_2):
@@ -75,9 +76,12 @@ def tile_list_xcross_reluP_kernel(tc, tab_words, tab_scales, wb_words, wb_scales
         dn_bf = keep("dn_bf", [P, R * PACK], BF16)
         dn_dealt = dn_bf[:].rearrange("p (t c e i) -> p c i e t", t=PACK, e=2, i=PACK)
         dn_rows = dn_raw[:].rearrange("p i (c e t) -> p c i e t", e=2, t=PACK)
-        nc.scalar.copy(dn_dealt[:, :32], dn_rows[:, :32])
-        nc.vector.tensor_copy(dn_dealt[:, 32:], dn_rows[:, 32:])
-        ws_rows = keep("ws_rows", [P, N], U8)
+        nc.scalar.copy(dn_dealt[:, :DN_S], dn_rows[:, :DN_S])
+        nc.vector.tensor_copy(dn_dealt[:, DN_S:], dn_rows[:, DN_S:])
+        dn_w = keep("dn_w", [P, R], U32)
+        dn_s = keep("dn_s", [P, R], U8)
+        nc.vector.quantize_mx(out=dn_w[:].bitcast(FP8X4), scales=dn_s[:], in_=dn_bf[:])
+        ws_rows = keep("ws_rows", [P, N], U8, tag="dn_raw")
         nc.vector.tensor_copy(ws_rows[:].rearrange("p (t m) -> p t m", t=PACK), ws_raw[:].rearrange("p (m t) -> p t m", t=PACK))
         for q in range(4):
             nc.sync.dma_start(w_s[32 * q : 32 * q + 4, :].bitcast(I32), ws_rows[P - 32 + 8 * q : P - 24 + 8 * q, :].bitcast(I32))
@@ -86,9 +90,6 @@ def tile_list_xcross_reluP_kernel(tc, tab_words, tab_scales, wb_words, wb_scales
         load_x0(1, "ws_raw")
         bias1 = keep("bias1", [P, PACK], F32)
         nc.gpsimd.tensor_scalar(bias1[:], bias[:], 1.0, 1.0, ALU.mult, ALU.add)
-        dn_w = keep("dn_w", [P, R], U32)
-        dn_s = keep("dn_s", [P, R], U8)
-        nc.vector.quantize_mx(out=dn_w[:].bitcast(FP8X4), scales=dn_s[:], in_=dn_bf[:])
         v_w_all = keep("v_w", [P, J], U32, tag="dn_bf")
         v_w = [v_w_all[:, :HALF], v_w_all[:, HALF:]]
         for j0, count in ((0, QUARTER), (QUARTER, QUARTER), (HALF, HALF)):
@@ -154,7 +155,7 @@ def tile_list_xcross_reluP_kernel(tc, tab_words, tab_scales, wb_words, wb_scales
             nc.vector.tensor_copy(x_first[g][:], x0[0][:].indirect(listed(g * QUARTER, QUARTER)))
         for c in range(8):
             first(c, c)
-        h_w0 = keep("h_w0", [P, HALF], U32, tag="v_rows")
+        h_w0 = keep("h_w0", [P, HALF], U32, tag="dn_raw")
         for g in range(2):
             cols = slice(g * QUARTER, (g + 1) * QUARTER)
             nc.vector.quantize_mx(out=h_w0[:, cols].bitcast(FP8X4), scales=h_s[0][:, cols], in_=h_bf0[g][:])

@@ -103,7 +103,10 @@ def tile_list_xcross_reluP_kernel(tc, tab_words, tab_scales, wb_words, wb_scales
         h_s = [keep("h_s%d" % h, [P, HALF], U8) for h in range(2)]
         h_bf0 = [keep("h_bf0%d" % g, [P, QUARTER * PACK], BF16) for g in range(2)]
         h_bf1 = keep("h_bf1", [P, HALF * PACK], BF16)
-        res0 = keep("res0", [P, PACK, HALF], F32)
+        results = keep("results", [P, 17 * QUARTER], F32)
+        res0 = results[:, 6 * QUARTER : 14 * QUARTER].rearrange("p (t j) -> p t j", t=PACK)
+        res2 = results[:, : 8 * QUARTER].rearrange("p (t j) -> p t j", t=PACK)[:, :, :QUARTER]
+        res3 = results[:, 5 * QUARTER :].rearrange("p (t j) -> p t j", t=PACK)[:, :, :QUARTER]
 
         def first(c, bank):
             cols = slice(c * SUB, (c + 1) * SUB)
@@ -132,23 +135,21 @@ def tile_list_xcross_reluP_kernel(tc, tab_words, tab_scales, wb_words, wb_scales
         res_s = keep("res_s", [P, J], U8)
         out_rows = out_0.rearrange("(p t) j -> p t j", t=PACK)
         out_words = out_1[0].rearrange("p j i -> p (j i)").bitcast(I32)
-        rounded = {}
 
-        def cross(res, h, t, c0, count, lifted):
-            nc.vector.tensor_tensor(res[:, t, c0 : c0 + count], x0[t][:].indirect(listed(h * HALF + c0, count)), lifted, ALU.mult)
+        def cross(dst, t, j0, count, lifted):
+            nc.vector.tensor_tensor(dst, x0[t][:].indirect(listed(j0, count)), lifted, ALU.mult)
 
-        def store(res, h, t, c0=0, count=HALF):
-            nc.sync.dma_start(out_rows[:, t, h * HALF + c0 : h * HALF + c0 + count], res[:, t, c0 : c0 + count])
+        def store(src, t, j0, count):
+            nc.sync.dma_start(out_rows[:, t, j0 : j0 + count], src)
 
-        def round_out(engine_copy, res, h, c0, count, tag=None):
-            rounded[h, c0] = keep("rounded%d_%d" % (h, c0), [P, count * PACK], BF16, tag=tag)
-            engine_copy(rounded[h, c0][:].rearrange("p (c i t) -> p c t i", i=4, t=PACK),
-                        res[:, :, c0 : c0 + count].rearrange("p t (c i) -> p c t i", i=4))
+        def round_out(engine_copy, rounded, res):
+            engine_copy(rounded.rearrange("p (c i t) -> p c t i", i=4, t=PACK), res.rearrange("p t (c i) -> p c t i", i=4))
 
-        def quantise_out(h, c0, count):
-            cols = slice(h * HALF + c0, h * HALF + c0 + count)
-            nc.vector.quantize_mx(out=res_w[:, cols].bitcast(FP8X4), scales=res_s[:, cols], in_=rounded[h, c0][:])
-            nc.sync.dma_start(out_words[:, cols], res_w[:, cols].bitcast(I32))
+        def quantise_out(rounded, j0, count):
+            nc.vector.quantize_mx(out=res_w[:, j0 : j0 + count].bitcast(FP8X4), scales=res_s[:, j0 : j0 + count], in_=rounded)
+
+        def store_words(j0):
+            nc.sync.dma_start(out_words[:, j0 : j0 + QUARTER], res_w[:, j0 : j0 + QUARTER].bitcast(I32))
 
         x_first = [keep("x_first%d" % g, [P, QUARTER], F32) for g in range(2)]
         for g in range(2):
@@ -165,10 +166,8 @@ def tile_list_xcross_reluP_kernel(tc, tab_words, tab_scales, wb_words, wb_scales
         for g in range(2):
             cols = slice(g * QUARTER, (g + 1) * QUARTER)
             nc.vector.scalar_tensor_tensor(res0[:, 0, cols], y0[0][:, cols], bias1[:, 0:1], x_first[g][:], ALU.add, ALU.mult)
-        store(res0, 0, 0)
-        res1 = keep("res1", [P, PACK, HALF], F32)
-        up01b = keep("up01b", [P, QUARTER], F32)
-        up01 = [res1[:, 0, SUB : SUB + QUARTER], up01b[:]]
+        store(res0[:, 0, :], 0, 0, HALF)
+        up01 = [res2[:, 0, :], res3[:, 0, :]]
         for g in range(2):
             lift(up01[g], y0[1], 1, g * QUARTER, QUARTER)
         up02 = keep("up02", [P, HALF], F32)
@@ -177,36 +176,55 @@ def tile_list_xcross_reluP_kernel(tc, tab_words, tab_scales, wb_words, wb_scales
         nc.vector.quantize_mx(out=h_w1[:].bitcast(FP8X4), scales=h_s[1][:], in_=h_bf1[:])
         y1 = [second(1, t, PACK + t, h_w1) for t in range(PACK)]
         for g in range(2):
-            cross(res0, 0, 1, g * QUARTER, QUARTER, up01[g])
-        store(res0, 0, 1)
-        up03 = [res1[:, 1 + g, SUB : SUB + QUARTER] for g in range(2)]
+            cross(res0[:, 1, g * QUARTER : (g + 1) * QUARTER], 1, g * QUARTER, QUARTER, up01[g])
+        store(res0[:, 1, :], 1, 0, HALF)
+        up03 = [res2[:, 1 + g, :] for g in range(2)]
         for g in range(2):
             lift(up03[g], y0[3], 3, g * QUARTER, QUARTER)
         up1 = {}
         for t in range(1, PACK):
             up1[t] = keep("up1%d" % t, [P, HALF], F32)
             lift(up1[t][:], y1[t], t, 0, HALF)
-        cross(res0, 0, 2, 0, HALF, up02[:])
-        store(res0, 0, 2)
-        nc.vector.scalar_tensor_tensor(res1[:, 0, :], y1[0][:], bias1[:, 0:1], x_third[:], ALU.add, ALU.mult)
-        store(res1, 1, 0)
+        cross(res0[:, 2, :], 2, 0, HALF, up02[:])
+        store(res0[:, 2, :], 2, 0, HALF)
+        for g, res in enumerate((res2, res3)):
+            cols = slice(g * QUARTER, (g + 1) * QUARTER)
+            nc.vector.scalar_tensor_tensor(res[:, 0, :], y1[0][:, cols], bias1[:, 0:1], x_third[:, cols], ALU.add, ALU.mult)
+            store(res[:, 0, :], 0, HALF + g * QUARTER, QUARTER)
         for g in range(2):
-            cross(res0, 0, 3, g * QUARTER, QUARTER, up03[g])
-        store(res0, 0, 3)
-        for g in range(2):
-            round_out(nc.scalar.copy, res0, 0, g * QUARTER, QUARTER)
-        for t in (1, 2):
-            cross(res1, 1, t, 0, HALF, up1[t][:])
-            store(res1, 1, t)
-        quantise_out(0, 0, QUARTER)
-        cross(res1, 1, 3, 0, QUARTER, up1[3][:, :QUARTER])
-        store(res1, 1, 3, 0, QUARTER)
-        round_out(nc.scalar.copy, res1, 1, 0, QUARTER)
-        cross(res1, 1, 3, QUARTER, QUARTER, up1[3][:, QUARTER:])
-        store(res1, 1, 3, QUARTER, QUARTER)
-        quantise_out(0, QUARTER, QUARTER)
-        round_out(nc.vector.tensor_copy, res1, 1, QUARTER, QUARTER, tag="res0")
-        quantise_out(1, 0, QUARTER)
-        quantise_out(1, QUARTER, QUARTER)
+            cross(res0[:, 3, g * QUARTER : (g + 1) * QUARTER], 3, g * QUARTER, QUARTER, up03[g])
+        store(res0[:, 3, :], 3, 0, HALF)
+        rounded0 = keep("rounded0", [P, QUARTER * PACK], BF16)
+        rounded1 = results[:, 14 * QUARTER : 16 * QUARTER].bitcast(BF16)
+        round_out(nc.scalar.copy, rounded0[:], res0[:, :, :QUARTER])
+        round_out(nc.scalar.copy, rounded1, res0[:, :, QUARTER:])
+
+        def cross_late(res, g, t):
+            cross(res[:, t, :], t, HALF + g * QUARTER, QUARTER, up1[t][:, g * QUARTER : (g + 1) * QUARTER])
+            store(res[:, t, :], t, HALF + g * QUARTER, QUARTER)
+
+        cross_late(res2, 0, 1)
+        cross_late(res2, 0, 2)
+        quantise_out(rounded0[:], 0, QUARTER)
+        store_words(0)
+        cross_late(res2, 0, 3)
+        rounded2 = keep("rounded2", [P, QUARTER * PACK], BF16)
+        round_out(nc.scalar.copy, rounded2[:], res2)
+        cross_late(res3, 1, 1)
+        quantise_out(rounded1, QUARTER, QUARTER)
+        store_words(QUARTER)
+        cross_late(res3, 1, 2)
+        for e in range(2):
+            cross(res3[:, 3, e * SUB : (e + 1) * SUB], 3, J - QUARTER + e * SUB, SUB, up1[3][:, QUARTER + e * SUB : QUARTER + (e + 1) * SUB])
+        store(res3[:, 3, :], 3, J - QUARTER, QUARTER)
+        rounded3 = keep("rounded3", [P, SUB * PACK], BF16)
+        round_out(nc.scalar.copy, rounded3[:], res3[:, :, :SUB])
+        quantise_out(rounded2[:], HALF, QUARTER)
+        store_words(HALF)
+        rounded4 = res2[:, 0, :].bitcast(BF16)
+        round_out(nc.vector.tensor_copy, rounded4, res3[:, :, SUB:])
+        quantise_out(rounded3[:], J - QUARTER, SUB)
+        quantise_out(rounded4, J - SUB, SUB)
+        store_words(J - QUARTER)
         for q in range(4):
             nc.scalar.dma_start(out_2[0, 4 * q : 4 * q + 4, :].bitcast(I32), res_s[32 * q : 32 * q + 4, :].bitcast(I32))

@@ -28,6 +28,7 @@ def tile_list_xcross_reluP_kernel(tc, tab_words, tab_scales, wb_words, wb_scales
     nc = tc.nc
     with ExitStack() as ctx:
         held = ctx.enter_context(tc.tile_pool(name="held", bufs=1))
+        laid = ctx.enter_context(tc.tile_pool(name="laid", bufs=1))
         psum = ctx.enter_context(tc.psum_pool(name="psum", bufs=1))
 
         def keep(name, shape, dtype, tag=None):
@@ -38,7 +39,7 @@ def tile_list_xcross_reluP_kernel(tc, tab_words, tab_scales, wb_words, wb_scales
 
         rows16 = slice(P - 16, P)
         offsets = held.tile([P, J // 16], U16, name="offsets")
-        ws_raw = keep("ws_raw", [P, N], U8)
+        ws_raw = laid.tile([P, N], U8, name="ws_raw", offset=0, align_bytes=64)
         w_s = keep("w_s", [P, 2 * N], U8)
         tab_s = keep("tab_s", [P, T], U8)
         v_s_all = keep("v_s", [P, J], U8)
@@ -60,9 +61,9 @@ def tile_list_xcross_reluP_kernel(tc, tab_words, tab_scales, wb_words, wb_scales
         x0_rows = x0T.rearrange("(p t) c -> p t c", t=PACK)
         x0 = []
 
-        def load_x0(t, tag):
-            x0.append(keep("x0_%d" % t, [P, T], F32, tag=tag))
-            nc.sync.dma_start(x0[t][:], x0_rows[:, t, :])
+        def load_x0(t, plane):
+            x0.append(plane)
+            nc.sync.dma_start(plane[:], x0_rows[:, t, :])
 
         def to_quadrants(plane, rows):
             for q in range(4):
@@ -72,7 +73,7 @@ def tile_list_xcross_reluP_kernel(tc, tab_words, tab_scales, wb_words, wb_scales
         nc.vector.tensor_copy(v_rows[:], tab_s[:].indirect(offsets[:]))
         to_quadrants(v_s_all, v_rows)
         v_s = [v_s_all[:, :HALF], v_s_all[:, HALF:]]
-        load_x0(0, "tab_s")
+        load_x0(0, keep("x0_0", [P, T], F32, tag="tab_s"))
         dn_bf = keep("dn_bf", [P, R * PACK], BF16)
         dn_dealt = dn_bf[:].rearrange("p (t c e i) -> p c i e t", t=PACK, e=2, i=PACK)
         dn_rows = dn_raw[:].rearrange("p i (c e t) -> p c i e t", e=2, t=PACK)
@@ -85,20 +86,20 @@ def tile_list_xcross_reluP_kernel(tc, tab_words, tab_scales, wb_words, wb_scales
         nc.vector.tensor_copy(ws_rows[:].rearrange("p (t m) -> p t m", t=PACK), ws_raw[:].rearrange("p (m t) -> p t m", t=PACK))
         for q in range(4):
             nc.sync.dma_start(w_s[32 * q : 32 * q + 4, :].bitcast(I32), ws_rows[P - 32 + 8 * q : P - 24 + 8 * q, :].bitcast(I32))
-        bias = keep("bias", [P, PACK], F32, tag="v_rows")
+        bias = laid.tile([P, PACK], F32, name="bias", offset=0, align_bytes=64)
         nc.sync.dma_start(bias[:], b.rearrange("(p t) -> p t", t=PACK))
-        load_x0(1, "ws_raw")
+        load_x0(1, laid.tile([P, T], F32, name="x0_1", offset=64, align_bytes=64))
         bias1 = keep("bias1", [P, PACK], F32)
         nc.gpsimd.tensor_scalar(bias1[:], bias[:], 1.0, 1.0, ALU.mult, ALU.add)
         v_w_all = keep("v_w", [P, J], U32, tag="dn_bf")
         v_w = [v_w_all[:, :HALF], v_w_all[:, HALF:]]
         for j0, count in ((0, QUARTER), (QUARTER, QUARTER), (HALF, HALF)):
             nc.vector.tensor_copy(v_w_all[:, j0 : j0 + count], tab_w[:].indirect(listed(j0, count)))
-        load_x0(2, "tab_w")
+        load_x0(2, keep("x0_2", [P, T], F32, tag="tab_w"))
         w_all = keep("w_all", [P, 2, 2 * N], U8)
         nc.vector.tensor_copy(w_all[:].bitcast(U16).rearrange("p u (t m) -> p u t m", t=PACK), w_raw[:].bitcast(U16).rearrange("p u (m t) -> p u t m", t=PACK))
         w_w = [w_all[:, u, :] for u in range(2)]
-        load_x0(3, "w_raw")
+        load_x0(3, keep("x0_3", [P, T], F32, tag="w_raw"))
 
         h_s = [keep("h_s%d" % h, [P, HALF], U8) for h in range(2)]
         h_bf0 = [keep("h_bf0%d" % g, [P, QUARTER * PACK], BF16) for g in range(2)]
@@ -132,7 +133,7 @@ def tile_list_xcross_reluP_kernel(tc, tab_words, tab_scales, wb_words, wb_scales
             nc.scalar.activation(dst, y[:, c0 : c0 + count], ACT.Identity, bias=bias1[:, t : t + 1])
 
         res_w = keep("res_w", [P, J], U32)
-        res_s = keep("res_s", [P, J], U8)
+        res_s = keep("res_s", [P, QUARTER], U8)
         out_rows = out_0.rearrange("(p t) j -> p t j", t=PACK)
         out_words = out_1[0].rearrange("p j i -> p (j i)").bitcast(I32)
 
@@ -146,7 +147,8 @@ def tile_list_xcross_reluP_kernel(tc, tab_words, tab_scales, wb_words, wb_scales
             engine_copy(rounded.rearrange("p (c i t) -> p c t i", i=4, t=PACK), res.rearrange("p t (c i) -> p c t i", i=4))
 
         def quantise_out(rounded, j0, count):
-            nc.vector.quantize_mx(out=res_w[:, j0 : j0 + count].bitcast(FP8X4), scales=res_s[:, j0 : j0 + count], in_=rounded)
+            c0 = j0 % QUARTER
+            nc.vector.quantize_mx(out=res_w[:, j0 : j0 + count].bitcast(FP8X4), scales=res_s[4 * (j0 // QUARTER) :, c0 : c0 + count], in_=rounded)
 
         def store_words(j0):
             nc.sync.dma_start(out_words[:, j0 : j0 + QUARTER], res_w[:, j0 : j0 + QUARTER].bitcast(I32))
@@ -227,4 +229,4 @@ def tile_list_xcross_reluP_kernel(tc, tab_words, tab_scales, wb_words, wb_scales
         quantise_out(rounded4, J - SUB, SUB)
         store_words(J - QUARTER)
         for q in range(4):
-            nc.scalar.dma_start(out_2[0, 4 * q : 4 * q + 4, :].bitcast(I32), res_s[32 * q : 32 * q + 4, :].bitcast(I32))
+            (nc.scalar, nc.sync)[q // 2].dma_start(out_2[0, 4 * q : 4 * q + 4, :].bitcast(I32).rearrange("r (g c) -> g r c", g=4), res_s[32 * q : 32 * q + 16, :].bitcast(I32))

@@ -52,7 +52,7 @@ def tile_list_xcross_reluP_kernel(tc, tab_words, tab_scales, wb_words, wb_scales
         dn_raw = keep("dn_raw", [P, PACK, R], F32)
         nc.sync.dma_start(dn_raw[:], dn.rearrange("(p i) r -> p i r", i=PACK))
         for u, scales in enumerate((wb_scales, upw_scales)):
-            nc.sync.dma_start(ws_raw[P - 32 + u : P : 2, :].bitcast(I32), scales[0].bitcast(I32))
+            nc.sync.dma_start(ws_raw[P - 32 + u : P : 2, :].bitcast(I32), scales[0].bitcast(I32).rearrange("(q r) n -> r q n", r=4))
         tab_w = keep("tab_w", [P, T], U32)
         nc.sync.dma_start(tab_w[:].bitcast(I32), tab_words[0].rearrange("p t i -> p (t i)").bitcast(I32))
         w_raw = keep("w_raw", [P, 2, 2 * N], U8)
@@ -66,8 +66,8 @@ def tile_list_xcross_reluP_kernel(tc, tab_words, tab_scales, wb_words, wb_scales
             nc.sync.dma_start(plane[:], x0_rows[:, t, :])
 
         def to_quadrants(plane, rows):
-            for q in range(4):
-                nc.sync.dma_start(plane[32 * q : 32 * q + 4, :].bitcast(I32), rows[P - 16 + 4 * q : P - 12 + 4 * q, :].bitcast(I32))
+            for r in range(4):
+                nc.sync.dma_start(plane[r:P:32, :].bitcast(I32), rows[P - 16 + r : P : 4, :].bitcast(I32))
 
         v_rows = keep("v_rows", [P, J], U8)
         nc.vector.tensor_copy(v_rows[:], tab_s[:].indirect(offsets[:]))
@@ -84,8 +84,8 @@ def tile_list_xcross_reluP_kernel(tc, tab_words, tab_scales, wb_words, wb_scales
         nc.vector.quantize_mx(out=dn_w[:].bitcast(FP8X4), scales=dn_s[:], in_=dn_bf[:])
         ws_rows = keep("ws_rows", [P, N], U8, tag="dn_raw")
         nc.vector.tensor_copy(ws_rows[:].rearrange("p (t m) -> p t m", t=PACK), ws_raw[:].rearrange("p (m t) -> p t m", t=PACK))
-        for q in range(4):
-            nc.sync.dma_start(w_s[32 * q : 32 * q + 4, :].bitcast(I32), ws_rows[P - 32 + 8 * q : P - 24 + 8 * q, :].bitcast(I32))
+        for r in range(4):
+            nc.sync.dma_start(w_s[r:P:32, :].bitcast(I32), ws_rows[P - 32 + 8 * r : P - 24 + 8 * r, :].bitcast(I32))
         bias = laid.tile([P, PACK], F32, name="bias", offset=0, align_bytes=64)
         nc.sync.dma_start(bias[:], b.rearrange("(p t) -> p t", t=PACK))
         load_x0(1, laid.tile([P, T], F32, name="x0_1", offset=64, align_bytes=64))

@@ -21,7 +21,8 @@ PACK = 4
 HALF = 512
 QUARTER = 256
 SUB = 128
-DN_S = 22
+DN_S = 30
+SCALES_AT = 16384
 
 
 def tile_list_xcross_reluP_kernel(tc, tab_words, tab_scales, wb_words, wb_scales, dn, upw_words, upw_scales, x0T, b, offs, out_0, out_1, out_2):
@@ -39,12 +40,13 @@ def tile_list_xcross_reluP_kernel(tc, tab_words, tab_scales, wb_words, wb_scales
 
         rows16 = slice(P - 16, P)
         offsets = held.tile([P, J // 16], U16, name="offsets")
-        ws_raw = laid.tile([P, N], U8, name="ws_raw", offset=0, align_bytes=64)
+        ws_raw = laid.tile([P, 2 * N], U8, name="ws_raw", offset=0, align_bytes=64)
         w_s = keep("w_s", [P, 2 * N], U8)
-        tab_s = keep("tab_s", [P, T], U8)
+        tab_s = laid.tile([P, T], U8, name="tab_s", offset=SCALES_AT, align_bytes=64)
         v_s_all = keep("v_s", [P, J], U8)
         nc.vector.memset(tab_s[: P - 16, :].bitcast(I32), 0)
-        nc.vector.memset(ws_raw[: P - 32, :].bitcast(I32), 0)
+        nc.vector.memset(ws_raw[:48, :].bitcast(I32), 0)
+        nc.vector.memset(ws_raw[64:, :].bitcast(I32), 0)
         nc.vector.memset(v_s_all[:].bitcast(I32), 0)
         nc.vector.memset(w_s[:].bitcast(I32), 0)
         nc.sync.dma_start(offsets[:], offs)
@@ -52,12 +54,11 @@ def tile_list_xcross_reluP_kernel(tc, tab_words, tab_scales, wb_words, wb_scales
         dn_raw = keep("dn_raw", [P, PACK, R], F32)
         nc.sync.dma_start(dn_raw[:], dn.rearrange("(p i) r -> p i r", i=PACK))
         for u, scales in enumerate((wb_scales, upw_scales)):
-            nc.sync.dma_start(ws_raw[P - 32 + u : P : 2, :].bitcast(I32), scales[0].bitcast(I32).rearrange("(q r) n -> r q n", r=4))
+            nc.sync.dma_start(ws_raw[48:64, u * N : (u + 1) * N].bitcast(I32), scales[0].bitcast(I32))
         tab_w = keep("tab_w", [P, T], U32)
         nc.sync.dma_start(tab_w[:].bitcast(I32), tab_words[0].rearrange("p t i -> p (t i)").bitcast(I32))
-        w_raw = keep("w_raw", [P, 2, 2 * N], U8)
-        for u, words in enumerate((wb_words, upw_words)):
-            nc.sync.dma_start(w_raw[:, u, :].bitcast(I32), words[0].bitcast(I32))
+        wb_raw = keep("wb_raw", [P, 2 * N], U8)
+        nc.sync.dma_start(wb_raw[:].bitcast(I32), wb_words[0].bitcast(I32))
         x0_rows = x0T.rearrange("(p t) c -> p t c", t=PACK)
         x0 = []
 
@@ -73,19 +74,21 @@ def tile_list_xcross_reluP_kernel(tc, tab_words, tab_scales, wb_words, wb_scales
         nc.vector.tensor_copy(v_rows[:], tab_s[:].indirect(offsets[:]))
         to_quadrants(v_s_all, v_rows)
         v_s = [v_s_all[:, :HALF], v_s_all[:, HALF:]]
-        load_x0(0, keep("x0_0", [P, T], F32, tag="tab_s"))
+        load_x0(0, laid.tile([P, T], F32, name="x0_0", offset=SCALES_AT + 1024, align_bytes=64))
+        upw_raw = laid.tile([P, 2 * N], U8, name="upw_raw", offset=SCALES_AT, align_bytes=64)
+        nc.sync.dma_start(upw_raw[:].bitcast(I32), upw_words[0].bitcast(I32))
         dn_bf = keep("dn_bf", [P, R * PACK], BF16)
         dn_dealt = dn_bf[:].rearrange("p (t c e i) -> p c i e t", t=PACK, e=2, i=PACK)
         dn_rows = dn_raw[:].rearrange("p i (c e t) -> p c i e t", e=2, t=PACK)
         nc.scalar.copy(dn_dealt[:, :DN_S], dn_rows[:, :DN_S])
         nc.vector.tensor_copy(dn_dealt[:, DN_S:], dn_rows[:, DN_S:])
+        ws_rows = keep("ws_rows", [P, 2 * N], U8)
+        nc.vector.tensor_copy(ws_rows[:].rearrange("p (u t m) -> p u t m", u=2, t=PACK), ws_raw[:].rearrange("p (u m t) -> p u t m", u=2, t=PACK))
         dn_w = keep("dn_w", [P, R], U32)
         dn_s = keep("dn_s", [P, R], U8)
         nc.vector.quantize_mx(out=dn_w[:].bitcast(FP8X4), scales=dn_s[:], in_=dn_bf[:])
-        ws_rows = keep("ws_rows", [P, N], U8, tag="dn_raw")
-        nc.vector.tensor_copy(ws_rows[:].rearrange("p (t m) -> p t m", t=PACK), ws_raw[:].rearrange("p (m t) -> p t m", t=PACK))
         for r in range(4):
-            nc.sync.dma_start(w_s[r:P:32, :].bitcast(I32), ws_rows[P - 32 + 8 * r : P - 24 + 8 * r, :].bitcast(I32))
+            nc.sync.dma_start(w_s[r:P:32, :].bitcast(I32), ws_rows[48 + r : 64 : 4, :].bitcast(I32))
         bias = laid.tile([P, PACK], F32, name="bias", offset=0, align_bytes=64)
         nc.sync.dma_start(bias[:], b.rearrange("(p t) -> p t", t=PACK))
         load_x0(1, laid.tile([P, T], F32, name="x0_1", offset=64, align_bytes=64))
@@ -93,21 +96,28 @@ def tile_list_xcross_reluP_kernel(tc, tab_words, tab_scales, wb_words, wb_scales
         nc.gpsimd.tensor_scalar(bias1[:], bias[:], 1.0, 1.0, ALU.mult, ALU.add)
         v_w_all = keep("v_w", [P, J], U32, tag="dn_bf")
         v_w = [v_w_all[:, :HALF], v_w_all[:, HALF:]]
-        for j0, count in ((0, QUARTER), (QUARTER, QUARTER), (HALF, HALF)):
+        for j0, count in ((0, SUB), (SUB, SUB), (QUARTER, QUARTER), (HALF, HALF)):
             nc.vector.tensor_copy(v_w_all[:, j0 : j0 + count], tab_w[:].indirect(listed(j0, count)))
         load_x0(2, keep("x0_2", [P, T], F32, tag="tab_w"))
-        w_all = keep("w_all", [P, 2, 2 * N], U8)
-        nc.vector.tensor_copy(w_all[:].bitcast(U16).rearrange("p u (t m) -> p u t m", t=PACK), w_raw[:].bitcast(U16).rearrange("p u (m t) -> p u t m", t=PACK))
-        w_w = [w_all[:, u, :] for u in range(2)]
-        load_x0(3, keep("x0_3", [P, T], F32, tag="w_raw"))
+        wb_w = keep("wb_w", [P, 2 * N], U8)
+        nc.vector.tensor_copy(wb_w[:].bitcast(U16).rearrange("p (t m) -> p t m", t=PACK), wb_raw[:].bitcast(U16).rearrange("p (m t) -> p t m", t=PACK))
+        load_x0(3, keep("x0_3", [P, T], F32, tag="wb_raw"))
+        upw_dealt = upw_raw[:].rearrange("p (m t e) -> p t m e", t=PACK, e=2)
+        upw_w = [keep("upw_w0", [P, N], U8)]
+        nc.gpsimd.tensor_copy(upw_w[0][:].rearrange("p (t m e) -> p t m e", t=2, e=2), upw_dealt[:, :2])
+
+        def weight_words(u, t):
+            if u == 0:
+                return wb_w[:, 2 * t * P : 2 * (t + 1) * P]
+            return upw_w[t // 2][:, 2 * (t % 2) * P : 2 * (t % 2 + 1) * P]
 
         h_s = [keep("h_s%d" % h, [P, HALF], U8) for h in range(2)]
         h_bf0 = [keep("h_bf0%d" % g, [P, QUARTER * PACK], BF16) for g in range(2)]
         h_bf1 = keep("h_bf1", [P, HALF * PACK], BF16)
-        results = keep("results", [P, 17 * QUARTER], F32)
+        results = keep("results", [P, 14 * QUARTER], F32)
         res0 = results[:, 6 * QUARTER : 14 * QUARTER].rearrange("p (t j) -> p t j", t=PACK)
         res2 = results[:, : 8 * QUARTER].rearrange("p (t j) -> p t j", t=PACK)[:, :, :QUARTER]
-        res3 = results[:, 5 * QUARTER :].rearrange("p (t j) -> p t j", t=PACK)[:, :, :QUARTER]
+        res3 = results[:, 5 * QUARTER : 13 * QUARTER].rearrange("p (t j) -> p t j", t=PACK)[:, :, :QUARTER]
 
         def first(c, bank):
             cols = slice(c * SUB, (c + 1) * SUB)
@@ -125,14 +135,14 @@ def tile_list_xcross_reluP_kernel(tc, tab_words, tab_scales, wb_words, wb_scales
             moving = ((v_w[h], v_s[h]), (h_w[:], h_s[h][:]))
             for i, u in enumerate(((0, 1), (1, 0))[h]):
                 mw, ms = moving[u]
-                nc.tensor.matmul_mx(out=y[:], lhsT=w_w[u][:, 2 * t * P : 2 * (t + 1) * P].bitcast(FP4X4), lhsT_scale=w_s[:, u * N + t * P : u * N + (t + 1) * P],
+                nc.tensor.matmul_mx(out=y[:], lhsT=weight_words(u, t).bitcast(FP4X4), lhsT_scale=w_s[:, u * N + t * P : u * N + (t + 1) * P],
                                     rhs=mw.bitcast(FP8X4), rhs_scale=ms, start=(i == 0), stop=(i == 1))
             return y
 
         def lift(dst, y, t, c0, count):
             nc.scalar.activation(dst, y[:, c0 : c0 + count], ACT.Identity, bias=bias1[:, t : t + 1])
 
-        res_w = keep("res_w", [P, J], U32)
+        res_w = {}
         res_s = keep("res_s", [P, QUARTER], U8)
         out_rows = out_0.rearrange("(p t) j -> p t j", t=PACK)
         out_words = out_1[0].rearrange("p j i -> p (j i)").bitcast(I32)
@@ -148,20 +158,22 @@ def tile_list_xcross_reluP_kernel(tc, tab_words, tab_scales, wb_words, wb_scales
 
         def quantise_out(rounded, j0, count):
             c0 = j0 % QUARTER
-            nc.vector.quantize_mx(out=res_w[:, j0 : j0 + count].bitcast(FP8X4), scales=res_s[4 * (j0 // QUARTER) :, c0 : c0 + count], in_=rounded)
+            nc.vector.quantize_mx(out=res_w[j0 // QUARTER][:, c0 : c0 + count].bitcast(FP8X4), scales=res_s[4 * (j0 // QUARTER) :, c0 : c0 + count], in_=rounded)
 
         def store_words(j0):
-            nc.sync.dma_start(out_words[:, j0 : j0 + QUARTER], res_w[:, j0 : j0 + QUARTER].bitcast(I32))
+            nc.sync.dma_start(out_words[:, j0 : j0 + QUARTER], res_w[j0 // QUARTER][:].bitcast(I32))
 
         x_first = [keep("x_first%d" % g, [P, QUARTER], F32) for g in range(2)]
         for g in range(2):
             nc.vector.tensor_copy(x_first[g][:], x0[0][:].indirect(listed(g * QUARTER, QUARTER)))
         for c in range(8):
             first(c, c)
-        h_w0 = keep("h_w0", [P, HALF], U32, tag="dn_raw")
+        h_w0 = keep("h_w0", [P, HALF], U32, tag="ws_rows")
         for g in range(2):
             cols = slice(g * QUARTER, (g + 1) * QUARTER)
             nc.vector.quantize_mx(out=h_w0[:, cols].bitcast(FP8X4), scales=h_s[0][:, cols], in_=h_bf0[g][:])
+        upw_w.append(keep("upw_w1", [P, N], U8, tag="h_bf01"))
+        nc.gpsimd.tensor_copy(upw_w[1][:].rearrange("p (t m e) -> p t m e", t=2, e=2), upw_dealt[:, 2:])
         x_third = keep("x_third", [P, HALF], F32, tag="h_bf00")
         nc.vector.tensor_copy(x_third[:], x0[0][:].indirect(listed(HALF, HALF)))
         y0 = [second(0, t, t, h_w0) for t in range(PACK)]
@@ -185,8 +197,13 @@ def tile_list_xcross_reluP_kernel(tc, tab_words, tab_scales, wb_words, wb_scales
             lift(up03[g], y0[3], 3, g * QUARTER, QUARTER)
         up1 = {}
         for t in range(1, PACK):
-            up1[t] = keep("up1%d" % t, [P, HALF], F32)
-            lift(up1[t][:], y1[t], t, 0, HALF)
+            count = HALF if t < PACK - 1 else HALF - SUB
+            up1[t] = keep("up1%d" % t, [P, count], F32)
+            lift(up1[t][:], y1[t], t, 0, count)
+        up_last = keep("up_last", [P, SUB], F32)
+        lift(up_last[:], y1[PACK - 1], PACK - 1, HALF - SUB, SUB)
+        for g in range(4):
+            res_w[g] = keep("res_w%d" % g, [P, QUARTER], U32, tag="up13" if g == 2 else None)
         cross(res0[:, 2, :], 2, 0, HALF, up02[:])
         store(res0[:, 2, :], 2, 0, HALF)
         for g, res in enumerate((res2, res3)):
@@ -196,9 +213,10 @@ def tile_list_xcross_reluP_kernel(tc, tab_words, tab_scales, wb_words, wb_scales
         for g in range(2):
             cross(res0[:, 3, g * QUARTER : (g + 1) * QUARTER], 3, g * QUARTER, QUARTER, up03[g])
         store(res0[:, 3, :], 3, 0, HALF)
-        rounded0 = keep("rounded0", [P, QUARTER * PACK], BF16)
-        rounded1 = results[:, 14 * QUARTER : 16 * QUARTER].bitcast(BF16)
-        round_out(nc.scalar.copy, rounded0[:], res0[:, :, :QUARTER])
+        rounded01 = keep("rounded01", [P, HALF * PACK], BF16, tag="dn_bf")
+        rounded0 = rounded01[:, : QUARTER * PACK]
+        rounded1 = rounded01[:, QUARTER * PACK :]
+        round_out(nc.scalar.copy, rounded0, res0[:, :, :QUARTER])
         round_out(nc.scalar.copy, rounded1, res0[:, :, QUARTER:])
 
         def cross_late(res, g, t):
@@ -207,17 +225,17 @@ def tile_list_xcross_reluP_kernel(tc, tab_words, tab_scales, wb_words, wb_scales
 
         cross_late(res2, 0, 1)
         cross_late(res2, 0, 2)
-        quantise_out(rounded0[:], 0, QUARTER)
+        quantise_out(rounded0, 0, QUARTER)
         store_words(0)
         cross_late(res2, 0, 3)
         rounded2 = keep("rounded2", [P, QUARTER * PACK], BF16)
         round_out(nc.scalar.copy, rounded2[:], res2)
-        cross_late(res3, 1, 1)
         quantise_out(rounded1, QUARTER, QUARTER)
         store_words(QUARTER)
+        cross_late(res3, 1, 1)
         cross_late(res3, 1, 2)
-        for e in range(2):
-            cross(res3[:, 3, e * SUB : (e + 1) * SUB], 3, J - QUARTER + e * SUB, SUB, up1[3][:, QUARTER + e * SUB : QUARTER + (e + 1) * SUB])
+        for e, lifted in enumerate((up1[3][:, QUARTER:], up_last[:])):
+            cross(res3[:, 3, e * SUB : (e + 1) * SUB], 3, J - QUARTER + e * SUB, SUB, lifted)
         store(res3[:, 3, :], 3, J - QUARTER, QUARTER)
         rounded3 = keep("rounded3", [P, SUB * PACK], BF16)
         round_out(nc.scalar.copy, rounded3[:], res3[:, :, :SUB])

@@ -117,7 +117,7 @@ def tile_list_xcross_reluP_kernel(tc, tab_words, tab_scales, wb_words, wb_scales
         results = keep("results", [P, 14 * QUARTER], F32)
         res0 = results[:, 6 * QUARTER : 14 * QUARTER].rearrange("p (t j) -> p t j", t=PACK)
         res2 = results[:, : 8 * QUARTER].rearrange("p (t j) -> p t j", t=PACK)[:, :, :QUARTER]
-        res3 = results[:, 5 * QUARTER : 13 * QUARTER].rearrange("p (t j) -> p t j", t=PACK)[:, :, :QUARTER]
+        res3 = results[:, 3 * QUARTER : 11 * QUARTER].rearrange("p (t j) -> p t j", t=PACK)[:, :, :QUARTER]
 
         def first(c, bank):
             cols = slice(c * SUB, (c + 1) * SUB)
@@ -184,15 +184,15 @@ def tile_list_xcross_reluP_kernel(tc, tab_words, tab_scales, wb_words, wb_scales
         up01 = [res2[:, 0, :], res3[:, 0, :]]
         for g in range(2):
             lift(up01[g], y0[1], 1, g * QUARTER, QUARTER)
-        up02 = keep("up02", [P, HALF], F32)
-        lift(up02[:], y0[2], 2, 0, HALF)
+        up02 = results[:, QUARTER : 3 * QUARTER]
+        lift(up02, y0[2], 2, 0, HALF)
         h_w1 = keep("h_w1", [P, HALF], U32, tag="x_first0")
         nc.vector.quantize_mx(out=h_w1[:].bitcast(FP8X4), scales=h_s[1][:], in_=h_bf1[:])
         y1 = [second(1, t, PACK + t, h_w1) for t in range(PACK)]
         for g in range(2):
             cross(res0[:, 1, g * QUARTER : (g + 1) * QUARTER], 1, g * QUARTER, QUARTER, up01[g])
         store(res0[:, 1, :], 1, 0, HALF)
-        up03 = [res2[:, 1 + g, :] for g in range(2)]
+        up03 = [res2[:, 2, :], res3[:, 1, :]]
         for g in range(2):
             lift(up03[g], y0[3], 3, g * QUARTER, QUARTER)
         up1 = {}
@@ -204,12 +204,20 @@ def tile_list_xcross_reluP_kernel(tc, tab_words, tab_scales, wb_words, wb_scales
         lift(up_last[:], y1[PACK - 1], PACK - 1, HALF - SUB, SUB)
         for g in range(4):
             res_w[g] = keep("res_w%d" % g, [P, QUARTER], U32, tag="up13" if g == 2 else None)
-        cross(res0[:, 2, :], 2, 0, HALF, up02[:])
-        store(res0[:, 2, :], 2, 0, HALF)
         for g, res in enumerate((res2, res3)):
             cols = slice(g * QUARTER, (g + 1) * QUARTER)
             nc.vector.scalar_tensor_tensor(res[:, 0, :], y1[0][:, cols], bias1[:, 0:1], x_third[:, cols], ALU.add, ALU.mult)
             store(res[:, 0, :], 0, HALF + g * QUARTER, QUARTER)
+        for g in (1, 0):
+            cols = slice(g * QUARTER, (g + 1) * QUARTER)
+            cross(res0[:, 2, cols], 2, g * QUARTER, QUARTER, up02[:, cols])
+        store(res0[:, 2, :], 2, 0, HALF)
+
+        def cross_late(res, g, t):
+            cross(res[:, t, :], t, HALF + g * QUARTER, QUARTER, up1[t][:, g * QUARTER : (g + 1) * QUARTER])
+            store(res[:, t, :], t, HALF + g * QUARTER, QUARTER)
+
+        cross_late(res2, 0, 1)
         for g in range(2):
             cross(res0[:, 3, g * QUARTER : (g + 1) * QUARTER], 3, g * QUARTER, QUARTER, up03[g])
         store(res0[:, 3, :], 3, 0, HALF)
@@ -218,13 +226,8 @@ def tile_list_xcross_reluP_kernel(tc, tab_words, tab_scales, wb_words, wb_scales
         rounded1 = rounded01[:, QUARTER * PACK :]
         round_out(nc.scalar.copy, rounded0, res0[:, :, :QUARTER])
         round_out(nc.scalar.copy, rounded1, res0[:, :, QUARTER:])
-
-        def cross_late(res, g, t):
-            cross(res[:, t, :], t, HALF + g * QUARTER, QUARTER, up1[t][:, g * QUARTER : (g + 1) * QUARTER])
-            store(res[:, t, :], t, HALF + g * QUARTER, QUARTER)
-
-        cross_late(res2, 0, 1)
         cross_late(res2, 0, 2)
+        cross_late(res3, 1, 1)
         quantise_out(rounded0, 0, QUARTER)
         store_words(0)
         cross_late(res2, 0, 3)
@@ -232,7 +235,6 @@ def tile_list_xcross_reluP_kernel(tc, tab_words, tab_scales, wb_words, wb_scales
         round_out(nc.scalar.copy, rounded2[:], res2)
         quantise_out(rounded1, QUARTER, QUARTER)
         store_words(QUARTER)
-        cross_late(res3, 1, 1)
         cross_late(res3, 1, 2)
         for e, lifted in enumerate((up1[3][:, QUARTER:], up_last[:])):
             cross(res3[:, 3, e * SUB : (e + 1) * SUB], 3, J - QUARTER + e * SUB, SUB, lifted)

@@ -198,6 +198,12 @@ def tile_list_xcross_reluP_kernel(tc, tab_words, tab_scales, wb_words, wb_scales
         up1 = {}
         for t in range(1, PACK):
             count = HALF if t < PACK - 1 else HALF - SUB
+            if t == 1:
+                up12 = results[:, 12 * QUARTER + SUB : 13 * QUARTER + SUB]
+                lift(up12, y1[t], t, 0, QUARTER)
+                up13 = keep("up_13", [P, QUARTER], F32)
+                lift(up13[:], y1[t], t, QUARTER, QUARTER)
+                continue
             up1[t] = keep("up1%d" % t, [P, count], F32)
             lift(up1[t][:], y1[t], t, 0, count)
         up_last = keep("up_last", [P, SUB], F32)
@@ -217,7 +223,10 @@ def tile_list_xcross_reluP_kernel(tc, tab_words, tab_scales, wb_words, wb_scales
             cross(res[:, t, :], t, HALF + g * QUARTER, QUARTER, up1[t][:, g * QUARTER : (g + 1) * QUARTER])
             store(res[:, t, :], t, HALF + g * QUARTER, QUARTER)
 
-        cross_late(res2, 0, 1)
+        for e in range(2):
+            cols = slice(e * SUB, (e + 1) * SUB)
+            cross(res2[:, 1, cols], 1, HALF + e * SUB, SUB, up12[:, cols])
+        store(res2[:, 1, :], 1, HALF, QUARTER)
         for g in range(2):
             cross(res0[:, 3, g * QUARTER : (g + 1) * QUARTER], 3, g * QUARTER, QUARTER, up03[g])
         store(res0[:, 3, :], 3, 0, HALF)
@@ -227,7 +236,8 @@ def tile_list_xcross_reluP_kernel(tc, tab_words, tab_scales, wb_words, wb_scales
         round_out(nc.scalar.copy, rounded0, res0[:, :, :QUARTER])
         round_out(nc.scalar.copy, rounded1, res0[:, :, QUARTER:])
         cross_late(res2, 0, 2)
-        cross_late(res3, 1, 1)
+        cross(res3[:, 1, :], 1, J - QUARTER, QUARTER, up13[:])
+        store(res3[:, 1, :], 1, J - QUARTER, QUARTER)
         quantise_out(rounded0, 0, QUARTER)
         store_words(0)
         cross_late(res2, 0, 3)

@@ -33,16 +33,16 @@ def tile_list_xcross_reluP_kernel(tc, tab_words, tab_scales, wb_words, wb_scales
         psum = ctx.enter_context(tc.psum_pool(name="psum", bufs=1))
 
         def keep(name, shape, dtype, tag=None):
-            return held.tile(shape, dtype, name=name, tag=tag or name, align_bytes=64)
+            return held.tile(shape, dtype, name=name, tag=tag or name, align_bytes=256)
 
         def listed(j0, count):
             return offsets[:, j0 // 16 : (j0 + count) // 16]
 
         rows16 = slice(P - 16, P)
-        offsets = held.tile([P, J // 16], U16, name="offsets")
-        ws_raw = laid.tile([P, 2 * N], U8, name="ws_raw", offset=0, align_bytes=64)
+        offsets = held.tile([P, J // 16], U16, name="offsets", align_bytes=256)
+        ws_raw = laid.tile([P, 2 * N], U8, name="ws_raw", offset=0, align_bytes=256)
         w_s = keep("w_s", [P, 2 * N], U8)
-        tab_s = laid.tile([P, T], U8, name="tab_s", offset=SCALES_AT, align_bytes=64)
+        tab_s = laid.tile([P, T], U8, name="tab_s", offset=SCALES_AT, align_bytes=256)
         v_s_all = keep("v_s", [P, J], U8)
         nc.vector.memset(tab_s[: P - 16, :].bitcast(I32), 0)
         nc.vector.memset(ws_raw[:48, :].bitcast(I32), 0)
@@ -74,8 +74,8 @@ def tile_list_xcross_reluP_kernel(tc, tab_words, tab_scales, wb_words, wb_scales
         nc.vector.tensor_copy(v_rows[:], tab_s[:].indirect(offsets[:]))
         to_quadrants(v_s_all, v_rows)
         v_s = [v_s_all[:, :HALF], v_s_all[:, HALF:]]
-        load_x0(0, laid.tile([P, T], F32, name="x0_0", offset=SCALES_AT + 1024, align_bytes=64))
-        upw_raw = laid.tile([P, 2 * N], U8, name="upw_raw", offset=SCALES_AT, align_bytes=64)
+        load_x0(0, laid.tile([P, T], F32, name="x0_0", offset=SCALES_AT + 1024, align_bytes=256))
+        upw_raw = laid.tile([P, 2 * N], U8, name="upw_raw", offset=SCALES_AT, align_bytes=256)
         nc.sync.dma_start(upw_raw[:].bitcast(I32), upw_words[0].bitcast(I32))
         dn_bf = keep("dn_bf", [P, R * PACK], BF16)
         dn_dealt = dn_bf[:].rearrange("p (t c e i) -> p c i e t", t=PACK, e=2, i=PACK)
@@ -89,9 +89,9 @@ def tile_list_xcross_reluP_kernel(tc, tab_words, tab_scales, wb_words, wb_scales
         nc.vector.quantize_mx(out=dn_w[:].bitcast(FP8X4), scales=dn_s[:], in_=dn_bf[:])
         for r in range(4):
             nc.sync.dma_start(w_s[r:P:32, :].bitcast(I32), ws_rows[48 + r : 64 : 4, :].bitcast(I32))
-        bias = laid.tile([P, PACK], F32, name="bias", offset=0, align_bytes=64)
+        bias = laid.tile([P, PACK], F32, name="bias", offset=0, align_bytes=256)
         nc.sync.dma_start(bias[:], b.rearrange("(p t) -> p t", t=PACK))
-        load_x0(1, laid.tile([P, T], F32, name="x0_1", offset=64, align_bytes=64))
+        load_x0(1, laid.tile([P, T], F32, name="x0_1", offset=256, align_bytes=256))
         bias1 = keep("bias1", [P, PACK], F32)
         nc.gpsimd.tensor_scalar(bias1[:], bias[:], 1.0, 1.0, ALU.mult, ALU.add)
         v_w_all = keep("v_w", [P, J], U32, tag="dn_bf")

from contextlib import ExitStack

import concourse.mybir as mybir

K, R, N, T, J = 512, 512, 512, 2048, 1024
FLOPS = 2 * J * (K * R + K * N + R * N)

F32 = mybir.dt.float32
BF16 = mybir.dt.bfloat16
I32 = mybir.dt.int32
U32 = mybir.dt.uint32
U16 = mybir.dt.uint16
U8 = mybir.dt.uint8
FP8X4 = mybir.dt.float8_e4m3fn_x4
FP4X4 = mybir.dt.float4_e2m1fn_x4
ALU = mybir.AluOpType
ACT = mybir.ActivationFunctionType

P = 128
PACK = 4
HALF = 512
QUARTER = 256
SUB = 128
DN_S = 30
SCALES_AT = 16384


def tile_list_xcross_reluP_kernel(tc, tab_words, tab_scales, wb_words, wb_scales, dn, upw_words, upw_scales, x0T, b, offs, out_0, out_1, out_2):
    nc = tc.nc
    with ExitStack() as ctx:
        held = ctx.enter_context(tc.tile_pool(name="held", bufs=1))
        laid = ctx.enter_context(tc.tile_pool(name="laid", bufs=1))
        psum = ctx.enter_context(tc.psum_pool(name="psum", bufs=1))

        def keep(name, shape, dtype, tag=None):
            return held.tile(shape, dtype, name=name, tag=tag or name, align_bytes=256)

        def listed(j0, count):
            return offsets[:, j0 // 16 : (j0 + count) // 16]

        rows16 = slice(P - 16, P)
        offsets = held.tile([P, J // 16], U16, name="offsets", align_bytes=256)
        ws_raw = laid.tile([P, 2 * N], U8, name="ws_raw", offset=0, align_bytes=256)
        w_s = keep("w_s", [P, 2 * N], U8)
        tab_s = laid.tile([P, T], U8, name="tab_s", offset=SCALES_AT, align_bytes=256)
        v_s_all = keep("v_s", [P, J], U8)
        nc.vector.memset(tab_s[: P - 16, :].bitcast(I32), 0)
        nc.vector.memset(ws_raw[:48, :].bitcast(I32), 0)
        nc.vector.memset(ws_raw[64:, :].bitcast(I32), 0)
        nc.vector.memset(v_s_all[:].bitcast(I32), 0)
        nc.vector.memset(w_s[:].bitcast(I32), 0)
        nc.sync.dma_start(offsets[:], offs)
        nc.sync.dma_start(tab_s[rows16, :].bitcast(I32), tab_scales[0].bitcast(I32))
        dn_raw = keep("dn_raw", [P, PACK, R], F32)
        nc.sync.dma_start(dn_raw[:], dn.rearrange("(p i) r -> p i r", i=PACK))
        for u, scales in enumerate((wb_scales, upw_scales)):
            nc.sync.dma_start(ws_raw[48:64, u * N : (u + 1) * N].bitcast(I32), scales[0].bitcast(I32))
        tab_w = keep("tab_w", [P, T], U32)
        nc.sync.dma_start(tab_w[:].bitcast(I32), tab_words[0].rearrange("p t i -> p (t i)").bitcast(I32))
        wb_raw = keep("wb_raw", [P, 2 * N], U8)
        nc.sync.dma_start(wb_raw[:].bitcast(I32), wb_words[0].bitcast(I32))
        x0_rows = x0T.rearrange("(p t) c -> p t c", t=PACK)
        x0 = []

        def load_x0(t, plane):
            x0.append(plane)
            nc.sync.dma_start(plane[:], x0_rows[:, t, :])

        def to_quadrants(plane, rows):
            for r in range(4):
                nc.sync.dma_start(plane[r:P:32, :].bitcast(I32), rows[P - 16 + r : P : 4, :].bitcast(I32))

        v_rows = keep("v_rows", [P, J], U8)
        nc.vector.tensor_copy(v_rows[:], tab_s[:].indirect(offsets[:]))
        to_quadrants(v_s_all, v_rows)
        v_s = [v_s_all[:, :HALF], v_s_all[:, HALF:]]
        load_x0(0, laid.tile([P, T], F32, name="x0_0", offset=SCALES_AT + 1024, align_bytes=256))
        upw_raw = laid.tile([P, 2 * N], U8, name="upw_raw", offset=SCALES_AT, align_bytes=256)
        nc.sync.dma_start(upw_raw[:].bitcast(I32), upw_words[0].bitcast(I32))
        dn_bf = keep("dn_bf", [P, R * PACK], BF16)
        dn_dealt = dn_bf[:].rearrange("p (t c e i) -> p c i e t", t=PACK, e=2, i=PACK)
        dn_rows = dn_raw[:].rearrange("p i (c e t) -> p c i e t", e=2, t=PACK)
        nc.scalar.copy(dn_dealt[:, :DN_S], dn_rows[:, :DN_S])
        nc.vector.tensor_copy(dn_dealt[:, DN_S:], dn_rows[:, DN_S:])
        ws_rows = keep("ws_rows", [P, 2 * N], U8)
        nc.vector.tensor_copy(ws_rows[:].rearrange("p (u t m) -> p u t m", u=2, t=PACK), ws_raw[:].rearrange("p (u m t) -> p u t m", u=2, t=PACK))
        dn_w = keep("dn_w", [P, R], U32)
        dn_s = keep("dn_s", [P, R], U8)
        nc.vector.quantize_mx(out=dn_w[:].bitcast(FP8X4), scales=dn_s[:], in_=dn_bf[:])
        for r in range(4):
            nc.sync.dma_start(w_s[r:P:32, :].bitcast(I32), ws_rows[48 + r : 64 : 4, :].bitcast(I32))
        bias = laid.tile([P, PACK], F32, name="bias", offset=0, align_bytes=256)
        nc.sync.dma_start(bias[:], b.rearrange("(p t) -> p t", t=PACK))
        load_x0(1, laid.tile([P, T], F32, name="x0_1", offset=256, align_bytes=256))
        bias1 = keep("bias1", [P, PACK], F32)
        nc.gpsimd.tensor_scalar(bias1[:], bias[:], 1.0, 1.0, ALU.mult, ALU.add)
        v_w_all = keep("v_w", [P, J], U32, tag="dn_bf")
        v_w = [v_w_all[:, :HALF], v_w_all[:, HALF:]]
        for j0, count in ((0, SUB), (SUB, SUB), (QUARTER, QUARTER), (HALF, HALF)):
            nc.vector.tensor_copy(v_w_all[:, j0 : j0 + count], tab_w[:].indirect(listed(j0, count)))
        load_x0(2, keep("x0_2", [P, T], F32, tag="tab_w"))
        wb_w = keep("wb_w", [P, 2 * N], U8)
        nc.vector.tensor_copy(wb_w[:].bitcast(U16).rearrange("p (t m) -> p t m", t=PACK), wb_raw[:].bitcast(U16).rearrange("p (m t) -> p t m", t=PACK))
        load_x0(3, keep("x0_3", [P, T], F32, tag="wb_raw"))
        upw_dealt = upw_raw[:].rearrange("p (m t e) -> p t m e", t=PACK, e=2)
        upw_w = [keep("upw_w0", [P, N], U8)]
        nc.gpsimd.tensor_copy(upw_w[0][:].rearrange("p (t m e) -> p t m e", t=2, e=2), upw_dealt[:, :2])

        def weight_words(u, t):
            if u == 0:
                return wb_w[:, 2 * t * P : 2 * (t + 1) * P]
            return upw_w[t // 2][:, 2 * (t % 2) * P : 2 * (t % 2 + 1) * P]

        h_s = [keep("h_s%d" % h, [P, HALF], U8) for h in range(2)]
        h_bf0 = [keep("h_bf0%d" % g, [P, QUARTER * PACK], BF16) for g in range(2)]
        h_bf1 = keep("h_bf1", [P, HALF * PACK], BF16)
        results = keep("results", [P, 14 * QUARTER], F32)
        res0 = results[:, 6 * QUARTER : 14 * QUARTER].rearrange("p (t j) -> p t j", t=PACK)
        res2 = results[:, : 8 * QUARTER].rearrange("p (t j) -> p t j", t=PACK)[:, :, :QUARTER]
        res3 = results[:, 3 * QUARTER : 11 * QUARTER].rearrange("p (t j) -> p t j", t=PACK)[:, :, :QUARTER]

        def first(c, bank):
            cols = slice(c * SUB, (c + 1) * SUB)
            hs = psum.tile([P, PACK, SUB], F32, name="hs%d" % c, tag="bank%d" % bank)
            for t in range(PACK):
                rows = slice(t * P, (t + 1) * P)
                nc.tensor.matmul_mx(out=hs[:, t, :], lhsT=dn_w[:, rows].bitcast(FP8X4), lhsT_scale=dn_s[:, rows],
                                    rhs=v_w_all[:, cols].bitcast(FP8X4), rhs_scale=v_s_all[:, cols], start=True, stop=True)
            width = SUB * PACK
            dst = h_bf0[c // 2][:, (c % 2) * width : (c % 2 + 1) * width] if c < 4 else h_bf1[:, (c - 4) * width : (c - 3) * width]
            nc.scalar.activation(dst.rearrange("p (j t) -> p j t", t=PACK), hs[:].rearrange("p t j -> p j t"), ACT.Relu)

        def second(h, t, bank, h_w):
            y = psum.tile([P, HALF], F32, name="y%d%d" % (h, t), tag="bank%d" % bank)
            moving = ((v_w[h], v_s[h]), (h_w[:], h_s[h][:]))
            for i, u in enumerate(((0, 1), (1, 0))[h]):
                mw, ms = moving[u]
                nc.tensor.matmul_mx(out=y[:], lhsT=weight_words(u, t).bitcast(FP4X4), lhsT_scale=w_s[:, u * N + t * P : u * N + (t + 1) * P],
                                    rhs=mw.bitcast(FP8X4), rhs_scale=ms, start=(i == 0), stop=(i == 1))
            return y

        def lift(dst, y, t, c0, count):
            nc.scalar.activation(dst, y[:, c0 : c0 + count], ACT.Identity, bias=bias1[:, t : t + 1])

        res_w = {}
        res_s = keep("res_s", [P, QUARTER], U8)
        out_rows = out_0.rearrange("(p t) j -> p t j", t=PACK)
        out_words = out_1[0].rearrange("p j i -> p (j i)").bitcast(I32)

        def cross(dst, t, j0, count, lifted):
            nc.vector.tensor_tensor(dst, x0[t][:].indirect(listed(j0, count)), lifted, ALU.mult)

        def store(src, t, j0, count):
            nc.sync.dma_start(out_rows[:, t, j0 : j0 + count], src)

        def round_out(engine_copy, rounded, res):
            engine_copy(rounded.rearrange("p (c i t) -> p c t i", i=4, t=PACK), res.rearrange("p t (c i) -> p c t i", i=4))

        def quantise_out(rounded, j0, count):
            c0 = j0 % QUARTER
            nc.vector.quantize_mx(out=res_w[j0 // QUARTER][:, c0 : c0 + count].bitcast(FP8X4), scales=res_s[4 * (j0 // QUARTER) :, c0 : c0 + count], in_=rounded)

        def store_words(j0):
            nc.sync.dma_start(out_words[:, j0 : j0 + QUARTER], res_w[j0 // QUARTER][:].bitcast(I32))

        x_first = [keep("x_first%d" % g, [P, QUARTER], F32) for g in range(2)]
        for g in range(2):
            nc.vector.tensor_copy(x_first[g][:], x0[0][:].indirect(listed(g * QUARTER, QUARTER)))
        for c in range(8):
            first(c, c)
        h_w0 = keep("h_w0", [P, HALF], U32, tag="ws_rows")
        for g in range(2):
            cols = slice(g * QUARTER, (g + 1) * QUARTER)
            nc.vector.quantize_mx(out=h_w0[:, cols].bitcast(FP8X4), scales=h_s[0][:, cols], in_=h_bf0[g][:])
        upw_w.append(keep("upw_w1", [P, N], U8, tag="h_bf01"))
        nc.gpsimd.tensor_copy(upw_w[1][:].rearrange("p (t m e) -> p t m e", t=2, e=2), upw_dealt[:, 2:])
        x_third = keep("x_third", [P, HALF], F32, tag="h_bf00")
        nc.vector.tensor_copy(x_third[:], x0[0][:].indirect(listed(HALF, HALF)))
        y0 = [second(0, t, t, h_w0) for t in range(PACK)]
        for g in range(2):
            cols = slice(g * QUARTER, (g + 1) * QUARTER)
            nc.vector.scalar_tensor_tensor(res0[:, 0, cols], y0[0][:, cols], bias1[:, 0:1], x_first[g][:], ALU.add, ALU.mult)
        store(res0[:, 0, :], 0, 0, HALF)
        up01 = [res2[:, 0, :], res3[:, 0, :]]
        for g in range(2):
            lift(up01[g], y0[1], 1, g * QUARTER, QUARTER)
        up02 = results[:, QUARTER : 3 * QUARTER]
        lift(up02, y0[2], 2, 0, HALF)
        h_w1 = keep("h_w1", [P, HALF], U32, tag="x_first0")
        nc.vector.quantize_mx(out=h_w1[:].bitcast(FP8X4), scales=h_s[1][:], in_=h_bf1[:])
        y1 = [second(1, t, PACK + t, h_w1) for t in range(PACK)]
        for g in range(2):
            cross(res0[:, 1, g * QUARTER : (g + 1) * QUARTER], 1, g * QUARTER, QUARTER, up01[g])
        store(res0[:, 1, :], 1, 0, HALF)
        up03 = [res2[:, 2, :], res3[:, 1, :]]
        for g in range(2):
            lift(up03[g], y0[3], 3, g * QUARTER, QUARTER)
        up1 = {}
        for t in range(1, PACK):
            count = HALF if t < PACK - 1 else HALF - SUB
            if t == 1:
                up12 = results[:, 12 * QUARTER + SUB : 13 * QUARTER + SUB]
                lift(up12, y1[t], t, 0, QUARTER)
                up13 = keep("up_13", [P, QUARTER], F32)
                lift(up13[:], y1[t], t, QUARTER, QUARTER)
                continue
            up1[t] = keep("up1%d" % t, [P, count], F32)
            lift(up1[t][:], y1[t], t, 0, count)
        up_last = keep("up_last", [P, SUB], F32)
        lift(up_last[:], y1[PACK - 1], PACK - 1, HALF - SUB, SUB)
        for g in range(4):
            res_w[g] = keep("res_w%d" % g, [P, QUARTER], U32, tag="up13" if g == 2 else None)
        for g, res in enumerate((res2, res3)):
            cols = slice(g * QUARTER, (g + 1) * QUARTER)
            nc.vector.scalar_tensor_tensor(res[:, 0, :], y1[0][:, cols], bias1[:, 0:1], x_third[:, cols], ALU.add, ALU.mult)
            store(res[:, 0, :], 0, HALF + g * QUARTER, QUARTER)
        for g in (1, 0):
            cols = slice(g * QUARTER, (g + 1) * QUARTER)
            cross(res0[:, 2, cols], 2, g * QUARTER, QUARTER, up02[:, cols])
        store(res0[:, 2, :], 2, 0, HALF)

        def cross_late(res, g, t):
            cross(res[:, t, :], t, HALF + g * QUARTER, QUARTER, up1[t][:, g * QUARTER : (g + 1) * QUARTER])
            store(res[:, t, :], t, HALF + g * QUARTER, QUARTER)

        for e in range(2):
            cols = slice(e * SUB, (e + 1) * SUB)
            cross(res2[:, 1, cols], 1, HALF + e * SUB, SUB, up12[:, cols])
        store(res2[:, 1, :], 1, HALF, QUARTER)
        for g in range(2):
            cross(res0[:, 3, g * QUARTER : (g + 1) * QUARTER], 3, g * QUARTER, QUARTER, up03[g])
        store(res0[:, 3, :], 3, 0, HALF)
        rounded01 = keep("rounded01", [P, HALF * PACK], BF16, tag="dn_bf")
        rounded0 = rounded01[:, : QUARTER * PACK]
        rounded1 = rounded01[:, QUARTER * PACK :]
        round_out(nc.scalar.copy, rounded0, res0[:, :, :QUARTER])
        round_out(nc.scalar.copy, rounded1, res0[:, :, QUARTER:])
        cross_late(res2, 0, 2)
        cross(res3[:, 1, :], 1, J - QUARTER, QUARTER, up13[:])
        store(res3[:, 1, :], 1, J - QUARTER, QUARTER)
        quantise_out(rounded0, 0, QUARTER)
        store_words(0)
        cross_late(res2, 0, 3)
        rounded2 = keep("rounded2", [P, QUARTER * PACK], BF16)
        round_out(nc.scalar.copy, rounded2[:], res2)
        quantise_out(rounded1, QUARTER, QUARTER)
        store_words(QUARTER)
        cross_late(res3, 1, 2)
        for e, lifted in enumerate((up1[3][:, QUARTER:], up_last[:])):
            cross(res3[:, 3, e * SUB : (e + 1) * SUB], 3, J - QUARTER + e * SUB, SUB, lifted)
        store(res3[:, 3, :], 3, J - QUARTER, QUARTER)
        rounded3 = keep("rounded3", [P, SUB * PACK], BF16)
        round_out(nc.scalar.copy, rounded3[:], res3[:, :, :SUB])
        quantise_out(rounded2[:], HALF, QUARTER)
        store_words(HALF)
        rounded4 = res2[:, 0, :].bitcast(BF16)
        round_out(nc.vector.tensor_copy, rounded4, res3[:, :, SUB:])
        quantise_out(rounded3[:], J - QUARTER, SUB)
        quantise_out(rounded4, J - SUB, SUB)
        store_words(J - QUARTER)
        for q in range(4):
            (nc.scalar, nc.sync)[q // 2].dma_start(out_2[0, 4 * q : 4 * q + 4, :].bitcast(I32).rearrange("r (g c) -> g r c", g=4), res_s[32 * q : 32 * q + 16, :].bitcast(I32))
